import numpy as np, ml_dtypes
CORES = [2,6,10,14,18,22,26,30]
N = 8
BF = ml_dtypes.bfloat16
V, L, T, RO, MIN = 8192, 128, 32, 3, 7
B, S = T // 16, V // L
def place(n, u, kk):
    return (((n * (2 * u + 1)) >> 5) + n + kk) & (V - 1)
def pack(X, A, z, w):
    a = np.ascontiguousarray(A.reshape(N, 8, B, 16, L).transpose(0, 1, 3, 2, 4)).reshape(N, 128, B * L)
    return {"xt": np.ascontiguousarray(X.reshape(N, 128, V)).astype(np.float32).astype(BF), "am": a.astype(np.int32),
            "zv": np.ascontiguousarray(z.reshape(N, 128, L)).astype(np.float32).astype(BF), "wt": np.ascontiguousarray(w.reshape(N, 128, 1)).astype(np.int32)}
def pools(rng, sizes):
    m = rng.choice(np.array(sizes), (N, 8, 1, L)); pool = rng.integers(0, V, (N, 8, T, L))
    return np.take_along_axis(pool, rng.integers(0, m, (N, 8, T, L)), 2)
def setup_inputs(rng):
    base = rng.integers(0, 256, (N, 8, 16, 1)).astype(np.int16); share = rng.choice(np.array([0.3, 0.5, 0.7], np.float32), (N, 8, 1, 1))
    X = np.where(rng.random((N, 8, 16, V), dtype=np.float32) < share, base, rng.integers(0, 256, (N, 8, 16, V), dtype=np.int16))
    return pack(X, pools(rng, [1, 2, 3, T, T, T, T, T]), rng.integers(0, 256, (N, 8, 16, L)), rng.integers(0, 16, (N, 8, 16)))
def setup_inputs_spread(rng):
    X = np.minimum(np.exp2(8 * rng.random((N, 8, 1, V))) * rng.random((N, 8, 16, V)), 255).astype(np.int16)
    A = np.exp2((V.bit_length() - 1) * rng.random((N, 8, T, L))).astype(np.int64) - 1
    A = np.where(rng.random((N, 8, T, L)) < rng.random((N, 8, 1, L)), V - 1 - A, A)
    z = np.minimum(np.exp2(8 * rng.random((N, 8, 1, L))) * rng.random((N, 8, 16, L)), 255).astype(np.int64)
    w = np.minimum(np.exp2(4 * rng.random((N, 8, 1))) * rng.random((N, 8, 16)), 15).astype(np.int64)
    return pack(X, A, z, w)
def setup_inputs_ends(rng):
    kd = rng.integers(0, 8, (N, 8, 1, V)); X = 255 * rng.integers(0, 2, (N, 8, 16, V), dtype=np.int16)
    kd[N - 1] = np.maximum(kd[N - 1], 2)
    X = np.where(kd == 0, 0, np.where(kd == 1, 255, X))
    full = np.all(X[N - 1] == 255, axis=1); X[N - 1, :, 15] = np.where(full, 0, X[N - 1, :, 15])
    X[::2, :, :, 0] = 255; X[1::2, :, :, 0] = 0; X[N - 1, :, :, 0] = 255
    c1 = place(V - 1, 1023, 0); X[:, 7, :, c1] = 255; X[::2, 7, :, c1] = 0; X[N - 1, 7, :, c1] = 0
    A = (V - 1) * (rng.random((N, 8, T, L)) < rng.choice(np.array([0.1, 0.5, 0.9]), (N, 8, 1, L))).astype(np.int64)
    A[:, :, 0, L - 1] = V - 1; A[:, :, T - 1, L - 1] = V - 1; A[:, :, T - 2, L - 1] = 0
    one = (V - 1) * rng.integers(0, 2, (8, 1, L)); one[:, :, 0] = 0; one[:, :, L - 1] = V - 1
    A[N - 2] = one; A[N - 1] = V - 1; A[N - 1, :, T - 1] = 0
    zk = rng.integers(0, 4, (N, 8, 1, L)); zk[..., 0] = 1; zk[..., 1] = 0; zk[..., L - 2] = 1
    z = np.where(zk == 0, 0, np.where(zk == 1, 255, 255 * rng.integers(0, 2, (N, 8, 16, L))))
    vec = np.array([255] * 13 + [30, 0, 0]); o = np.argsort(rng.random((N, 16, L)), axis=1)
    hit = rng.random((N, 1, L)) < 0.125; hit[..., L - 1] = True; hit[..., 0] = False; hit[..., 1] = False; hit[..., L - 2] = False
    z[:, 7] = np.where(hit, vec[o], z[:, 7])
    w = 15 * rng.integers(0, 2, (N, 8, 16)); w[:, 7] = 15; w[::2, 0] = 0
    return pack(X, A, z, w)
def setup_inputs_corners(rng):
    X = rng.integers(0, 256, (N, 8, 16, V), dtype=np.int16); c = np.arange(V); base = rng.choice(np.array([0, 1, 100, 255]), (N, 8, 16))
    prs = [(0, 1), (14, 15), (0, 15), (7, 8), (3, 4), (6, 9), (2, 12), (8, 15)]
    for q in range(N):
        o = rng.permutation(8)
        for g in range(8):
            p0, p1 = prs[int(o[g])]
            X[q, g, :p1] = base[q, g, :p1, None]
            X[q, g, p0] = (c >> 8) + (0 if rng.random() < 0.5 else 256 - (V >> 8)); X[q, g, p1] = c & 255
    zk = rng.integers(0, 4, (N, 8, 1, L))
    z = np.where(zk == 0, 0, np.where(zk == 1, 255, rng.integers(0, 256, (N, 8, 16, L))))
    wk = rng.integers(0, 4, (N, 8, 1)); w = np.where(wk == 0, 0, np.where(wk == 1, 15, rng.integers(0, 16, (N, 8, 16))))
    r = rng.permutation(N); z[r[0]] = 0; w[r[0]] = rng.integers(1, 16, (8, 16)); w[r[1]] = 0
    s = rng.choice(np.array([1, 2, T // 2, T // 2 + 1, T - 1, T]), (N, 8, 1, L))
    s[r[0]] = 1; s[r[1]] = 1; s[r[1], 7, 0, L - 1] = 2; s[r[2]] = T
    k = np.arange(T).reshape(1, 1, T, 1); h = V // 16 * 15 // T
    nm = k * h + rng.integers(0, h, (N, 8, T, L))
    u = np.sum(w[..., None] * z, axis=2, keepdims=True) & 1023
    nm = np.take_along_axis(nm, np.argsort(place(nm, u, 0), axis=2, kind="stable"), 2)
    A = np.take_along_axis(nm, np.where(k < T - s, k, 2 * T - 1 - s - k), 2)
    return pack(X, A, z, w)
def setup_inputs_ties(rng):
    base = rng.integers(1, 255, (N, 8, 16, 1)); base[:, 1::2] = rng.choice(np.array([1, 254]), (N, 4, 16, 1)); base = base.astype(np.int16)
    X = base + np.where(rng.random((N, 8, 16, V), dtype=np.float32) < 0.03, rng.integers(-1, 2, (N, 8, 16, V), dtype=np.int16), 0)
    A = pools(rng, [1, 2, T, T]); A[:, 0] = A[:, 0, :, :1]
    n = rng.choice(np.array([0, MIN - 1, MIN, MIN, MIN + 1, 16]), (N, 8, 1, L)); o = np.argsort(np.argsort(rng.random((N, 8, 16, L)), axis=2), axis=2)
    return pack(X, A, base.astype(np.int64) - (o >= n), rng.integers(0, 16, (N, 8, 16)))
def setup_inputs_few(rng):
    base = rng.integers(0, 256, (N, 8, 16, 1)).astype(np.int16)
    X = np.where(rng.random((N, 8, 16, V), dtype=np.float32) < 0.4, base, rng.integers(0, 256, (N, 8, 16, V), dtype=np.int16))
    A = pools(rng, [1, 2, 3, T, T, T, T, T]); w = rng.integers(0, 16, (N, 8, 16))
    q = int(rng.integers(0, N)); p = (q + 1) % N; a = rng.permutation(3) + 1
    near = [(q - d) % N for d in range((RO - 2) * (RO - 1) // 2 + 1)]
    A[near] = rng.integers(0, V, (8, 1, L)); A[p] = rng.integers(0, V, (8, 1, L))
    w[q] = 0; w[p] = 0
    nm = np.arange(V); rest = place(nm, 0, 0) % S; ok = (rest >= 1) & (rest <= S - 4)
    lows, highs = nm[ok & (nm < V // 4)], nm[ok & (nm >= V // 2) & (nm < 3 * V // 4)]
    for r, rs, kinds in ((q, near, np.repeat(np.arange(RO - 1), a[:RO - 1])), (p, [p], np.zeros(int(a[2]), np.int64))):
        for g, t in zip(rng.permutation(8), kinds):
            i = int(rng.integers(0, L)); n, m = int(rng.choice(lows)), int(rng.choice(highs))
            if rng.random() < 0.5: n, m = m, n
            for v in rs: A[v, g, :, i] = n
            A[r, g, 0, i] = m
            for j in range(int(t) + 1):
                k = 0 if j == 0 else int(a[j - 1])
                X[r, g, 0, place(n, 0, k)] = 0 if j < t else 255
                X[r, g, 0, place(m, 0, k)] = 255 if j < t else 0
    return pack(X, A, rng.integers(0, 256, (N, 8, 16, L)), w)
def check_inputs(d):
    bad = []
    for k, lo, hi in (("xt", 0, 255), ("am", 0, V - 1), ("zv", 0, 255), ("wt", 0, 15)):
        v = np.asarray(d[k]).astype(np.float64)
        if not (np.min(v) >= lo and np.max(v) <= hi and np.all(v == np.floor(v))): bad.append("range of " + k)
    return bad
def pick(X, c):
    return np.take_along_axis(X, c.reshape(N, 8, 1, T * L), 3).reshape(N, 8, 16, T, L)
def keys(v):
    out = []
    for b in (0, 8):
        h = np.zeros((N, 8, T, L), np.uint64)
        for p in range(b, b + 8): h = (h << np.uint64(8)) | v[:, :, p].astype(np.uint64)
        out.append(h)
    return out
def below(h, l, h0, l0):
    return (h < h0) | ((h == h0) & (l < l0))
def close(n, keep):
    o = np.argsort(~keep, axis=2, kind="stable")
    return np.where(np.take_along_axis(keep, o, 2), np.take_along_axis(n, o, 2), -1)
def reference(xt, am, zv, wt):
    X = xt.astype(np.float32).astype(np.int32).reshape(N, 8, 16, V)
    A = am.astype(np.int64).reshape(N, 8, 16, B, L).transpose(0, 1, 3, 2, 4).reshape(N, 8, T, L)
    z = zv.astype(np.float32).astype(np.int64).reshape(N, 8, 16, L); w = wt.astype(np.int64).reshape(N, 8, 16, 1)
    kk = np.zeros((N, 1, 1, 1), np.int64); lane = np.arange(L).reshape(1, 1, 1, L); row = np.arange(T).reshape(1, 1, T, 1)
    for t in range(RO):
        u = np.sum(w * z, axis=2, keepdims=True) & 1023
        x = pick(X, place(A, u, kk)); ha, la = keys(x)
        live = np.ones((N, 8, T, L), bool); mh, ml = ha[:, :, T - 1], la[:, :, T - 1]
        for k in range(T - 2, -1, -1):
            less = below(ha[:, :, k], la[:, :, k], mh, ml); live[:, :, k] = ~less
            mh = np.where(less, mh, ha[:, :, k]); ml = np.where(less, ml, la[:, :, k])
        alpha = close(A, live)
        first = np.argmax(live, axis=2)
        M = np.take_along_axis(x, first[:, :, None, None, :], 3)[:, :, :, 0]
        beta = np.stack([alpha[(q - 1 - t % (N - 1)) % N] for q in range(N)]); has = beta >= 0
        y = pick(X, place(np.maximum(beta, 0), u, kk)); hy, ly = keys(y)
        front = np.sum(z >= M, axis=2, keepdims=True) >= MIN
        ka = live & ~below(ha, la, hy[:, :, :1], ly[:, :, :1]); kb = has & ~below(hy, ly, mh[:, :, None], ml[:, :, None])
        names = np.where(front, np.concatenate([A, beta], axis=2), np.concatenate([beta, A], axis=2))
        keep = np.where(front, np.concatenate([ka, has], axis=2), np.concatenate([kb, live], axis=2))
        new = close(names, keep)[:, :, :T]
        A = np.where(new >= 0, new, (((A * u) >> 5) + 37 * row + u) & (V - 1))
        col = np.broadcast_to(S * lane + (u & (S - 1)), (N, 8, 16, L))
        np.put_along_axis(X, col, ((np.take_along_axis(X, col, 3) + M) >> 1).astype(np.int32), 3)
        z = np.abs(z - y[:, :, :, 0])
        kk = np.sum(~live, axis=(1, 2, 3)).reshape(N, 1, 1, 1)
    yx = np.sum(X.reshape(N, 128, 4, V // 4), axis=2)
    ya = A.reshape(N, 8, B, 16, L).transpose(0, 1, 3, 2, 4).reshape(N, 128, B * L)
    return {"yx": yx.astype(np.float32), "ya": np.ascontiguousarray(ya).astype(np.float32), "yz": z.reshape(N, 128, L).astype(np.float32)}

@@ -1,0 +1,604 @@
+from concourse.bass import DstId, RemoteDMATransfer
+from concourse.mybir import dt, AluOpType, AxisListType, ActivationFunctionType
+
+OP = AluOpType
+AF = ActivationFunctionType
+RO = 3
+BIG1 = 2.0 ** 90
+BIG2 = 2.0 ** 98
+DOWN = 2.0 ** -20
+UP = 2.0 ** 20
+SPLIT = [(64, 64), (32, 32)]
+NENG = 8
+
+F, B, I, U = "float32", "bfloat16", "int32", "uint16"
+
+
+def _s(shape, d):
+    return ("sbuf", [128] + list(shape), d)
+
+
+SCRATCH = {
+    "X": _s([8192], B), "xg": _s([4096], B), "yg": _s([4096], B), "S": _s([2048], F),
+    "ami": _s([256], I), "amf": _s([256], F), "Z": _s([128], B), "wi": _s([8], I), "wf": _s([8], F),
+    "VA": _s([8, 32], F), "VL": _s([256], F), "VB0": _s([8, 32], F), "VB1": _s([8, 32], F), "VB2": _s([8, 32], F),
+    "LT": _s([256], B), "LB0": _s([256], B), "LB1": _s([256], B), "LB2": _s([256], B),
+    "J": _s([8], U), "JB0": _s([8], U), "JB1": _s([8], U), "JB2": _s([8], U),
+    "pA": _s([256], I), "fa": _s([256], I), "h1": _s([256], I), "h2": _s([256], I), "offA": _s([256], U), "offB": _s([256], U),
+    "fbf": _s([256], F), "cm": _s([256], F), "uk": _s([256], F), "u32": _s([256], F), "gu": _s([128], B), "gf": _s([256], B),
+    "NV": _s([1536], F), "si": _s([8], I), "sj": _s([8], I), "sk": _s([8], F), "sf": _s([8], F), "offX": _s([8], U),
+    "w": _s([256], F), "r0": _s([256], B), "rA": _s([256], B), "rB": _s([256], B), "lt": _s([256], B),
+    "KF": _s([256], F), "HB": _s([136], F), "HS": _s([136], F), "hold": _s([128], F), "inc": _s([256], F), "M": _s([128], B), "y0": _s([128], B), "ge": _s([128], B),
+    "bonA": _s([256], B), "bonB": _s([256], B), "cA": _s([1536], B), "cY": _s([1536], B),
+    "IL": _s([1024], B), "DD": _s([1024], B), "NK": _s([512], B), "KA": _s([256], B), "KB": _s([256], B),
+    "cB": _s([256], B), "fr": _s([8], B), "nf": _s([8], B), "hA": _s([8], B), "hB": _s([8], B),
+    "G1": _s([512], B), "G2": _s([512], B), "G3": _s([512], B), "G4": _s([512], B), "G5": _s([512], B),
+    "E0": _s([16, 16], F), "E1": _s([16, 16], F), "AP": _s([8, 32], F), "v1": _s([8, 32], F),
+    "nd": _s([256], B), "nc": _s([256], B), "nr": _s([256], B),
+    "xs": _s([128], I), "xh": _s([128], I), "zd": _s([128], F),
+    "rs": _s([8], F), "rsb": _s([256], B),
+    "ones": _s([512], B), "zero": _s([256], B), "ID": _s([13, 128], B), "IU": _s([128], F), "IDN": _s([128], F),
+    "pc": _s([16], I), "pf": _s([24], F), "io1": _s([8], F), "io2": _s([128], F), "io3": _s([128], F), "io4": _s([6], F), "kio": _s([256], B),
+    "vtmp": _s([6], F), "W48": _s([48], B), "WN": _s([48], B), "WR": _s([48, 32], B),
+    "BD": _s([8, 32], B), "BW": _s([128], B), "WZ": _s([144], B),
+    "br": _s([8, 32], B), "top0": _s([128], B), "top1": _s([128], B), "tb0": _s([256], B), "tb1": _s([256], B),
+    "topl": _s([256], B), "topf": _s([256], B), "tagc": _s([512], B), "rows": _s([3, 128], B),
+    "dp": _s([8], F), "dn": _s([8], F), "jb": _s([8], F), "cx": _s([8], F),
+    "X0": ("psum", [128, 512], F), "X1": ("psum", [128, 512], F), "X2": ("psum", [128, 512], F),
+    "Y0": ("psum", [128, 16, 32], F), "Y1": ("psum", [128, 16, 32], F), "Y2": ("psum", [128, 16, 32], F),
+    "TG": ("psum", [128, 16, 32], F), "OB": ("psum", [128, 512], F),
+}
+PSUM = ("X0", "X1", "X2", "Y0", "Y1", "Y2", "TG", "OB")
+SEMAPHORES = ["eV", "eA", "eP", "eG"] + ["d%d" % k for k in range(16)] + ["l%d" % k for k in range(9)] + ["a%d" % k for k in range(9)]
+
+
+def make_plan():
+    ops, lastw, readers, bank, out = [], {}, {}, {}, {}
+
+    def op(eng, fn, R=(), W=(), sem=None, inc=None):
+        k = len(ops)
+        own = sem is not None
+        deps = set()
+
+        def other(j):
+            return own or ops[j]["sem"] is not None or ops[j]["eng"] != eng
+        for r in R:
+            j = lastw.get(r)
+            if j is not None and (other(j) or eng != "P"):
+                deps.add(j)
+        for x in W:
+            j = lastw.get(x)
+            if j is not None and other(j):
+                deps.add(j)
+            for j in readers.get(x, ()):
+                if other(j):
+                    deps.add(j)
+        for x in set(R) | set(W):
+            b = x.split(".")[0]
+            if b in PSUM:
+                for e, j in bank.setdefault(b, {}).items():
+                    if e != eng:
+                        deps.add(j)
+                bank[b][eng] = k
+        for r in R:
+            readers.setdefault(r, []).append(k)
+        for x in W:
+            lastw[x] = k
+            readers[x] = []
+        ops.append({"eng": eng, "fn": fn, "deps": deps, "sem": sem, "inc": inc})
+        return k
+
+    def emit(g, T):
+        q = {"V": g.vector, "A": g.scalar, "P": g.tensor, "G": g, "S": g.sync}
+        known = {e: {} for e in q}
+        for k, o in enumerate(ops):
+            o["key"] = o["sem"] if o["sem"] is not None else o["eng"]
+            o["need"] = False
+            if o["fn"] is None:
+                o["clock"] = {o["key"]: k}
+                o["waits"] = []
+                continue
+            kn = known[o["eng"]]
+            waits = []
+            for j in sorted(o["deps"], reverse=True):
+                if kn.get(ops[j]["key"], -1) >= j:
+                    continue
+                waits.append(j)
+                ops[j]["need"] = True
+                for key, val in ops[j]["clock"].items():
+                    if kn.get(key, -1) < val:
+                        kn[key] = val
+            o["waits"] = waits
+            o["clock"] = dict(kn)
+            o["clock"][o["key"]] = k
+        count = {}
+        for o in ops:
+            if o["sem"] is not None:
+                o["wait"] = (o["sem"], o["inc"])
+                count[o["sem"]] = o["inc"]
+            elif o["need"]:
+                name = "e" + o["eng"]
+                count[name] = count.get(name, 0) + 1
+                o["wait"] = (name, count[name])
+        for o in ops:
+            if o["fn"] is None:
+                continue
+            for j in o["waits"]:
+                q[o["eng"]].wait_ge(T.sem[ops[j]["wait"][0]], ops[j]["wait"][1])
+            ins = o["fn"]()
+            if o["sem"] is not None:
+                if o["sem"][0] == "d":
+                    ins.then_inc(T.sem[o["sem"]], 16)
+            elif o["need"]:
+                ins.then_inc(T.sem[o["wait"][0]], 1)
+        for name, val in count.items():
+            g.sync.wait_ge(T.sem[name], val)
+    out["op"], out["emit"] = op, emit
+    return out
+
+
+def rank_program(g, core, T, topo):
+    rank = T.rank_of(core)
+    if rank is None:
+        return
+    N = len(T.cores)
+    plan = make_plan()
+    op = plan["op"]
+    v, a, pe = g.vector, g.scalar, g.tensor
+    nd = [0]
+
+    def tt(o, x, y, alu, R, W):
+        op("V", lambda: v.tensor_tensor(o, x, y, alu), R, W)
+
+    def ts(o, x, s1, s2, o0, o1, R, W):
+        if o1 is None:
+            op("V", lambda: v.tensor_scalar(o, x, s1, None, o0), R, W)
+        else:
+            op("V", lambda: v.tensor_scalar(o, x, s1, s2, o0, o1), R, W)
+
+    def cp(o, x, R, W):
+        op("V", lambda: v.tensor_copy(o, x), R, W)
+
+    def ms(o, c, W):
+        op("V", lambda: v.memset(o, c), (), W)
+
+    def scan(o, x, y, o0, o1, R, W):
+        op("V", lambda: v.tensor_tensor_scan(o, x, y, 0.0, o0, o1), R, W)
+
+    def act(o, x, f, R, W, bias=0.0, scale=1.0, acc=None):
+        if f == AF.Copy:
+            op("A", lambda: a.activation(o, x, f), R, W)
+        elif acc is None:
+            op("A", lambda: a.activation(o, x, f, bias=bias, scale=scale), R, W)
+        else:
+            op("A", lambda: a.activation(o, x, f, accum_out=acc), R, W)
+
+    def mm(o, l, r, st, sp, R, W):
+        op("P", lambda: pe.matmul(o, l, r, st, sp), R, W)
+
+    def dma(eng, o, x, R, W):
+        qq = {"S": g.sync, "A": g.scalar, "G": g}[eng]
+        name = "d%d" % nd[0]
+        nd[0] += 1
+        op(eng, lambda: qq.dma_start(o, x), R, W, sem=name, inc=16)
+
+    def iota(o, pat, base, ch, W, flt=True):
+        if flt:
+            op("G", lambda: g.iota(o, pat, base, ch, allow_small_or_imprecise_dtypes=True), (), W)
+        else:
+            op("G", lambda: g.iota(o, pat, base, ch), (), W)
+
+    def send(k, t, src, dst):
+        to = T.cores[(rank + 1 + t % (N - 1)) % N]
+        fr = T.cores[(rank - 1 - t % (N - 1)) % N]
+        eng = topo.engines(core, to)[:NENG]
+        mask = sum(1 << e for e in eng)
+        rid, pid = topo.addr(to)[:2]
+        n = 3 * t + k
+        op("G", lambda: g.remote_dma(T[dst][:], T[src][:], T.sem["a%d" % n], T.sem["l%d" % n], pid, rid, mask),
+           [src], [], sem="l%d" % n, inc=len(eng))
+        op("G", None, [], [dst], sem="a%d" % n, inc=len(topo.engines(fr, core)[:NENG]))
+
+    XB, YB = [T.X0, T.X1, T.X2], [T.Y0, T.Y1, T.Y2]
+
+    def lev(bk, l):
+        if bk is YB:
+            return bk[l % 3][:, (l // 3) * 8:(l // 3) * 8 + 8, :]
+        return bk[l % 3][:, (l // 3) * 256:(l // 3) * 256 + 256]
+
+    dma("S", T.ami[:], T.am[:], [], ["ami"])
+    dma("A", T.Z[:], T.zv[:], [], ["Z"])
+    dma("A", T.wi[:, 0:1], T.wt[:], [], ["wi"])
+    dma("S", T.X[:, 0:4096], T.xt[:, 0:4096], [], ["X.a"])
+    dma("A", T.X[:, 4096:8192], T.xt[:, 4096:8192], [], ["X.b"])
+    XK = ["X.a", "X.b"]
+
+    ms(T.ones[:], 1.0, ["ones"])
+    iota(T.pc[:, 0:1], [[0, 1]], 0, 1, ["pc0"], flt=False)
+    op("G", lambda: g.affine_select(T.ID[:, 0, :], T.ones[:, 0:128], [[-1, 128]], OP.is_equal, 0.0, 0, 1), ["ones"], ["ID0"])
+    iota(T.io3[:], [[1, 8], [0, 16]], 0, 0, ["io3"])
+    iota(T.io1[:], [[1, 8]], 0, 0, ["io1"])
+    iota(T.io4[:], [[3, 6]], 2, 0, ["io4"])
+    ms(T.W48[:], 0.0, ["W48"])
+
+    def key_weights(rows):
+        for p in rows:
+            l = p // 3
+            c0 = 16 * (l % 3) + 8 * (l // 3)
+            op("G", lambda p=p, l=l, c0=c0: g.affine_select(T.W48[:, c0:c0 + 8], T.W48[:, c0:c0 + 8], [[-16, 8]], OP.not_equal,
+                                                            2.0 ** (48 - 25 * l + 8 * (2 - p % 3)), -p, 1), ["W48.%d" % l, "W48"], ["W48.%d" % l])
+    key_weights([0, 3, 6, 9, 12, 15, 1, 4, 7, 10])
+    ms(T.br[:, :, 0:1], 0.0, ["br"])
+    ms(T.zero[:], 0.0, ["zero"])
+    for s in range(5):
+        ts(T.br[:, :, 2 ** s:2 ** (s + 1)], T.br[:, :, 0:2 ** s], float(4 * 2 ** (4 - s)), None, OP.add, None, ["br"], ["br"])
+    act(T.IDN[:], T.ID[:, 0, :], AF.Identity, ["ID0"], ["IDN"], scale=DOWN)
+    act(T.topl[:], T.br[:], AF.Identity, ["br"], ["topl"], scale=2.0 ** -7)
+    act(T.IU[:], T.ID[:, 0, :], AF.Identity, ["ID0"], ["IU"], scale=UP)
+    act(T.top0[:], T.br[:, :, 0::2], AF.Identity, ["br"], ["top0"], scale=-8192.0)
+    act(T.ID[:, 10, :], T.ID[:, 0, :], AF.Identity, ["ID0"], ["IDu"], scale=-1024.0)
+    ms(T.tb0[0:1, 0:128], 0.0, ["tb0"])
+    ms(T.tb0[0:1, 128:256], -64.0 * 8192, ["tb0"])
+    ms(T.rows[0:1, 0, :], 280.0, ["rows"])
+    ms(T.rows[0:1, 1, :], 192.0 * 1024, ["rows"])
+    ms(T.rsb[:], 0.0, ["rsb"])
+    ms(T.WZ[:], 0.0, ["WZ"])
+    ts(T.pc[:, 1:2], T.pc[:, 0:1], 15, None, OP.bitwise_and, None, ["pc0"], ["pc1"])
+    ts(T.pc[:, 2:3], T.pc[:, 0:1], 4, None, OP.arith_shift_right, None, ["pc0"], ["pc2"])
+    cp(T.pf[:, 1:3], T.pc[:, 1:3], ["pc1", "pc2"], ["pf"])
+    P_, G_ = T.pf[:, 1:2], T.pf[:, 2:3]
+    cp(T.amf[:], T.ami[:], ["ami"], ["amf"])
+    mm(T.TG[:, 0:8, :], T.ones[0:1, 0:128], T.topl[0:1, :], True, False, ["ones", "topl"], ["TG"])
+    for b in range(2):
+        mm(T.TG[:, 0:8, 16 * b:16 * b + 16], T.amf[:, 128 * b:128 * b + 128], T.IDN[:], False, b == 1, ["amf", "IDN"], ["TG"])
+    cp(T.wf[:, 0:1], T.wi[:, 0:1], ["wi"], ["wf"])
+    ts(T.BW[:], T.io3[:], G_, T.wf[:, 0:1], OP.is_equal, OP.mult, ["io3", "pf", "wf"], ["BW"])
+    ts(T.WZ[:, 16::16], T.io1[:], G_, T.wf[:, 0:1], OP.is_equal, OP.mult, ["io1", "pf", "wf", "WZ"], ["WZ"])
+    cp(T.VA[:], T.TG[:, 0:8, :], ["TG"], ["VA"])
+    send(0, 0, "VA", "VB0")
+    key_weights([13, 2, 5, 8, 11, 14])
+    iota(T.kio[:], [[0, 8], [1, 32]], 0, 0, ["kio"])
+    iota(T.io2[:], [[0, 8], [1, 16]], 0, 0, ["io2"])
+    fill0 = -131072.0 - 31.0 / 64
+    ts(T.pf[:, 8:9], P_, 74.0, fill0, OP.mult, OP.add, ["pf"], ["pf8"])
+    ts(T.pf[:, 9:10], P_, 74.0, fill0 + 37, OP.mult, OP.add, ["pf"], ["pf8"])
+    ts(T.pf[:, 11:12], P_, 16.0 * DOWN, None, OP.mult, None, ["pf"], ["pf10"])
+    ts(T.vtmp[:], T.io4[:], 15.0, P_, OP.min, OP.is_equal, ["io4", "pf"], ["vtmp"])
+    ts(T.jb[:], T.io1[:], 256.0 * DOWN, T.pf[:, 11:12], OP.mult, OP.add, ["io1", "pf10"], ["jb"])
+    op("V", lambda: v.tensor_reduce(T.pf[:, 15:16], T.vtmp[:], AxisListType.X, OP.add), ["vtmp"], ["pe"])
+    ts(T.cx[:], T.jb[:], 4.0 * UP, None, OP.mult, None, ["jb"], ["cx"])
+    ts(T.pf[:, 16:17], T.pf[:, 15:16], -1.0, None, OP.mult, None, ["pe"], ["pn"])
+    E_, NE_ = T.pf[:, 15:16], T.pf[:, 16:17]
+
+    def make_u(between=None):
+        raw, big, small = T.Y0[:, 0:4, :], T.Y0[:, 8:12, :], T.Y0[:, 4, 0:8]
+        mm(raw, T.BW[:], T.Z[:], True, True, ["BW", "Z"], ["Y0"])
+        act(T.gu[:], raw, AF.Identity, ["Y0"], ["gu"], bias=192.0 - 0.5 + 2.0 ** -11, scale=2.0 ** -10)
+        if between:
+            between(0)
+        mm(big, T.rows[0:1, 1, :], T.ones[0:1, 0:128], True, False, ["rows", "ones"], ["Y0"])
+        mm(big, T.BW[:], T.Z[:], False, False, ["BW", "Z"], ["Y0"])
+        mm(big, T.ID[:, 10, :], T.gu[:], False, True, ["IDu", "gu"], ["Y0"])
+        if between:
+            between(1)
+        for e in (1, 0):
+            act(T.cm[:, 128 * e:128 * e + 128], big, AF.Identity, ["Y0"], ["cm"], bias=1.0, scale=2.0)
+        if between:
+            between(2)
+        for e in range(2):
+            act(T.u32[:, 128 * e:128 * e + 128], big, AF.Identity, ["Y0"], ["u32"], scale=1.0 / 32)
+            act(T.uk[:, 128 * e:128 * e + 128], big, AF.Identity, ["Y0", "pf8"], ["uk"], bias=T.pf[:, 8 + e:9 + e])
+        for r in range(16):
+            mm(small, T.WZ[:, 16 - r:144 - r], T.Z[:, r::16], r == 0, r == 15, ["WZ", "Z"], ["Y0"])
+        act(T.sf[:], small, AF.Copy, ["Y0"], ["sf"])
+
+    def columns():
+        cp(T.si[:], T.sf[:], ["sf"], ["si"])
+        ts(T.sj[:], T.si[:], 63, None, OP.bitwise_and, None, ["si"], ["sj"])
+        tt(T.sk[:], T.sj[:], T.cx[:], OP.add, ["sj", "cx"], ["sk"])
+        cp(T.offX[:], T.sk[:], ["sk"], ["offX"])
+
+    def turn_init(bk, name, h, top="0"):
+        o = bk[:, 8 * h:8 * h + 8, :]
+        mm(o, T["top" + top][0:1, :], T.ones[0:1, 0:256], True, False, ["top" + top, "ones"], [name])
+        mm(o, T.ones[0:1, 0:128], T["tb" + top][0:1, :], False, False, ["tb" + top, "ones"], [name])
+        if name == "Y2":
+            mm(o, T.ones[:, 0:128], T.rsb[:], False, False, ["rsb", "ones"], [name])
+
+    def half_init(bk, name, e):
+        o = bk[:, 4 * e:4 * e + 4, :]
+        mm(o, T.top0[0:1, :], T.ones[0:1, 0:128], True, False, ["top0", "ones"], [name])
+        if e == 1:
+            mm(o, T.ones[0:1, 0:128], T.tb0[0:1, 128:256], False, False, ["tb0", "ones"], [name])
+        if name == "Y2":
+            mm(o, T.ones[:, 0:128], T.rsb[:, 0:128], False, False, ["rsb", "ones"], [name])
+
+    def turn(h, src):
+        for bk, name in ((T.TG, "TG"), (T.Y2, "Y2")):
+            for e in range(2):
+                mm(bk[:, 8 * h + 4 * e:8 * h + 4 * e + 4, :], T[src][:, :, e::2], T.IU[:], False, e == 1, [src, "IU"], [name])
+
+    def hashing(h, off):
+        tt(T.pA[:], T.TG[:, 8 * h:8 * h + 8, :], T.cm[:], OP.mult, ["TG", "cm"], ["pA"])
+        ts(T.h1[:], T.pA[:], 5, None, OP.arith_shift_right, None, ["pA"], ["h1"])
+        tt(T.h2[:], T.Y2[:, 8 * h:8 * h + 8, :], T.h1[:], OP.add, ["Y2", "h1"], ["h2"])
+        ts(T.h1[:], T.h2[:], 8191, None, OP.bitwise_and, None, ["h2"], ["h1"])
+        cp(T[off][:], T.h1[:], ["h1"], [off])
+
+    def turn_hash_halves():
+        for e in (1, 0):
+            c = slice(128 * e, 128 * e + 128)
+            for bk, name in ((T.TG, "TG"), (T.Y2, "Y2")):
+                if e == 0:
+                    half_init(bk, name, 0)
+                mm(bk[:, 4 * e:4 * e + 4, :], T.VA[:, :, e::2], T.IU[:], False, True, ["VA", "IU"], [name])
+            tt(T.pA[:, c], T.TG[:, 4 * e:4 * e + 4, :], T.cm[:, c], OP.mult, ["TG", "cm"], ["pA"])
+            ts(T.h1[:, c], T.pA[:, c], 5, None, OP.arith_shift_right, None, ["pA"], ["h1"])
+            tt(T.h2[:, c], T.Y2[:, 4 * e:4 * e + 4, :], T.h1[:, c], OP.add, ["Y2", "h1"], ["h2"])
+            ts(T.h1[:, c], T.h2[:, c], 8191, None, OP.bitwise_and, None, ["h2"], ["h1"])
+            cp(T.offA[:, c], T.h1[:, c], ["h1"], ["offA%d" % e])
+
+    def gather(eng, dst, off, e, i0, i1):
+        c0, c1 = 128 * e + i0, 128 * e + i1
+        o, x = T[dst][:, 16 * c0:16 * c1], T.X[:, 0:8192].indirect(T[off][:, c0:c1])
+        key = "%s.%d%s" % (dst, e, eng)
+        if off == "offA":
+            off = "offA%d" % e
+        if eng == "V":
+            ts(o, x, E_, None, OP.add, None, XK + [off, "pe"], [key])
+        elif dst == "xg":
+            act(o, x, AF.Identity, XK + [off, "pe"], [key], bias=E_)
+        else:
+            act(o, x, AF.Copy, XK + [off], [key])
+
+    def allkeys(dst):
+        return ["%s.%d%s" % (dst, e, q) for e in range(2) for q in "VA"]
+
+    def keys(dst, bk, name, e, j):
+        for r in range(16):
+            k = 2 * r + e
+            mm(bk[j][:, :, k] if bk is YB else bk[j][:, k::32], T[dst][:, 2048 * e + r:2048 * e + 2048:16], T.WN[:, 16 * j:16 * j + 16],
+               e == 1 and r == 0, name == "X" and j == 0 and k == 30, ["%s.%dV" % (dst, e), "%s.%dA" % (dst, e), "WN"], ["%s%d" % (name, j)])
+
+    for b in range(2):
+        ts(T.BD[:, :, 16 * b:16 * b + 16], T.io3[:], G_, None, OP.is_equal, None, ["io3", "pf"], ["BD"])
+    ts(T.dp[:], T.io1[:], G_, None, OP.is_equal, None, ["io1", "pf"], ["dp"])
+    ts(T.dn[:], T.io1[:], G_, -1.0, OP.is_equal, OP.mult, ["io1", "pf"], ["dn"])
+    ms(T.HS[:, 128:136], 0.0, ["HS"])
+    ms(T.w[:, 255:256], 0.0, ["w"])
+    ms(T.OB[:, 255:256], 0.0, ["OB.w"])
+
+    def first_turn(k):
+        if k == 0:
+            half_init(T.TG, "TG", 1)
+            half_init(T.Y2, "Y2", 1)
+        if k == 2:
+            turn_hash_halves()
+    make_u(first_turn)
+    WK = ["W48.%d" % l for l in range(6)]
+    act(T.ID[:, 1, :], T.ID[:, 0, :], AF.Identity, ["ID0"], ["ID"], scale=BIG2)
+    act(T.ID[:, 2, :], T.ID[:, 0, :], AF.Identity, ["ID0"], ["ID"], scale=-BIG1)
+    act(T.WN[:], T.W48[:], AF.Identity, WK, ["WN"], scale=-1.0)
+    iota(T.inc[:], [[0, 128], [-4095, 2]], 2048, 0, ["inc"])
+    iota(T.HB[:], [[0, 136]], 0, 0, ["HB"])
+    iota(T.nd[:], [[0, 256]], -1, 0, ["nd"])
+
+    def late_constants():
+        act(T.WR[:, :, 0:1], T.W48[:], AF.Copy, WK, ["WR"])
+        ts(T.hold[:], T.io2[:], P_, None, OP.is_le, None, ["io2", "pf"], ["hold"])
+        act(T.r0[:], T.kio[:], AF.Sign, ["kio"], ["r0"], bias=31.0, scale=-1.0)
+        for s in range(5):
+            act(T.WR[:, :, 2 ** s:2 ** (s + 1)], T.WR[:, :, 0:2 ** s], AF.Copy, ["WR"], ["WR"])
+        ms(T.tb1[0:1, 0:128], 0.0, ["tb1"])
+        ms(T.tb1[0:1, 128:256], -4.0 * 8192, ["tb1"])
+        ts(T.hold[:, 0::16], T.hold[:, 0::16], 0.0, None, OP.mult, None, ["hold"], ["hold"])
+
+    def sums(j):
+        name = ("X0", "X1", "X2", "Y0")[j]
+        for q in range(4):
+            mm(T[name][:], T.ID[:, 0, :], T.X[:, 2048 * q + 512 * j:2048 * q + 512 * j + 512], q == 0, q == 3, ["ID0"] + XK, [name])
+
+    def store_sums(j):
+        name = ("X0", "X1", "X2", "Y0")[j]
+        act(T.S[:, 512 * j:512 * j + 512], T[name][:], AF.Copy, [name], ["S.%d" % j])
+        dma("S", T.yx[:, 512 * j:512 * j + 512], T.S[:, 512 * j:512 * j + 512], ["S.%d" % j], [])
+
+    def join_constants():
+        act(T.nc[:], T.kio[:], AF.Sign, ["kio"], ["nc"])
+        act(T.NK[:, 0::2], T.zero[:], AF.Copy, ["zero"], ["NK"])
+        act(T.NK[:, 1::2], T.kio[:], AF.Identity, ["kio"], ["NK"], scale=-1.0)
+        act(T.topf[:], T.br[:], AF.Identity, ["br"], ["topf"], scale=2.0 ** -7, bias=1.5)
+        for h in range(2):
+            act(T.tagc[:, 256 * h:256 * h + 256], T.br[:], AF.Identity, ["br"], ["tagc"], scale=-(2.0 ** -7))
+
+    def tag_constants():
+        for n_, c_ in ((12, -1.0), (3, 2.0), (4, 64.0), (5, -96.0), (6, -48.0), (7, -24.0), (8, -12.0), (9, -7.0)):
+            act(T.ID[:, n_, :], T.ID[:, 0, :], AF.Identity, ["ID0"], ["IDt"], scale=c_ / 128)
+        act(T.top1[:], T.br[:, :, 0:16], AF.Identity, ["br"], ["top1"], scale=-8192.0)
+
+    for t in range(RO):
+        last = t == RO - 1
+        VB, LB, JB = "VB%d" % t, "LB%d" % t, "JB%d" % t
+        s1, s0 = SPLIT[min(t, 1)]
+        if t > 0:
+            gather("A", "xg", "offA", 1, s1, 128)
+            gather("A", "xg", "offA", 0, s0, 128)
+        turn_init(T.TG, "TG", 1)
+        turn_init(T.Y2, "Y2", 1)
+        turn(1, VB)
+        if t > 0:
+            gather("V", "xg", "offA", 1, 0, s1)
+            gather("V", "xg", "offA", 0, 0, s0)
+        else:
+            late_constants()
+        hashing(1, "offB")
+        if t == 0:
+            gather("A", "xg", "offA", 1, s1, 128)
+            gather("A", "xg", "offA", 0, s0, 128)
+            gather("V", "xg", "offA", 1, 0, s1)
+            gather("V", "xg", "offA", 0, 0, s0)
+        tt(T.TG[:, 0:8, :], T.TG[:, 0:8, :], T.u32[:], OP.mult, ["TG", "u32"], ["TG"])
+        tt(T.fa[:], T.TG[:, 0:8, :], T.uk[:], OP.add, ["TG", "uk"], ["fa"])
+        cp(T.fbf[:], T.fa[:], ["fa"], ["fbf"])
+        gather("A", "yg", "offB", 1, 0, 128)
+        gather("A", "yg", "offB", 0, 0, 128)
+        if t == 0:
+            join_constants()
+        for j in range(3):
+            keys("xg", XB, "X", 1, j)
+        keys("xg", XB, "X", 0, 0)
+        keys("xg", XB, "X", 0, 1)
+        r = "r0"
+        for l in range(6):
+            if l < 3:
+                src, c0, kx, w, kw = XB[l], 0, "X%d" % l, T.w, "w"
+            else:
+                src, c0, kx, w, kw = T.NV, 512 * (l - 3) + 256, "NV.%d" % l, T.OB, "OB.w"
+            nv = src[:, c0:c0 + 256]
+            scan(w[:, 254::-1], src[:, c0 + 255:(c0 if c0 else 0):-1], T[r][:, 254::-1], OP.min, OP.mult, [kx, r], [kw])
+            if l < 5:
+                tt(T.lt[:], nv, w[:, 0:256], OP.is_gt, [kx, kw], ["lt"])
+                if l < 2:
+                    mm(lev(XB, l + 1), T.ID[:, 1, :], T.lt[:], False, True, ["ID", "lt"], ["X%d" % (l + 1)])
+                if l == 0:
+                    keys("xg", XB, "X", 0, 2)
+                if l == 2:
+                    for j in range(3):
+                        keys("yg", YB, "Y", 1, j)
+                r = "rA" if l % 2 == 0 else "rB"
+                tt(T[r][:], nv, w[:, 0:256], OP.is_ge, [kx, kw], [r])
+                if l >= 2:
+                    tt(T.NV[:, 512 * (l - 2) + 256:512 * (l - 2) + 512], lev(XB, l + 1), T.lt[:], OP.add, ["X%d" % (l - 2), "lt"], ["NV.%d" % (l + 1)])
+            else:
+                tt(T.LT[:], nv, w[:, 0:256], OP.is_gt, [kx, kw], ["LT"])
+        for l in range(3):
+            act(T.NV[:, 512 * l:512 * l + 256], lev(XB, l), AF.Copy, ["X%d" % l], ["NV.%d" % l])
+        mm(T.TG[:, 8, 0:8], T.IU[:], T.jb[:], True, False, ["IU", "jb"], ["TG"])
+        send(2, t, "LT", LB)
+        keys("yg", YB, "Y", 0, 2)
+        keys("yg", YB, "Y", 0, 1)
+        scan(T.KF[:, ::-1], T.inc[:, ::-1], T.LT[:, ::-1], OP.add, OP.mult, ["inc", "LT"], ["KF"])
+        cp(T.HB[:, 0:128:16], T.KF[:, 0::32], ["KF"], ["HB"])
+        scan(T.HS[:, 0:128], T.hold[:], T.HB[:, 0:128], OP.mult, OP.add, ["hold", "HB"], ["HS"])
+        mm(T.TG[:, 8, 0:8], T.HB[:, 1:129], T.dp[:], False, False, ["HB", "dp"], ["TG"])
+        mm(T.TG[:, 8, 0:8], T.HS[:, 0:128], T.dp[:], False, False, ["HS", "dp"], ["TG"])
+        mm(T.TG[:, 8, 0:8], T.HS[:, 1:129], T.dn[:], False, True, ["HS", "dn"], ["TG"])
+        cp(T.J[:], T.TG[:, 8, 0:8], ["TG"], ["J"])
+        send(1, t, "J", JB)
+        keys("yg", YB, "Y", 0, 0)
+        ts(T.M[:], T.xg[:, 0:4096].indirect(T.J[:, 0:8]), NE_, None, OP.add, None, allkeys("xg") + ["J", "pn"], ["M"])
+        tt(T.ge[:], T.Z[:], T.M[:], OP.is_ge, ["Z", "M"], ["ge"])
+        for j in (2, 1, 0):
+            mm(YB[j][:], T.M[:], T.WR[:, 16 * j:16 * j + 16, :], False, True, ["M", "WR"], ["Y%d" % j])
+            if j == 2:
+                mm(T.TG[:, 0:8, :], T.ge[:], T.BD[:], True, True, ["ge", "BD"], ["TG"])
+        act(T.cY[:, 0:512], T.Y2[:], AF.Copy, ["Y2"], ["cY.2"])
+        act(T.bonB[:], T.TG[:, 0:8, :], AF.Relu, ["TG"], ["bonB"], bias=-6.0, scale=1.0)
+        act(T.cY[:, 1024:1536], T.Y0[:], AF.Copy, ["Y0"], ["cY.0"])
+        act(T.bonA[:], T.TG[:, 0:8, :], AF.Relu, ["TG"], ["bonA"], bias=7.0, scale=-1.0)
+        columns()
+        tt(T.xs[:], T.X[:, 0:8192].indirect(T.offX[:, 0:8]), T.M[:], OP.add, XK + ["offX", "M"], ["xs"])
+        ts(T.xh[:], T.xs[:], 1, None, OP.arith_shift_right, None, ["xs"], ["xh"])
+        cp(T.cY[:, 512:1024], T.Y1[:], ["Y1"], ["cY.1"])
+        act(T.nf[:], T.bonA[:, 0::32], AF.Sign, ["bonA"], ["nf"])
+        act(T.fr[:], T.bonB[:, 0::32], AF.Sign, ["bonB"], ["fr"])
+        act(T.gf[:], T.fbf[:], AF.Identity, ["fbf"], ["gf"], bias=192.0 - 0.5 + 2.0 ** -14, scale=2.0 ** -13)
+        sumA, sumB = T.TG[:, 8:16, :], T.OB[:, 256:512]
+        mm(sumB, T.ID[:, 1, :], T[LB][:], True, False, ["ID", LB], ["OB.s"])
+        for c in (0, 1, -1, 4, 5, 2, 3):
+            if c < 0:
+                mm(sumB, T.ID[:, 2, :], T.bonB[:], False, False, ["ID", "bonB"], ["OB.s"])
+            else:
+                mm(sumB, T.ID[:, 0, :], T.cY[:, 256 * c:256 * c + 256], False, c == 3, ["ID0", "cY.%d" % (2 - c // 2)], ["OB.s"])
+        mm(sumA, T.ID[:, 1, :], T.LT[:], True, False, ["ID", "LT"], ["TG"])
+        mm(sumA, T.ID[:, 2, :], T.bonA[:], False, False, ["ID", "bonA"], ["TG"])
+        cp(T.X[:, 0:8192].indirect(T.offX[:, 0:8]), T.xh[:], ["xh", "offX"], XK)
+        ts(T.y0[:], T.yg[:, 0:4096].indirect(T[JB][:, 0:8]), E_, None, OP.add, None, allkeys("yg") + [JB, "pe"], ["y0"])
+        for j in range(3):
+            mm(XB[j][:], T.y0[:], T.WR[:, 16 * j:16 * j + 16, :], True, True, ["y0", "WR"], ["X%d" % j])
+        mm(T.Y2[:, 0:8, :], T.ones[0:1, 0:128], T.topf[0:1, :], True, False, ["ones", "topf"], ["Y2"])
+        ts(T.KB[:], sumB, 0.0, None, OP.is_le, None, ["OB.s"], ["KB"])
+        for j in range(3):
+            tt(T.cA[:, 512 * j:512 * j + 512], XB[j][:], T.NV[:, 512 * j:512 * j + 512], OP.add, ["X%d" % j, "NV.%d" % j, "NV.%d" % (j + 3)], ["cA.%d" % j])
+            for c in (2 * j, 2 * j + 1):
+                mm(sumA, T.ID[:, 0, :], T.cA[:, 256 * c:256 * c + 256], False, c == 5, ["ID0", "cA.%d" % j], ["TG"])
+            if j < 2:
+                mm(T.Y2[:, 0:8, j::2], T.fbf[:, 128 * j:128 * j + 128], T.IDN[:], False, False, ["fbf", "IDN"], ["Y2"])
+        if last:
+            sums(0)
+            store_sums(0)
+        ts(T.IL[:, 512::2], T.KB[:], -1.0, 1.0, OP.mult, OP.add, ["KB"], ["nkB"])
+        tt(T.zd[:], T.yg[:, 0:4096].indirect(T[JB][:, 0:8]), T.Z[:], OP.subtract, allkeys("yg") + [JB, "Z"], ["zd"])
+        if not last:
+            act(T.Z[:], T.zd[:], AF.Abs, ["zd"], ["Z"])
+            act(T.G5[:, 0:256], T.LT[:], AF.Identity, ["LT"], ["G5", "rs"], acc=T.rs[:, 0:1])
+            act(T.rsb[:], T.zero[:], AF.Identity, ["zero", "rs"], ["rsb"], bias=T.rs[:, 0:1])
+        else:
+            act(T.zd[:], T.zd[:], AF.Abs, ["zd"], ["zd"])
+            dma("S", T.yz[:], T.zd[:], ["zd"], [])
+        scan(T.cB[:], T.nc[:], T.KB[:], OP.mult, OP.add, ["nc", "KB"], ["cB"])
+        tt(T.hA[:], T.cB[:, 31::32], T.nf[:], OP.mult, ["cB", "nf"], ["hA"])
+        ts(T.KA[:], sumA, 0.0, None, OP.is_le, None, ["TG"], ["KA"])
+        mm(T.TG[:], T.rows[0:1, 0, :], T.ones[0:1, :], True, False, ["rows", "ones"], ["TG"])
+        mm(T.TG[:], T.ones[0:1, 0:128], T.tagc[0:1, :], False, False, ["tagc", "ones"], ["TG"])
+        ts(T.IL[:, 0:512:2], T.KA[:], -1.0, 1.0, OP.mult, OP.add, ["KA"], ["nkA"])
+        tt(T.KA[:, 0::32], T.KA[:, 0::32], T.hA[:], OP.add, ["KA", "hA", "nkA"], ["KA"])
+        if t == 0:
+            tag_constants()
+        mm(T.TG[:], T.ID[:, 3, :], T.IL[:, 0::2], False, False, ["IDt", "nkA", "nkB"], ["TG"])
+        for e in range(2):
+            mm(T.Y2[:, 0:8, e::2], T.gf[:, 128 * e:128 * e + 128], T.ID[:, 12, :], False, e == 1, ["gf", "IDt"], ["Y2"])
+        scan(T.IL[:, 1:512:2], T.nc[:], T.KA[:], OP.mult, OP.add, ["nc", "KA"], ["ccA"])
+        tt(T.hB[:], T.IL[:, 63:512:64], T.fr[:], OP.mult, ["ccA", "fr"], ["hB"])
+        scan(T.DD[:, 0:512], T.NK[:], T.IL[:, 0:512], OP.mult, OP.add, ["NK", "nkA", "ccA"], ["dd.a"])
+        off = [192.0 - 2.0 ** -s - 0.5 + 2.0 ** -(s + 1) for s in range(6)]
+        for s in (5, 4):
+            act(T["G%d" % s][:, 0:256], T.DD[:, 1:512:2], AF.Identity, ["dd.a"], ["G%d" % s], bias=off[s], scale=2.0 ** -s)
+        tt(T.KB[:, 0::32], T.KB[:, 0::32], T.hB[:], OP.add, ["KB", "hB"], ["KB"])
+        scan(T.IL[:, 513::2], T.nc[:], T.KB[:], OP.mult, OP.add, ["nc", "KB"], ["ccB"])
+        scan(T.DD[:, 512:1024], T.NK[:], T.IL[:, 512:1024], OP.mult, OP.add, ["NK", "nkB", "ccB", "dd.a"], ["dd"])
+        mm(T.TG[:], T.ID[:, 4, :], T.DD[:, 1::2], False, False, ["IDt", "dd"], ["TG"])
+        for s in (5, 4):
+            act(T["G%d" % s][:, 256:512], T.DD[:, 513::2], AF.Identity, ["dd"], ["G%d" % s], bias=off[s], scale=2.0 ** -s)
+        for s in (1, 2, 3):
+            ts(T["G%d" % s][:], T.DD[:, 1::2], 2.0 ** -s, off[s], OP.mult, OP.add, ["dd"], ["G%d" % s])
+        for s in (1, 5, 2, 4, 3):
+            mm(T.TG[:], T.ID[:, 4 + s, :], T["G%d" % s][:], False, s == 3, ["IDt", "G%d" % s], ["TG"])
+        if last:
+            for j in (1, 2, 3):
+                sums(j)
+                store_sums(j)
+        else:
+            make_u()
+        tt(T.nd[:, 0::32], T.IL[:, 63:512:64], T.IL[:, 575::64], OP.max, ["ccA", "ccB"], ["nd"])
+        scan(T.nr[:], T.nc[:], T.nd[:], OP.mult, OP.add, ["nc", "nd"], ["nr"])
+        tt(T.Y2[:, 8:16, :], T.Y2[:, 0:8, :], T.nr[:], OP.max, ["Y2", "nr"], ["Y2.f"])
+        for h, src in ((0, "VA"), (1, VB)):
+            tt(T.E0[:, 8 * h:8 * h + 8, :], T.TG[:, 8 * h:8 * h + 8, 0::2], T[src][:, :, 0::2], OP.add, ["TG", src], ["E0"])
+            tt(T.Y1[:, 8 * h:8 * h + 8, 0:16], T.TG[:, 8 * h:8 * h + 8, 1::2], T[src][:, :, 1::2], OP.add, ["TG", src], ["Y1"])
+        for s in range(4):
+            ei, eo = ("E0", "E1") if s % 2 == 0 else ("E1", "E0")
+            ki, ko = ("Y1", "TG") if s % 2 == 0 else ("TG", "Y1")
+            for hi, alu in ((0, OP.min), (1, OP.max)):
+                for par in range(2):
+                    o, ok = (T[eo], eo) if par == 0 else (T[ko], ko)
+                    tt(o[:, :, 8 * hi:8 * hi + 8], T[ei][:, :, par::2], T[ki][:, :, par:16:2], alu, [ei, ki], [ok])
+        for hi, alu in ((0, OP.min), (1, OP.max)):
+            tt(T.AP[:, :, 16 * hi:16 * hi + 16], T.E0[:, 0:8, :], T.Y1[:, 0:8, 0:16], alu, ["E0", "Y1"], ["AP"])
+            tt(T.TG[:, 0:8, 16 * hi:16 * hi + 16], T.E0[:, 8:16, :], T.Y1[:, 8:16, 0:16], alu, ["E0", "Y1"], ["TG"])
+        if not last:
+            half_init(T.Y2, "Y2", 1)
+        tt(T.v1[:], T.AP[:], T.TG[:, 0:8, :], OP.min, ["AP", "TG"], ["v1"])
+        if not last:
+            half_init(T.TG, "TG", 1)
+            tt(T.VA[:], T.v1[:], T.Y2[:, 8:16, :], OP.min, ["v1", "Y2.f"], ["VA"])
+            send(0, t + 1, "VA", "VB%d" % (t + 1))
+            turn_hash_halves()
+        else:
+            turn_init(T.TG, "TG", 0, "1")
+            for b in range(2):
+                tt(T.VL[:, 128 * b:128 * b + 128], T.v1[:, :, 16 * b:16 * b + 16], T.Y2[:, 8:16, 16 * b:16 * b + 16], OP.min, ["v1", "Y2.f"], ["VL.%d" % b])
+                mm(T.TG[:, 4 * b:4 * b + 4, :], T.VL[:, 128 * b:128 * b + 128], T.IU[:], False, b == 1, ["VL.%d" % b, "IU"], ["TG"])
+            cp(T.amf[:], T.TG[:, 0:8, :], ["TG"], ["amf"])
+            dma("S", T.ya[:], T.amf[:], ["amf"], [])
+    plan["emit"](g, T)

@@ -8,7 +8,8 @@ BIG1 = 2.0 ** 90
 BIG2 = 2.0 ** 98
 DOWN = 2.0 ** -20
 UP = 2.0 ** 20
-SPLIT = [(64, 64), (32, 32)]
+MAGIC = 1.5 * 2.0 ** 23
+SPLIT = [(64, 72), (64, 56)]
 NENG = 8
 
 F, B, I, U = "float32", "bfloat16", "int32", "uint16"
@@ -18,32 +19,42 @@ def _s(shape, d):
     return ("sbuf", [128] + list(shape), d)
 
 
+IDS = {"1": 1.0, "big": BIG2, "-1": -1.0, "1/2": 0.5, "-1024": -1024.0, "g1": -96.0 / 128, "g2": -48.0 / 128, "g3": -24.0 / 128,
+       "g4": -12.0 / 128, "g5": -7.0 / 128, "-1/128": -1.0 / 128, "-2/128": -2.0 / 128, "-64": -64.0}
+OS = {"1": 1.0, "1/2": 0.5}
+LS = {"1": 1.0, "-1": -1.0}
+BDS = {"-1/16": -1.0 / 16, "big": -BIG1 / 16}
+ROWS = {"own": -16, "got": -1, "len": 0}
+TOPS = [(0, -4096.0), (1, -4096.0), (0, 32.0), (1, 32.0), (0, 0.0), (1, 0.0)]
+
 SCRATCH = {
     "X": _s([8192], B), "xg": _s([4096], B), "yg": _s([4096], B), "S": _s([2048], F),
     "ami": _s([256], I), "amf": _s([256], F), "Z": _s([128], B), "wi": _s([8], I), "wf": _s([8], F),
     "VA": _s([8, 32], F), "VL": _s([256], F), "VB0": _s([8, 32], F), "VB1": _s([8, 32], F), "VB2": _s([8, 32], F),
     "LT": _s([256], B), "LB0": _s([256], B), "LB1": _s([256], B), "LB2": _s([256], B),
     "J": _s([8], U), "JB0": _s([8], U), "JB1": _s([8], U), "JB2": _s([8], U),
-    "pA": _s([256], I), "fa": _s([256], I), "h1": _s([256], I), "h2": _s([256], I), "offA": _s([256], U), "offB": _s([256], U),
-    "fbf": _s([256], F), "cm": _s([256], F), "uk": _s([256], F), "u32": _s([256], F), "gu": _s([128], B), "gf": _s([256], B),
-    "NV": _s([1536], F), "si": _s([8], I), "sj": _s([8], I), "sk": _s([8], F), "sf": _s([8], F), "offX": _s([8], U),
+    "h1": _s([256], I), "h2": _s([256], I), "offA": _s([256], U), "offB": _s([256], U),
+    "ft": _s([256], F), "f1": _s([256], F), "fbf": _s([256], F), "gf": _s([256], B),
+    "cm": _s([128], F), "Dm": _s([128], F), "u32": _s([128], F), "gu": _s([128], B),
+    "NV": _s([1536], F), "si": _s([8], I), "sj": _s([8], I), "sk": _s([8], F), "offX": _s([8], U),
     "w": _s([256], F), "r0": _s([256], B), "rA": _s([256], B), "rB": _s([256], B), "lt": _s([256], B),
-    "KF": _s([256], F), "HB": _s([136], F), "HS": _s([136], F), "hold": _s([128], F), "inc": _s([256], F), "M": _s([128], B), "y0": _s([128], B), "ge": _s([128], B),
-    "bonA": _s([256], B), "bonB": _s([256], B), "cA": _s([1536], B), "cY": _s([1536], B),
-    "IL": _s([1024], B), "DD": _s([1024], B), "NK": _s([512], B), "KA": _s([256], B), "KB": _s([256], B),
-    "cB": _s([256], B), "fr": _s([8], B), "nf": _s([8], B), "hA": _s([8], B), "hB": _s([8], B),
+    "KF": _s([256], F), "HB": _s([136], F), "HS": _s([136], F), "hold": _s([128], F), "inc": _s([256], F), "B16": _s([128], B), "M": _s([128], B), "y0": _s([128], B), "ge": _s([128], B),
+    "fr": _s([128], B), "nf": _s([128], B), "mm": _s([128], B), "LTt": _s([256], B), "KA": _s([256], B), "KB": _s([256], B), "s2": _s([256], B),
+    "sl": _s([8], F), "offS": _s([8], U), "xd": _s([128], F), "xp": _s([128], F),
+    "cA": _s([1536], B), "cY": _s([1536], B), "DA": _s([256], B), "DB": _s([256], B), "nr": _s([256], B),
     "G1": _s([512], B), "G2": _s([512], B), "G3": _s([512], B), "G4": _s([512], B), "G5": _s([512], B),
     "E0": _s([16, 16], F), "E1": _s([16, 16], F), "AP": _s([8, 32], F), "v1": _s([8, 32], F),
-    "nd": _s([256], B), "nc": _s([256], B), "nr": _s([256], B),
-    "xs": _s([128], I), "xh": _s([128], I), "zd": _s([128], F),
-    "rs": _s([8], F), "rsb": _s([256], B),
-    "ones": _s([512], B), "zero": _s([256], B), "ID": _s([13, 128], B), "IU": _s([128], F), "IDN": _s([128], F),
-    "pc": _s([16], I), "pf": _s([24], F), "io1": _s([8], F), "io2": _s([128], F), "io3": _s([128], F), "io4": _s([6], F), "kio": _s([256], B),
-    "vtmp": _s([6], F), "W48": _s([48], B), "WN": _s([48], B), "WR": _s([48, 32], B),
-    "BD": _s([8, 32], B), "BW": _s([128], B), "WZ": _s([144], B),
-    "br": _s([8, 32], B), "top0": _s([128], B), "top1": _s([128], B), "tb0": _s([256], B), "tb1": _s([256], B),
-    "topl": _s([256], B), "topf": _s([256], B), "tagc": _s([512], B), "rows": _s([3, 128], B),
-    "dp": _s([8], F), "dn": _s([8], F), "jb": _s([8], F), "cx": _s([8], F),
+    "zd": _s([128], F),
+    "rs": _s([8], F), "kc": _s([8], F),
+    "ones": _s([512], B), "onesf": _s([128], F), "ID": _s([len(IDS), 128], B), "IU": _s([128], F), "IDN": _s([128], F),
+    "OM": _s([len(OS), 128], B), "LM": _s([len(LS), 128], B), "OT": _s([2, 128], B), "tri": _s([128], B), "dia": _s([128], B),
+    "pc": _s([16], I), "pf": _s([24], F), "io1": _s([8], F), "io3": _s([128], F), "io4": _s([6], F), "io5": _s([128], F),
+    "io2": _s([128], F), "io6": _s([8], F), "zero": _s([128], B),
+    "vtmp": _s([6], F), "WN": _s([48], B), "WR": _s([48, 32], B), "NE": _s([128], B),
+    "BD": _s([len(BDS), 8, 32], B), "BW": _s([128], B), "WZ": _s([144], B),
+    "br": _s([8, 32], B), "TP": _s([len(TOPS), 128], B), "CT": _s([256], B),
+    "topl": _s([256], B), "topf": _s([256], B), "rows": _s([len(ROWS), 256], B), "urow": _s([128], B),
+    "dp": _s([8], F), "dn": _s([8], F), "jb": _s([8], F), "cx": _s([8], F), "cs": _s([8], F),
     "X0": ("psum", [128, 512], F), "X1": ("psum", [128, 512], F), "X2": ("psum", [128, 512], F),
     "Y0": ("psum", [128, 16, 32], F), "Y1": ("psum", [128, 16, 32], F), "Y2": ("psum", [128, 16, 32], F),
     "TG": ("psum", [128, 16, 32], F), "OB": ("psum", [128, 512], F),
@@ -159,19 +170,19 @@ def rank_program(g, core, T, topo):
     def cp(o, x, R, W):
         op("V", lambda: v.tensor_copy(o, x), R, W)
 
-    def ms(o, c, W):
-        op("V", lambda: v.memset(o, c), (), W)
+    def ms(o, c, W, R=()):
+        op("V", lambda: v.memset(o, c), R, W)
 
     def scan(o, x, y, o0, o1, R, W):
         op("V", lambda: v.tensor_tensor_scan(o, x, y, 0.0, o0, o1), R, W)
 
     def act(o, x, f, R, W, bias=0.0, scale=1.0, acc=None):
-        if f == AF.Copy:
-            op("A", lambda: a.activation(o, x, f), R, W)
-        elif acc is None:
-            op("A", lambda: a.activation(o, x, f, bias=bias, scale=scale), R, W)
-        else:
+        if acc is not None:
             op("A", lambda: a.activation(o, x, f, accum_out=acc), R, W)
+        elif f == AF.Copy:
+            op("A", lambda: a.activation(o, x, f), R, W)
+        else:
+            op("A", lambda: a.activation(o, x, f, bias=bias, scale=scale), R, W)
 
     def mm(o, l, r, st, sp, R, W):
         op("P", lambda: pe.matmul(o, l, r, st, sp), R, W)
@@ -201,10 +212,25 @@ def rank_program(g, core, T, topo):
 
     XB, YB = [T.X0, T.X1, T.X2], [T.Y0, T.Y1, T.Y2]
 
-    def lev(bk, l):
-        if bk is YB:
-            return bk[l % 3][:, (l // 3) * 8:(l // 3) * 8 + 8, :]
-        return bk[l % 3][:, (l // 3) * 256:(l // 3) * 256 + 256]
+    def lev(l):
+        return XB[l % 3][:, (l // 3) * 256:(l // 3) * 256 + 256]
+
+    def pick(buf, names, name):
+        return T[buf][:, list(names).index(name)]
+
+    def ident(name):
+        return pick("ID", IDS, name)
+
+    def row(name):
+        return T.rows[0:1, list(ROWS).index(name), :]
+
+    def part(bk, c0, n):
+        if bk in ("X0", "X1", "X2", "OB"):
+            return T[bk][:, c0:c0 + n]
+        return T[bk][:, c0 // 32:(c0 + n) // 32, :]
+
+    def half(name, h):
+        return T[name][:, 128 * h:128 * h + 128]
 
     dma("S", T.ami[:], T.am[:], [], ["ami"])
     dma("A", T.Z[:], T.zv[:], [], ["Z"])
@@ -215,38 +241,57 @@ def rank_program(g, core, T, topo):
 
     ms(T.ones[:], 1.0, ["ones"])
     iota(T.pc[:, 0:1], [[0, 1]], 0, 1, ["pc0"], flt=False)
-    op("G", lambda: g.affine_select(T.ID[:, 0, :], T.ones[:, 0:128], [[-1, 128]], OP.is_equal, 0.0, 0, 1), ["ones"], ["ID0"])
+    ms(T.zero[:], 0.0, ["zero"])
+
+    def diagonals(which):
+        for n_ in which:
+            op("G", lambda n_=n_: g.affine_select(ident(n_), T.zero[:], [[-1, 128]], OP.not_equal, IDS[n_], 0, 1), ["zero"], ["ID." + n_])
+    diagonals(["1"])
     iota(T.io3[:], [[1, 8], [0, 16]], 0, 0, ["io3"])
     iota(T.io1[:], [[1, 8]], 0, 0, ["io1"])
     iota(T.io4[:], [[3, 6]], 2, 0, ["io4"])
-    ms(T.W48[:], 0.0, ["W48"])
+    diagonals(["-1024"])
+    ms(T.WN[:], 0.0, ["WN"])
 
     def key_weights(rows):
         for p in rows:
             l = p // 3
             c0 = 16 * (l % 3) + 8 * (l // 3)
-            op("G", lambda p=p, l=l, c0=c0: g.affine_select(T.W48[:, c0:c0 + 8], T.W48[:, c0:c0 + 8], [[-16, 8]], OP.not_equal,
-                                                            2.0 ** (48 - 25 * l + 8 * (2 - p % 3)), -p, 1), ["W48.%d" % l, "W48"], ["W48.%d" % l])
-    key_weights([0, 3, 6, 9, 12, 15, 1, 4, 7, 10])
+            op("G", lambda p=p, l=l, c0=c0: g.affine_select(T.WN[:, c0:c0 + 8], T.WN[:, c0:c0 + 8], [[-16, 8]], OP.not_equal,
+                                                            -2.0 ** (48 - 25 * l + 8 * (2 - p % 3)), -p, 1), ["WN.%d" % l, "WN"], ["WN.%d" % l])
+
+    def scaled(buf, names, which):
+        first = list(names)[0]
+        for n_ in which:
+            act(pick(buf, names, n_), pick(buf, names, first), AF.Identity, ["%s.%s" % (buf, first)], ["%s.%s" % (buf, n_)],
+                scale=names[n_] / names[first])
+    key_weights([0, 3, 6, 9, 12, 15, 1])
     ms(T.br[:, :, 0:1], 0.0, ["br"])
-    ms(T.zero[:], 0.0, ["zero"])
+    ms(T.TP[:], 0.0, ["TP"])
+    fills = [(T.urow[0:1, :], 192.0 * 1024, "urow"), (T.kc[:, 0:1], 4096.0 * 33 - 2.0 ** 23, "kc"), (T.WZ[:], 0.0, "WZ"),
+             (T.w[:, 255:256], 0.0, "w"), (T.OB[:, 255:256], 0.0, "OB")]
     for s in range(5):
         ts(T.br[:, :, 2 ** s:2 ** (s + 1)], T.br[:, :, 0:2 ** s], float(4 * 2 ** (4 - s)), None, OP.add, None, ["br"], ["br"])
-    act(T.IDN[:], T.ID[:, 0, :], AF.Identity, ["ID0"], ["IDN"], scale=DOWN)
-    act(T.topl[:], T.br[:], AF.Identity, ["br"], ["topl"], scale=2.0 ** -7)
-    act(T.IU[:], T.ID[:, 0, :], AF.Identity, ["ID0"], ["IU"], scale=UP)
-    act(T.top0[:], T.br[:, :, 0::2], AF.Identity, ["br"], ["top0"], scale=-8192.0)
-    act(T.ID[:, 10, :], T.ID[:, 0, :], AF.Identity, ["ID0"], ["IDu"], scale=-1024.0)
-    ms(T.tb0[0:1, 0:128], 0.0, ["tb0"])
-    ms(T.tb0[0:1, 128:256], -64.0 * 8192, ["tb0"])
-    ms(T.rows[0:1, 0, :], 280.0, ["rows"])
-    ms(T.rows[0:1, 1, :], 192.0 * 1024, ["rows"])
-    ms(T.rsb[:], 0.0, ["rsb"])
-    ms(T.WZ[:], 0.0, ["WZ"])
+        ms(fills[s][0], fills[s][1], [fills[s][2]])
+    act(T.IDN[:], ident("1"), AF.Identity, ["ID.1"], ["IDN"], scale=DOWN)
+    act(T.topl[0:1, :], T.br[0:1, :, :], AF.Identity, ["br"], ["topl"], scale=2.0 ** -7)
+    act(T.IU[:], ident("1"), AF.Identity, ["ID.1"], ["IU"], scale=UP)
+
+    def tops(which):
+        for n_ in which:
+            e, c = TOPS[n_]
+            act(T.TP[0:1, n_, :], T.br[0:1, :, 0::2] if c else T.br[0:1, :, 0:16], AF.Identity, ["br", "TP"], ["TP.a%d" % n_], scale=-8192.0)
+            if e:
+                ms(T.TP[32:33, n_, :], (-64.0 if c else -4.0) * 8192, ["TP.b%d" % n_])
+            if c:
+                ms(T.TP[64:65, n_, :], c, ["TP.b%d" % n_])
+    tops([0, 1, 2, 3])
     ts(T.pc[:, 1:2], T.pc[:, 0:1], 15, None, OP.bitwise_and, None, ["pc0"], ["pc1"])
-    ts(T.pc[:, 2:3], T.pc[:, 0:1], 4, None, OP.arith_shift_right, None, ["pc0"], ["pc2"])
-    cp(T.pf[:, 1:3], T.pc[:, 1:3], ["pc1", "pc2"], ["pf"])
-    P_, G_ = T.pf[:, 1:2], T.pf[:, 2:3]
+    ts(T.pc[:, 2:3], T.pc[:, 0:1], 4, None, OP.arith_shift_right, None, ["pc0"], ["pc1"])
+    ts(T.pc[:, 3:4], T.pc[:, 0:1], 31, None, OP.bitwise_and, None, ["pc0"], ["pc1"])
+    ts(T.pc[:, 4:5], T.pc[:, 0:1], 5, None, OP.arith_shift_right, None, ["pc0"], ["pc1"])
+    cp(T.pf[:, 1:5], T.pc[:, 1:5], ["pc1"], ["pf"])
+    P_, G_, K_, Q_ = T.pf[:, 1:2], T.pf[:, 2:3], T.pf[:, 3:4], T.pf[:, 4:5]
     cp(T.amf[:], T.ami[:], ["ami"], ["amf"])
     mm(T.TG[:, 0:8, :], T.ones[0:1, 0:128], T.topl[0:1, :], True, False, ["ones", "topl"], ["TG"])
     for b in range(2):
@@ -256,228 +301,299 @@ def rank_program(g, core, T, topo):
     ts(T.WZ[:, 16::16], T.io1[:], G_, T.wf[:, 0:1], OP.is_equal, OP.mult, ["io1", "pf", "wf", "WZ"], ["WZ"])
     cp(T.VA[:], T.TG[:, 0:8, :], ["TG"], ["VA"])
     send(0, 0, "VA", "VB0")
-    key_weights([13, 2, 5, 8, 11, 14])
-    iota(T.kio[:], [[0, 8], [1, 32]], 0, 0, ["kio"])
+    key_weights([4, 7, 10, 13, 2, 5, 8, 11, 14])
+    iota(T.io5[:], [[1, 4], [0, 32]], 0, 0, ["io5"])
     iota(T.io2[:], [[0, 8], [1, 16]], 0, 0, ["io2"])
-    fill0 = -131072.0 - 31.0 / 64
-    ts(T.pf[:, 8:9], P_, 74.0, fill0, OP.mult, OP.add, ["pf"], ["pf8"])
-    ts(T.pf[:, 9:10], P_, 74.0, fill0 + 37, OP.mult, OP.add, ["pf"], ["pf8"])
-    ts(T.pf[:, 11:12], P_, 16.0 * DOWN, None, OP.mult, None, ["pf"], ["pf10"])
-    ts(T.vtmp[:], T.io4[:], 15.0, P_, OP.min, OP.is_equal, ["io4", "pf"], ["vtmp"])
-    ts(T.jb[:], T.io1[:], 256.0 * DOWN, T.pf[:, 11:12], OP.mult, OP.add, ["io1", "pf10"], ["jb"])
-    op("V", lambda: v.tensor_reduce(T.pf[:, 15:16], T.vtmp[:], AxisListType.X, OP.add), ["vtmp"], ["pe"])
-    ts(T.cx[:], T.jb[:], 4.0 * UP, None, OP.mult, None, ["jb"], ["cx"])
-    ts(T.pf[:, 16:17], T.pf[:, 15:16], -1.0, None, OP.mult, None, ["pe"], ["pn"])
+    iota(T.io6[:], [[0, 4], [1024, 2]], 0, 0, ["io6"])
+    diagonals(["big"])
     E_, NE_ = T.pf[:, 15:16], T.pf[:, 16:17]
 
-    def make_u(between=None):
-        raw, big, small = T.Y0[:, 0:4, :], T.Y0[:, 8:12, :], T.Y0[:, 4, 0:8]
-        mm(raw, T.BW[:], T.Z[:], True, True, ["BW", "Z"], ["Y0"])
-        act(T.gu[:], raw, AF.Identity, ["Y0"], ["gu"], bias=192.0 - 0.5 + 2.0 ** -11, scale=2.0 ** -10)
-        if between:
-            between(0)
-        mm(big, T.rows[0:1, 1, :], T.ones[0:1, 0:128], True, False, ["rows", "ones"], ["Y0"])
-        mm(big, T.BW[:], T.Z[:], False, False, ["BW", "Z"], ["Y0"])
-        mm(big, T.ID[:, 10, :], T.gu[:], False, True, ["IDu", "gu"], ["Y0"])
-        if between:
-            between(1)
-        for e in (1, 0):
-            act(T.cm[:, 128 * e:128 * e + 128], big, AF.Identity, ["Y0"], ["cm"], bias=1.0, scale=2.0)
-        if between:
-            between(2)
+    def make_u(step):
+        raw, big, small = part("Y0", 0, 128), part("Y0", 256, 128), T.Y0[:, 4, 0:8]
+        if step == 0:
+            mm(raw, T.BW[:], T.Z[:], True, True, ["BW", "Z"], ["Y0"])
+            act(T.gu[:], raw, AF.Identity, ["Y0"], ["gu"], bias=192.0 - 0.5 + 2.0 ** -11, scale=2.0 ** -10)
+        if step == 1:
+            mm(big, T.urow[0:1, :], T.ones[0:1, 0:128], True, False, ["urow", "ones"], ["Y0"])
+            mm(big, T.BW[:], T.Z[:], False, False, ["BW", "Z"], ["Y0"])
+            mm(big, ident("-1024"), T.gu[:], False, True, ["ID.-1024", "gu"], ["Y0"])
+            act(T.cm[:], big, AF.Identity, ["Y0"], ["cm"], bias=33.0, scale=2.0)
+            act(T.Dm[:], big, AF.Identity, ["Y0", "kc"], ["Dm"], bias=T.kc[:, 0:1], scale=8192.0)
+            act(T.u32[:], big, AF.Identity, ["Y0"], ["u32"], scale=1.0 / 32)
+        if step == 2:
+            for r in range(16):
+                mm(small, T.WZ[:, 16 - r:144 - r], T.Z[:, r::16], r == 0, r == 15, ["WZ", "Z"], ["Y0"])
+
+    def columns(k):
+        if k == 0:
+            cp(T.si[:], T.Y0[:, 4, 0:8], ["Y0"], ["si"])
+        if k == 1:
+            ts(T.sj[:], T.si[:], 63, None, OP.bitwise_and, None, ["si"], ["sj"])
+        if k == 2:
+            tt(T.sk[:], T.sj[:], T.cx[:], OP.add, ["sj", "cx"], ["sk"])
+        if k == 3:
+            cp(T.offX[:], T.sk[:], ["sk"], ["offX"])
+        if k == 4:
+            tt(T.sl[:], T.sj[:], T.cs[:], OP.add, ["sj", "cs"], ["sl"])
+        if k == 5:
+            cp(T.offS[:], T.sl[:], ["sl"], ["offS"])
+
+    OWN, GOT, FIL = [("X2", 0), ("X1", 0)], [("OB", 256), ("TG", 0)], [("Y2", 0), ("Y2", 128)]
+
+    def turn_init(where, top, es=(1, 0)):
+        for e in es:
+            bk, c0 = where[e]
+            mm(part(bk, c0, 128), T.TP[:, top + e, :], T.ones[:, 0:128], True, False, ["TP", "TP.a%d" % (top + e), "TP.b%d" % (top + e), "ones"], [bk])
+
+    def turn(where, src, es=(1, 0)):
+        for e in es:
+            bk, c0 = where[e]
+            mm(part(bk, c0, 128), T[src][:, :, e::2], T.IU[:], False, True, [src, "IU"], [bk])
+
+    def hash_step(where, off, step, e):
+        bk, c0 = where[e]
+        c = slice(128 * e, 128 * e + 128)
+        if step == 0:
+            tt(part(bk, c0, 128), part(bk, c0, 128), T.cm[:], OP.mult, [bk, "cm"], [bk])
+        if step == 1:
+            tt(T.h1[:, c], part(bk, c0, 128), T.Dm[:], OP.add, [bk, "Dm"], ["h1.%d" % e])
+        if step == 2:
+            ts(T.h2[:, c], T.h1[:, c], 5, 8191, OP.arith_shift_right, OP.bitwise_and, ["h1.%d" % e], ["h2.%d" % e])
+        if step == 3:
+            cp(T[off][:, c], T.h2[:, c], ["h2.%d" % e], ["%s.%d" % (off, e)])
+
+    def fill_product(e):
+        tt(T.ft[:, 128 * e:128 * e + 128], part("Y2", 128 * e, 128), T.u32[:], OP.mult, ["Y2", "u32"], ["ft"])
+
+    def turn_own():
+        turn(OWN, "VA")
         for e in range(2):
-            act(T.u32[:, 128 * e:128 * e + 128], big, AF.Identity, ["Y0"], ["u32"], scale=1.0 / 32)
-            act(T.uk[:, 128 * e:128 * e + 128], big, AF.Identity, ["Y0", "pf8"], ["uk"], bias=T.pf[:, 8 + e:9 + e])
-        for r in range(16):
-            mm(small, T.WZ[:, 16 - r:144 - r], T.Z[:, r::16], r == 0, r == 15, ["WZ", "Z"], ["Y0"])
-        act(T.sf[:], small, AF.Copy, ["Y0"], ["sf"])
-
-    def columns():
-        cp(T.si[:], T.sf[:], ["sf"], ["si"])
-        ts(T.sj[:], T.si[:], 63, None, OP.bitwise_and, None, ["si"], ["sj"])
-        tt(T.sk[:], T.sj[:], T.cx[:], OP.add, ["sj", "cx"], ["sk"])
-        cp(T.offX[:], T.sk[:], ["sk"], ["offX"])
-
-    def turn_init(bk, name, h, top="0"):
-        o = bk[:, 8 * h:8 * h + 8, :]
-        mm(o, T["top" + top][0:1, :], T.ones[0:1, 0:256], True, False, ["top" + top, "ones"], [name])
-        mm(o, T.ones[0:1, 0:128], T["tb" + top][0:1, :], False, False, ["tb" + top, "ones"], [name])
-        if name == "Y2":
-            mm(o, T.ones[:, 0:128], T.rsb[:], False, False, ["rsb", "ones"], [name])
-
-    def half_init(bk, name, e):
-        o = bk[:, 4 * e:4 * e + 4, :]
-        mm(o, T.top0[0:1, :], T.ones[0:1, 0:128], True, False, ["top0", "ones"], [name])
-        if e == 1:
-            mm(o, T.ones[0:1, 0:128], T.tb0[0:1, 128:256], False, False, ["tb0", "ones"], [name])
-        if name == "Y2":
-            mm(o, T.ones[:, 0:128], T.rsb[:, 0:128], False, False, ["rsb", "ones"], [name])
-
-    def turn(h, src):
-        for bk, name in ((T.TG, "TG"), (T.Y2, "Y2")):
-            for e in range(2):
-                mm(bk[:, 8 * h + 4 * e:8 * h + 4 * e + 4, :], T[src][:, :, e::2], T.IU[:], False, e == 1, [src, "IU"], [name])
-
-    def hashing(h, off):
-        tt(T.pA[:], T.TG[:, 8 * h:8 * h + 8, :], T.cm[:], OP.mult, ["TG", "cm"], ["pA"])
-        ts(T.h1[:], T.pA[:], 5, None, OP.arith_shift_right, None, ["pA"], ["h1"])
-        tt(T.h2[:], T.Y2[:, 8 * h:8 * h + 8, :], T.h1[:], OP.add, ["Y2", "h1"], ["h2"])
-        ts(T.h1[:], T.h2[:], 8191, None, OP.bitwise_and, None, ["h2"], ["h1"])
-        cp(T[off][:], T.h1[:], ["h1"], [off])
-
-    def turn_hash_halves():
-        for e in (1, 0):
-            c = slice(128 * e, 128 * e + 128)
-            for bk, name in ((T.TG, "TG"), (T.Y2, "Y2")):
-                if e == 0:
-                    half_init(bk, name, 0)
-                mm(bk[:, 4 * e:4 * e + 4, :], T.VA[:, :, e::2], T.IU[:], False, True, ["VA", "IU"], [name])
-            tt(T.pA[:, c], T.TG[:, 4 * e:4 * e + 4, :], T.cm[:, c], OP.mult, ["TG", "cm"], ["pA"])
-            ts(T.h1[:, c], T.pA[:, c], 5, None, OP.arith_shift_right, None, ["pA"], ["h1"])
-            tt(T.h2[:, c], T.Y2[:, 4 * e:4 * e + 4, :], T.h1[:, c], OP.add, ["Y2", "h1"], ["h2"])
-            ts(T.h1[:, c], T.h2[:, c], 8191, None, OP.bitwise_and, None, ["h2"], ["h1"])
-            cp(T.offA[:, c], T.h1[:, c], ["h1"], ["offA%d" % e])
+            turn_init(FIL, 2, (e,))
+            turn(FIL, "VA", (e,))
+        make_u(2)
+        for step in range(4):
+            for e in (1, 0):
+                hash_step(OWN, "offA", step, e)
 
     def gather(eng, dst, off, e, i0, i1):
+        if i0 == i1:
+            return
         c0, c1 = 128 * e + i0, 128 * e + i1
         o, x = T[dst][:, 16 * c0:16 * c1], T.X[:, 0:8192].indirect(T[off][:, c0:c1])
         key = "%s.%d%s" % (dst, e, eng)
-        if off == "offA":
-            off = "offA%d" % e
         if eng == "V":
-            ts(o, x, E_, None, OP.add, None, XK + [off, "pe"], [key])
-        elif dst == "xg":
-            act(o, x, AF.Identity, XK + [off, "pe"], [key], bias=E_)
+            cp(o, x, XK + ["%s.%d" % (off, e)], [key])
         else:
-            act(o, x, AF.Copy, XK + [off], [key])
+            act(o, x, AF.Copy, XK + ["%s.%d" % (off, e)], [key])
 
     def allkeys(dst):
         return ["%s.%d%s" % (dst, e, q) for e in range(2) for q in "VA"]
 
-    def keys(dst, bk, name, e, j):
+    def key_init(j):
+        mm(XB[j][:], T.NE[:], T.WR[:, 16 * j:16 * j + 16, :], True, False, ["NE", "WR"], ["X%d" % j])
+
+    def keys(dst, name, e, j, stop=False):
         for r in range(16):
             k = 2 * r + e
-            mm(bk[j][:, :, k] if bk is YB else bk[j][:, k::32], T[dst][:, 2048 * e + r:2048 * e + 2048:16], T.WN[:, 16 * j:16 * j + 16],
-               e == 1 and r == 0, name == "X" and j == 0 and k == 30, ["%s.%dV" % (dst, e), "%s.%dA" % (dst, e), "WN"], ["%s%d" % (name, j)])
+            mm(YB[j][:, :, k] if name == "Y" else XB[j][:, k::32], T[dst][:, 2048 * e + r:2048 * e + 2048:16], T.WN[:, 16 * j:16 * j + 16],
+               name == "Y" and e == 1 and r == 0, stop and r == 15, ["%s.%dV" % (dst, e), "%s.%dA" % (dst, e)] + WK, ["%s%d" % (name, j)])
 
-    for b in range(2):
-        ts(T.BD[:, :, 16 * b:16 * b + 16], T.io3[:], G_, None, OP.is_equal, None, ["io3", "pf"], ["BD"])
+    def start_row(bk, name):
+        mm(part(bk, 0, 256), T.ones[0:1, 0:128], row(name), True, False, ["ones", "rows"], [bk])
+
+    def blocks(bk, c0, terms, stop, start=False):
+        for n_, (src, buf, names, name) in enumerate(terms):
+            for h in range(2):
+                mm(part(bk, c0 + 128 * h, 128), half(src, h), pick(buf, names, name), start and h == 0 and n_ == 0, stop and h == 1 and n_ == len(terms) - 1,
+                   [src, "%s.%s" % (buf, name)], [bk])
+
+    def sign_marks(bk, c0, marks):
+        for h in range(2):
+            mm(part(bk, c0 + 128 * h, 128), half(marks, h), ident("big"), h == 0, False, [marks, "ID.big"], [bk])
+
+    def sign_whole(bk, c0, flag):
+        for h in range(2):
+            mm(part(bk, c0 + 128 * h, 128), T.BD[:, 1, 4 * h:4 * h + 4, :], T[flag][:], False, False, ["BD.big", flag], [bk])
+
+    def sign_levels(bk, c0, src, j, stop):
+        for c in (2 * j, 2 * j + 1):
+            for h in range(2):
+                mm(part(bk, c0 + 128 * h, 128), T[src][:, 256 * c + 128 * h:256 * c + 128 * h + 128], ident("1"), False,
+                   stop and c % 2 == 1 and h == 1, ["%s.%d" % (src, j), "ID.1"], [bk])
+
+    WK = ["WN.%d" % l for l in range(6)]
+    turn_init(OWN, 0)
+    make_u(0)
+    make_u(1)
+    ts(T.vtmp[:], T.io4[:], 15.0, P_, OP.min, OP.is_equal, ["io4", "pf"], ["vtmp"])
+    ms(T.r0[:], 1.0, ["r0"])
+    op("V", lambda: v.tensor_reduce(T.pf[:, 15:16], T.vtmp[:], AxisListType.X, OP.add), ["vtmp"], ["pe"])
+    ms(T.r0[:, 31::32], 0.0, ["r0"], ["r0"])
+    ts(T.pf[:, 16:17], T.pf[:, 15:16], -1.0, None, OP.mult, None, ["pe"], ["pn"])
+    turn_own()
+    act(T.NE[:], T.ones[:, 0:128], AF.Identity, ["ones", "pn"], ["NE"], scale=NE_)
+    act(T.WR[:, :, 0:1], T.WN[:], AF.Identity, WK, ["WR"], scale=-1.0)
+    for s in range(5):
+        act(T.WR[:, :, 2 ** s:2 ** (s + 1)], T.WR[:, :, 0:2 ** s], AF.Copy, ["WR"], ["WR"])
+    fill0 = -131072.0 - 31.0 / 64
+    ts(T.pf[:, 8:9], P_, 74.0, fill0, OP.mult, OP.add, ["pf"], ["pf8"])
+    ts(T.pf[:, 9:10], P_, 74.0, fill0 + 37, OP.mult, OP.add, ["pf"], ["pf8"])
+    ts(T.pf[:, 11:12], P_, 16.0 * DOWN, None, OP.mult, None, ["pf"], ["pf10"])
+    ts(T.pf[:, 12:13], P_, 64.0, None, OP.mult, None, ["pf"], ["pf12"])
     ts(T.dp[:], T.io1[:], G_, None, OP.is_equal, None, ["io1", "pf"], ["dp"])
     ts(T.dn[:], T.io1[:], G_, -1.0, OP.is_equal, OP.mult, ["io1", "pf"], ["dn"])
+    ts(T.jb[:], T.io1[:], 256.0 * DOWN, T.pf[:, 11:12], OP.mult, OP.add, ["io1", "pf10"], ["jb"])
+    ts(T.cx[:], T.io1[:], 1024.0, T.pf[:, 12:13], OP.mult, OP.add, ["io1", "pf12"], ["cx"])
+    for b in range(2):
+        ts(T.BD[:, 0, :, 16 * b:16 * b + 16], T.io3[:], G_, -1.0 / 16, OP.is_equal, OP.mult, ["io3", "pf"], ["BD.-1/16"])
+    ts(T.B16[:], T.io3[:], G_, None, OP.is_equal, None, ["io3", "pf"], ["B16"])
+    for h in range(2):
+        ts(T.OT[:, h, :], T.io3[:], float(-4 * h), Q_, OP.add, OP.is_equal, ["io3", "pf"], ["OT"])
+    ms(T.HB[:], 0.0, ["HB"])
     ms(T.HS[:, 128:136], 0.0, ["HS"])
-    ms(T.w[:, 255:256], 0.0, ["w"])
-    ms(T.OB[:, 255:256], 0.0, ["OB.w"])
-
-    def first_turn(k):
-        if k == 0:
-            half_init(T.TG, "TG", 1)
-            half_init(T.Y2, "Y2", 1)
-        if k == 2:
-            turn_hash_halves()
-    make_u(first_turn)
-    WK = ["W48.%d" % l for l in range(6)]
-    act(T.ID[:, 1, :], T.ID[:, 0, :], AF.Identity, ["ID0"], ["ID"], scale=BIG2)
-    act(T.ID[:, 2, :], T.ID[:, 0, :], AF.Identity, ["ID0"], ["ID"], scale=-BIG1)
-    act(T.WN[:], T.W48[:], AF.Identity, WK, ["WN"], scale=-1.0)
+    ms(T.CT[:], 0.0, ["CT"])
+    ts(T.dia[:], ident("1"), K_, None, OP.mult, None, ["ID.1", "pf"], ["dia"])
+    ms(T.CT[0:1, :], 280.0, ["CT"], ["CT"])
+    ms(T.CT[32:33, :], 66.0 / 128, ["CT"])
+    ts(T.CT[64:65, :], T.br[64:65, :, :], -1.0 / 128, None, OP.mult, None, ["br"], ["CT"])
+    ts(T.topf[0:1, :], T.br[0:1, :, :], 2.0 ** -7, 1.5, OP.mult, OP.add, ["br"], ["topf"])
+    ts(pick("OM", OS, "1"), T.io5[:], Q_, None, OP.is_equal, None, ["io5", "pf"], ["OM.1"])
+    ts(pick("OM", OS, "1/2"), T.io5[:], Q_, 0.5, OP.is_equal, OP.mult, ["io5", "pf"], ["OM.1/2"])
+    ts(T.hold[:], T.io2[:], P_, None, OP.is_le, None, ["io2", "pf"], ["hold"])
+    ts(T.cs[:], T.io6[:], T.pf[:, 12:13], None, OP.add, None, ["io6", "pf12"], ["cs"])
+    ms(T.hold[:, 0::16], 0.0, ["hold"], ["hold"])
+    op("G", lambda: g.affine_select(T.tri[:], pick("OM", OS, "1"), [[1, 128]], OP.is_ge, 0.0, 0, -1), ["OM.1"], ["tri"])
     iota(T.inc[:], [[0, 128], [-4095, 2]], 2048, 0, ["inc"])
-    iota(T.HB[:], [[0, 136]], 0, 0, ["HB"])
-    iota(T.nd[:], [[0, 256]], -1, 0, ["nd"])
+    diagonals(["-64", "1/2", "-2/128", "g1", "g2", "g3", "g4", "g5", "-1", "-1/128"])
+    for k, (n_, c) in enumerate(ROWS.items()):
+        iota(T.rows[:, k, :], [[0, 8], [1 if n_ == "own" else -1, 32]], c, 0, ["rows"])
+    iota(T.onesf[:], [[0, 128]], 32, 0, ["onesf"])
 
     def late_constants():
-        act(T.WR[:, :, 0:1], T.W48[:], AF.Copy, WK, ["WR"])
-        ts(T.hold[:], T.io2[:], P_, None, OP.is_le, None, ["io2", "pf"], ["hold"])
-        act(T.r0[:], T.kio[:], AF.Sign, ["kio"], ["r0"], bias=31.0, scale=-1.0)
-        for s in range(5):
-            act(T.WR[:, :, 2 ** s:2 ** (s + 1)], T.WR[:, :, 0:2 ** s], AF.Copy, ["WR"], ["WR"])
-        ms(T.tb1[0:1, 0:128], 0.0, ["tb1"])
-        ms(T.tb1[0:1, 128:256], -4.0 * 8192, ["tb1"])
-        ts(T.hold[:, 0::16], T.hold[:, 0::16], 0.0, None, OP.mult, None, ["hold"], ["hold"])
+        scaled("BD", BDS, ["big"])
+        act(T.OT[:], T.OT[:], AF.Identity, ["OT"], ["OT"], scale=-1.0)
+        scaled("LM", LS, ["-1"])
+        tops([4, 5])
 
     def sums(j):
-        name = ("X0", "X1", "X2", "Y0")[j]
         for q in range(4):
-            mm(T[name][:], T.ID[:, 0, :], T.X[:, 2048 * q + 512 * j:2048 * q + 512 * j + 512], q == 0, q == 3, ["ID0"] + XK, [name])
+            mm(T.X0[:], ident("1"), T.X[:, 2048 * q + 512 * j:2048 * q + 512 * j + 512], q == 0, q == 3, ["ID.1"] + XK, ["X0"])
+        act(T.S[:, 512 * j:512 * j + 512], T.X0[:], AF.Copy, ["X0"], ["S.%d" % (j // 2)])
 
-    def store_sums(j):
-        name = ("X0", "X1", "X2", "Y0")[j]
-        act(T.S[:, 512 * j:512 * j + 512], T[name][:], AF.Copy, [name], ["S.%d" % j])
-        dma("S", T.yx[:, 512 * j:512 * j + 512], T.S[:, 512 * j:512 * j + 512], ["S.%d" % j], [])
+    def patch(t, k):
+        if t == 0:
+            return
+        q, n = k // 2, t
+        win = T.S[:, 0:1024 * n].indirect(T.offS[:, 2 * q:2 * q + n])
+        c = slice(32 * q, 32 * q + 16 * n)
+        SK = ["S.%d" % j for j in range(n)]
+        if k % 2 == 0:
+            tt(T.xp[:, c], win, T.xd[:, c], OP.subtract, SK + ["offS", "xd"], ["xp"])
+        else:
+            cp(win, T.xp[:, c], ["xp", "offS"], SK)
 
-    def join_constants():
-        act(T.nc[:], T.kio[:], AF.Sign, ["kio"], ["nc"])
-        act(T.NK[:, 0::2], T.zero[:], AF.Copy, ["zero"], ["NK"])
-        act(T.NK[:, 1::2], T.kio[:], AF.Identity, ["kio"], ["NK"], scale=-1.0)
-        act(T.topf[:], T.br[:], AF.Identity, ["br"], ["topf"], scale=2.0 ** -7, bias=1.5)
-        for h in range(2):
-            act(T.tagc[:, 256 * h:256 * h + 256], T.br[:], AF.Identity, ["br"], ["tagc"], scale=-(2.0 ** -7))
+    off = [192.0 - 0.5 + 2.0 ** -(s + 1) for s in range(6)]
 
-    def tag_constants():
-        for n_, c_ in ((12, -1.0), (3, 2.0), (4, 64.0), (5, -96.0), (6, -48.0), (7, -24.0), (8, -12.0), (9, -7.0)):
-            act(T.ID[:, n_, :], T.ID[:, 0, :], AF.Identity, ["ID0"], ["IDt"], scale=c_ / 128)
-        act(T.top1[:], T.br[:, :, 0:16], AF.Identity, ["br"], ["top1"], scale=-8192.0)
+    def quot(eng, s, h, src, key):
+        o = T["G%d" % s][:, 256 * h:256 * h + 256]
+        if eng == "V":
+            ts(o, src, 2.0 ** -s, off[s], OP.mult, OP.add, [key], ["G%d.%d" % (s, h)])
+        else:
+            act(o, src, AF.Identity, [key], ["G%d.%d" % (s, h)], bias=off[s], scale=2.0 ** -s)
+
+    def quot_add(bk, s, h, stop=False):
+        mm(part(bk, 0, 256), ident("g%d" % s), T["G%d" % s][:, 256 * h:256 * h + 256], False, stop, ["ID.g%d" % s, "G%d.%d" % (s, h)], [bk])
 
     for t in range(RO):
         last = t == RO - 1
         VB, LB, JB = "VB%d" % t, "LB%d" % t, "JB%d" % t
         s1, s0 = SPLIT[min(t, 1)]
+        gather("A", "xg", "offA", 1, s1, 128)
+        gather("A", "xg", "offA", 0, s0, 128)
+        turn_init(GOT, 0)
         if t > 0:
-            gather("A", "xg", "offA", 1, s1, 128)
-            gather("A", "xg", "offA", 0, s0, 128)
-        turn_init(T.TG, "TG", 1)
-        turn_init(T.Y2, "Y2", 1)
-        turn(1, VB)
+            for j in range(3):
+                key_init(j)
+        turn(GOT, VB)
+        spare = [lambda k=k: columns(k) for k in range(1, 6 if t > 0 else 4)]
         if t > 0:
             gather("V", "xg", "offA", 1, 0, s1)
             gather("V", "xg", "offA", 0, 0, s0)
+            for step, other in enumerate((lambda: fill_product(0), lambda: fill_product(1), lambda: columns(0), None)):
+                hash_step(GOT, "offB", step, 1)
+                if other:
+                    other()
+            spare = [lambda k=k: hash_step(GOT, "offB", k, 0) for k in range(4)] + spare
         else:
-            late_constants()
-        hashing(1, "offB")
-        if t == 0:
-            gather("A", "xg", "offA", 1, s1, 128)
-            gather("A", "xg", "offA", 0, s0, 128)
+            for step in range(4):
+                for e in (1, 0):
+                    hash_step(GOT, "offB", step, e)
+            for j in range(3):
+                key_init(j)
+            fill_product(0)
+            fill_product(1)
+            columns(0)
             gather("V", "xg", "offA", 1, 0, s1)
             gather("V", "xg", "offA", 0, 0, s0)
-        tt(T.TG[:, 0:8, :], T.TG[:, 0:8, :], T.u32[:], OP.mult, ["TG", "u32"], ["TG"])
-        tt(T.fa[:], T.TG[:, 0:8, :], T.uk[:], OP.add, ["TG", "uk"], ["fa"])
-        cp(T.fbf[:], T.fa[:], ["fa"], ["fbf"])
+            spare.append(lambda: tt(pick("LM", LS, "1"), T.dia[:], T.tri[:], OP.add, ["dia", "tri"], ["LM.1"]))
         gather("A", "yg", "offB", 1, 0, 128)
-        gather("A", "yg", "offB", 0, 0, 128)
-        if t == 0:
-            join_constants()
         for j in range(3):
-            keys("xg", XB, "X", 1, j)
-        keys("xg", XB, "X", 0, 0)
-        keys("xg", XB, "X", 0, 1)
+            keys("xg", "X", 1, j)
+        keys("xg", "X", 0, 0, True)
+        keys("xg", "X", 0, 1)
         r = "r0"
         for l in range(6):
             if l < 3:
-                src, c0, kx, w, kw = XB[l], 0, "X%d" % l, T.w, "w"
+                kx, kw = "X%d" % l, "w"
+                nv, w = lev(l), T.w[:]
+                scan(T.w[:, 254::-1], XB[l][:, 255:0:-1], T[r][:, 254::-1], OP.min, OP.mult, [kx, r], [kw])
             else:
-                src, c0, kx, w, kw = T.NV, 512 * (l - 3) + 256, "NV.%d" % l, T.OB, "OB.w"
-            nv = src[:, c0:c0 + 256]
-            scan(w[:, 254::-1], src[:, c0 + 255:(c0 if c0 else 0):-1], T[r][:, 254::-1], OP.min, OP.mult, [kx, r], [kw])
+                c0, kx, kw = 512 * (l - 3) + 256, "NV.%d" % l, "OB"
+                nv, w = T.NV[:, c0:c0 + 256], T.OB[:, 0:256]
+                scan(T.OB[:, 254::-1], T.NV[:, c0 + 255:c0:-1], T[r][:, 254::-1], OP.min, OP.mult, [kx, r], [kw])
+            if spare:
+                spare.pop(0)()
+            if l == 2:
+                gather("A", "yg", "offB", 0, 0, 128)
             if l < 5:
-                tt(T.lt[:], nv, w[:, 0:256], OP.is_gt, [kx, kw], ["lt"])
+                tt(T.lt[:], nv, w, OP.is_gt, [kx, kw], ["lt"])
                 if l < 2:
-                    mm(lev(XB, l + 1), T.ID[:, 1, :], T.lt[:], False, True, ["ID", "lt"], ["X%d" % (l + 1)])
+                    mm(lev(l + 1), ident("big"), T.lt[:], False, True, ["ID.big", "lt"], ["X%d" % (l + 1)])
                 if l == 0:
-                    keys("xg", XB, "X", 0, 2)
+                    keys("xg", "X", 0, 2)
                 if l == 2:
                     for j in range(3):
-                        keys("yg", YB, "Y", 1, j)
+                        keys("yg", "Y", 1, j)
                 r = "rA" if l % 2 == 0 else "rB"
-                tt(T[r][:], nv, w[:, 0:256], OP.is_ge, [kx, kw], [r])
+                tt(T[r][:], nv, w, OP.is_ge, [kx, kw], [r])
                 if l >= 2:
-                    tt(T.NV[:, 512 * (l - 2) + 256:512 * (l - 2) + 512], lev(XB, l + 1), T.lt[:], OP.add, ["X%d" % (l - 2), "lt"], ["NV.%d" % (l + 1)])
+                    tt(T.NV[:, 512 * (l - 2) + 256:512 * (l - 2) + 512], lev(l + 1), T.lt[:], OP.add, ["X%d" % (l - 2), "lt"], ["NV.%d" % (l + 1)])
+                if spare:
+                    spare.pop(0)()
+                if l == 4:
+                    mm(T.TG[:, 8, 0:8], T.IU[:], T.jb[:], True, False, ["IU", "jb"], ["TG"])
+                    for j in (2, 1, 0):
+                        keys("yg", "Y", 0, j)
+                if l == 3:
+                    key_init(0)
+                    keys("xg", "X", 1, 0)
+                    keys("xg", "X", 0, 0)
             else:
-                tt(T.LT[:], nv, w[:, 0:256], OP.is_gt, [kx, kw], ["LT"])
-        for l in range(3):
-            act(T.NV[:, 512 * l:512 * l + 256], lev(XB, l), AF.Copy, ["X%d" % l], ["NV.%d" % l])
-        mm(T.TG[:, 8, 0:8], T.IU[:], T.jb[:], True, False, ["IU", "jb"], ["TG"])
+                tt(T.LT[:], nv, w, OP.is_gt, [kx, kw], ["LT"])
+        if t == 0:
+            late_constants()
+        for l in (1, 2):
+            act(T.NV[:, 512 * l:512 * l + 256], lev(l), AF.Copy, ["X%d" % l], ["NV.%d" % l])
+        for e in range(2):
+            act(T.f1[:, 128 * e:128 * e + 128], T.ft[:, 128 * e:128 * e + 128], AF.Identity, ["ft", "pf8"], ["f1"], bias=T.pf[:, 8 + e:9 + e])
+        act(T.ft[:], T.f1[:], AF.Identity, ["f1"], ["ft"], bias=MAGIC)
         send(2, t, "LT", LB)
-        keys("yg", YB, "Y", 0, 2)
-        keys("yg", YB, "Y", 0, 1)
         scan(T.KF[:, ::-1], T.inc[:, ::-1], T.LT[:, ::-1], OP.add, OP.mult, ["inc", "LT"], ["KF"])
+        for h in range(2):
+            mm(part("OB", 256 + 128 * h, 128), half("LT", h), ident("1"), h == 0, h == 1, ["LT", "ID.1"], ["OB"])
+        act(T.LTt[:], part("OB", 256, 256), AF.Identity, ["OB"], ["LTt", "rs"], acc=T.rs[:, 0:1])
+        act(T.fbf[:], T.ft[:], AF.Identity, ["ft"], ["fbf"], bias=-MAGIC)
+        act(T.gf[:], T.fbf[:], AF.Identity, ["fbf"], ["gf"], bias=192.0 - 0.5 + 2.0 ** -14, scale=2.0 ** -13)
         cp(T.HB[:, 0:128:16], T.KF[:, 0::32], ["KF"], ["HB"])
         scan(T.HS[:, 0:128], T.hold[:], T.HB[:, 0:128], OP.mult, OP.add, ["hold", "HB"], ["HS"])
         mm(T.TG[:, 8, 0:8], T.HB[:, 1:129], T.dp[:], False, False, ["HB", "dp"], ["TG"])
@@ -485,97 +601,113 @@ def rank_program(g, core, T, topo):
         mm(T.TG[:, 8, 0:8], T.HS[:, 1:129], T.dn[:], False, True, ["HS", "dn"], ["TG"])
         cp(T.J[:], T.TG[:, 8, 0:8], ["TG"], ["J"])
         send(1, t, "J", JB)
-        keys("yg", YB, "Y", 0, 0)
-        ts(T.M[:], T.xg[:, 0:4096].indirect(T.J[:, 0:8]), NE_, None, OP.add, None, allkeys("xg") + ["J", "pn"], ["M"])
-        tt(T.ge[:], T.Z[:], T.M[:], OP.is_ge, ["Z", "M"], ["ge"])
+        cp(T.M[:], T.xg[:, 0:4096].indirect(T.J[:, 0:8]), allkeys("xg") + ["J"], ["M"])
+        tt(T.ge[:], T.xg[:, 0:4096].indirect(T.J[:, 0:8]), T.Z[:], OP.is_le, allkeys("xg") + ["J", "Z"], ["ge"])
+        tt(T.h1[:, 0:128], T.X[:, 0:8192].indirect(T.offX[:, 0:8]), T.M[:], OP.add, XK + ["offX", "M"], ["h1.0"])
         for j in (2, 1, 0):
             mm(YB[j][:], T.M[:], T.WR[:, 16 * j:16 * j + 16, :], False, True, ["M", "WR"], ["Y%d" % j])
             if j == 2:
-                mm(T.TG[:, 0:8, :], T.ge[:], T.BD[:], True, True, ["ge", "BD"], ["TG"])
-        act(T.cY[:, 0:512], T.Y2[:], AF.Copy, ["Y2"], ["cY.2"])
-        act(T.bonB[:], T.TG[:, 0:8, :], AF.Relu, ["TG"], ["bonB"], bias=-6.0, scale=1.0)
-        act(T.cY[:, 1024:1536], T.Y0[:], AF.Copy, ["Y0"], ["cY.0"])
-        act(T.bonA[:], T.TG[:, 0:8, :], AF.Relu, ["TG"], ["bonA"], bias=7.0, scale=-1.0)
-        columns()
-        tt(T.xs[:], T.X[:, 0:8192].indirect(T.offX[:, 0:8]), T.M[:], OP.add, XK + ["offX", "M"], ["xs"])
-        ts(T.xh[:], T.xs[:], 1, None, OP.arith_shift_right, None, ["xs"], ["xh"])
+                mm(part("TG", 0, 128), T.B16[:], T.ge[:], True, True, ["ge", "B16"], ["TG"])
+        act(T.cY[:, 1024:1536], T.Y2[:], AF.Copy, ["Y2"], ["cY.2"])
+        ts(T.h2[:, 0:128], T.h1[:, 0:128], 1, None, OP.arith_shift_right, None, ["h1.0"], ["h2.0"])
+        if t > 0:
+            tt(T.xd[:], T.X[:, 0:8192].indirect(T.offX[:, 0:8]), T.h2[:, 0:128], OP.subtract, XK + ["offX", "h2.0"], ["xd"])
+        patch(t, 0)
         cp(T.cY[:, 512:1024], T.Y1[:], ["Y1"], ["cY.1"])
-        act(T.nf[:], T.bonA[:, 0::32], AF.Sign, ["bonA"], ["nf"])
-        act(T.fr[:], T.bonB[:, 0::32], AF.Sign, ["bonB"], ["fr"])
-        act(T.gf[:], T.fbf[:], AF.Identity, ["fbf"], ["gf"], bias=192.0 - 0.5 + 2.0 ** -14, scale=2.0 ** -13)
-        sumA, sumB = T.TG[:, 8:16, :], T.OB[:, 256:512]
-        mm(sumB, T.ID[:, 1, :], T[LB][:], True, False, ["ID", LB], ["OB.s"])
-        for c in (0, 1, -1, 4, 5, 2, 3):
-            if c < 0:
-                mm(sumB, T.ID[:, 2, :], T.bonB[:], False, False, ["ID", "bonB"], ["OB.s"])
-            else:
-                mm(sumB, T.ID[:, 0, :], T.cY[:, 256 * c:256 * c + 256], False, c == 3, ["ID0", "cY.%d" % (2 - c // 2)], ["OB.s"])
-        mm(sumA, T.ID[:, 1, :], T.LT[:], True, False, ["ID", "LT"], ["TG"])
-        mm(sumA, T.ID[:, 2, :], T.bonA[:], False, False, ["ID", "bonA"], ["TG"])
-        cp(T.X[:, 0:8192].indirect(T.offX[:, 0:8]), T.xh[:], ["xh", "offX"], XK)
+        act(T.fr[:], part("TG", 0, 128), AF.Relu, ["TG"], ["fr"], bias=-6.0)
+        act(T.cY[:, 0:512], T.Y0[:], AF.Copy, ["Y0"], ["cY.0"])
+        act(T.nf[:], part("TG", 0, 128), AF.Relu, ["TG"], ["nf"], bias=7.0, scale=-1.0)
+        sign_marks("OB", 256, LB)
+        sign_levels("OB", 256, "cY", 2, False)
+        sign_whole("OB", 256, "fr")
+        sign_levels("OB", 256, "cY", 1, False)
+        blocks("Y1", 0, [("LTt", "LM", LS, "-1")], False, True)
+        mm(part("Y2", 256, 128), ident("-64"), T.fr[:], True, False, ["ID.-64", "fr"], ["Y2"])
+        for h in range(2):
+            mm(part("Y2", 256, 128), T.OT[:, h, :], half("LTt", h), False, h == 1, ["OT", "LTt"], ["Y2"])
+        patch(t, 1)
         ts(T.y0[:], T.yg[:, 0:4096].indirect(T[JB][:, 0:8]), E_, None, OP.add, None, allkeys("yg") + [JB, "pe"], ["y0"])
-        for j in range(3):
-            mm(XB[j][:], T.y0[:], T.WR[:, 16 * j:16 * j + 16, :], True, True, ["y0", "WR"], ["X%d" % j])
-        mm(T.Y2[:, 0:8, :], T.ones[0:1, 0:128], T.topf[0:1, :], True, False, ["ones", "topf"], ["Y2"])
-        ts(T.KB[:], sumB, 0.0, None, OP.is_le, None, ["OB.s"], ["KB"])
-        for j in range(3):
+        sign_levels("OB", 256, "cY", 0, True)
+        for j in (1, 2, 0):
+            mm(XB[j][:], T.y0[:], T.WR[:, 16 * j:16 * j + 16, :], j > 0, True, ["y0", "WR"], ["X%d" % j])
+        patch(t, 2)
+        patch(t, 3)
+        ts(T.KB[:], part("OB", 256, 256), 0.0, None, OP.is_le, None, ["OB"], ["KB"])
+        act(T.mm[:], part("Y2", 256, 128), AF.Relu, ["Y2"], ["mm"], bias=32.0)
+        act(T.s2[:], part("OB", 256, 256), AF.Sign, ["OB"], ["s2"], bias=BIG1 / 2)
+        act(T.cA[:, 0:512], T.X0[:], AF.Copy, ["X0"], ["cA.0"])
+        sign_marks("Y0", 0, "LT")
+        blocks("Y1", 0, [("KB", "OM", OS, "1"), ("s2", "OM", OS, "1/2")], True)
+        sign_whole("Y0", 0, "nf")
+        for j in (1, 2):
             tt(T.cA[:, 512 * j:512 * j + 512], XB[j][:], T.NV[:, 512 * j:512 * j + 512], OP.add, ["X%d" % j, "NV.%d" % j, "NV.%d" % (j + 3)], ["cA.%d" % j])
-            for c in (2 * j, 2 * j + 1):
-                mm(sumA, T.ID[:, 0, :], T.cA[:, 256 * c:256 * c + 256], False, c == 5, ["ID0", "cA.%d" % j], ["TG"])
-            if j < 2:
-                mm(T.Y2[:, 0:8, j::2], T.fbf[:, 128 * j:128 * j + 128], T.IDN[:], False, False, ["fbf", "IDN"], ["Y2"])
-        if last:
-            sums(0)
-            store_sums(0)
-        ts(T.IL[:, 512::2], T.KB[:], -1.0, 1.0, OP.mult, OP.add, ["KB"], ["nkB"])
-        tt(T.zd[:], T.yg[:, 0:4096].indirect(T[JB][:, 0:8]), T.Z[:], OP.subtract, allkeys("yg") + [JB, "Z"], ["zd"])
+            patch(t, 3 + j)
+        sign_levels("Y0", 0, "cA", 1, False)
+        sign_levels("Y0", 0, "cA", 0, False)
+        sign_levels("Y0", 0, "cA", 2, True)
+        mm(part("X1", 0, 256), T.mm[:], T.BD[:, 0, :, :], True, False, ["mm", "BD.-1/16"], ["X1"])
+        blocks("X1", 0, [("KB", "LM", LS, "1")], False)
+        tt(T.DA[:], part("Y1", 0, 256), T.rows[:, 0, :], OP.add, ["Y1", "rows"], ["DA"])
+        for s in (5, 4):
+            quot("A", s, 0, T.DA[:], "DA")
         if not last:
-            act(T.Z[:], T.zd[:], AF.Abs, ["zd"], ["Z"])
-            act(T.G5[:, 0:256], T.LT[:], AF.Identity, ["LT"], ["G5", "rs"], acc=T.rs[:, 0:1])
-            act(T.rsb[:], T.zero[:], AF.Identity, ["zero", "rs"], ["rsb"], bias=T.rs[:, 0:1])
-        else:
-            act(T.zd[:], T.zd[:], AF.Abs, ["zd"], ["zd"])
-            dma("S", T.yz[:], T.zd[:], ["zd"], [])
-        scan(T.cB[:], T.nc[:], T.KB[:], OP.mult, OP.add, ["nc", "KB"], ["cB"])
-        tt(T.hA[:], T.cB[:, 31::32], T.nf[:], OP.mult, ["cB", "nf"], ["hA"])
-        ts(T.KA[:], sumA, 0.0, None, OP.is_le, None, ["TG"], ["KA"])
-        mm(T.TG[:], T.rows[0:1, 0, :], T.ones[0:1, :], True, False, ["rows", "ones"], ["TG"])
-        mm(T.TG[:], T.ones[0:1, 0:128], T.tagc[0:1, :], False, False, ["tagc", "ones"], ["TG"])
-        ts(T.IL[:, 0:512:2], T.KA[:], -1.0, 1.0, OP.mult, OP.add, ["KA"], ["nkA"])
-        tt(T.KA[:, 0::32], T.KA[:, 0::32], T.hA[:], OP.add, ["KA", "hA", "nkA"], ["KA"])
-        if t == 0:
-            tag_constants()
-        mm(T.TG[:], T.ID[:, 3, :], T.IL[:, 0::2], False, False, ["IDt", "nkA", "nkB"], ["TG"])
-        for e in range(2):
-            mm(T.Y2[:, 0:8, e::2], T.gf[:, 128 * e:128 * e + 128], T.ID[:, 12, :], False, e == 1, ["gf", "IDt"], ["Y2"])
-        scan(T.IL[:, 1:512:2], T.nc[:], T.KA[:], OP.mult, OP.add, ["nc", "KA"], ["ccA"])
-        tt(T.hB[:], T.IL[:, 63:512:64], T.fr[:], OP.mult, ["ccA", "fr"], ["hB"])
-        scan(T.DD[:, 0:512], T.NK[:], T.IL[:, 0:512], OP.mult, OP.add, ["NK", "nkA", "ccA"], ["dd.a"])
-        off = [192.0 - 2.0 ** -s - 0.5 + 2.0 ** -(s + 1) for s in range(6)]
-        for s in (5, 4):
-            act(T["G%d" % s][:, 0:256], T.DD[:, 1:512:2], AF.Identity, ["dd.a"], ["G%d" % s], bias=off[s], scale=2.0 ** -s)
-        tt(T.KB[:, 0::32], T.KB[:, 0::32], T.hB[:], OP.add, ["KB", "hB"], ["KB"])
-        scan(T.IL[:, 513::2], T.nc[:], T.KB[:], OP.mult, OP.add, ["nc", "KB"], ["ccB"])
-        scan(T.DD[:, 512:1024], T.NK[:], T.IL[:, 512:1024], OP.mult, OP.add, ["NK", "nkB", "ccB", "dd.a"], ["dd"])
-        mm(T.TG[:], T.ID[:, 4, :], T.DD[:, 1::2], False, False, ["IDt", "dd"], ["TG"])
-        for s in (5, 4):
-            act(T["G%d" % s][:, 256:512], T.DD[:, 513::2], AF.Identity, ["dd"], ["G%d" % s], bias=off[s], scale=2.0 ** -s)
-        for s in (1, 2, 3):
-            ts(T["G%d" % s][:], T.DD[:, 1::2], 2.0 ** -s, off[s], OP.mult, OP.add, ["dd"], ["G%d" % s])
-        for s in (1, 5, 2, 4, 3):
-            mm(T.TG[:], T.ID[:, 4 + s, :], T["G%d" % s][:], False, s == 3, ["IDt", "G%d" % s], ["TG"])
+            cp(T.X[:, 0:8192].indirect(T.offX[:, 0:8]), T.h2[:, 0:128], ["h2.0", "offX"], XK)
+        patch(t, 6)
+        patch(t, 7)
         if last:
-            for j in (1, 2, 3):
-                sums(j)
-                store_sums(j)
+            dma("S", T.yx[:], T.S[:], ["S.0", "S.1"], [])
+        ts(T.KA[:], part("Y0", 0, 256), 0.0, None, OP.is_le, None, ["Y0"], ["KA"])
+        mm(part("TG", 0, 256), T.ones[:, 0:128], T.CT[:], True, False, ["ones", "CT"], ["TG"])
+        blocks("X1", 0, [("KA", "OM", OS, "1")], True)
+        quot("V", 1, 0, T.DA[:], "DA")
+        tt(T.DB[:], part("X1", 0, 256), T.rows[:, 1, :], OP.add, ["X1", "rows"], ["DB"])
+        for s in (2, 3):
+            quot("V", s, 0, T.DA[:], "DA")
+        for s in (5, 4):
+            quot("A", s, 1, T.DB[:], "DB")
+        mm(part("TG", 0, 256), ident("1/2"), T.DA[:], False, False, ["ID.1/2", "DA"], ["TG"])
+        blocks("TG", 0, [("KA", "ID", IDS, "-2/128")], False)
+        for s in (5, 1, 4):
+            quot_add("TG", s, 0)
+        mm(part("Y2", 0, 256), T.ones[:, 0:128], T.CT[:], True, False, ["ones", "CT"], ["Y2"])
+        for s in (2, 3):
+            quot_add("TG", s, 0, s == 3)
+        for s in (1, 2, 3):
+            quot("V", s, 1, T.DB[:], "DB")
+        blocks("Y2", 0, [("KB", "ID", IDS, "-2/128")], False)
+        mm(part("Y2", 0, 256), ident("1/2"), T.DB[:], False, False, ["ID.1/2", "DB"], ["Y2"])
+        for s in (1, 5, 2, 3, 4):
+            quot_add("Y2", s, 1, s == 4)
+        start_row("X2", "len")
+        blocks("X2", 0, [("KB", "OM", OS, "1"), ("KA", "OM", OS, "1")], True)
+        mm(part("Y0", 256, 128), ident("1"), T.y0[:], True, False, ["ID.1", "y0"], ["Y0"])
+        mm(part("Y0", 256, 128), ident("-1"), T.Z[:], False, True, ["ID.-1", "Z"], ["Y0"])
+        if not last:
+            act(T.Z[:], part("Y0", 256, 128), AF.Abs, ["Y0", "pn"], ["Z"], bias=NE_)
+        act(T.nr[:], part("X2", 0, 256), AF.Relu, ["X2"], ["nr"])
+        if not last:
+            mm(T.Y0[:, 12, 0:1], T.onesf[:], T.rs[:, 0:1], True, True, ["onesf", "rs"], ["Y0"])
+            act(T.kc[:, 0:1], T.Y0[:, 12, 0:1], AF.Identity, ["Y0"], ["kc"], bias=4096.0 * 33 - 2.0 ** 23)
         else:
-            make_u()
-        tt(T.nd[:, 0::32], T.IL[:, 63:512:64], T.IL[:, 575::64], OP.max, ["ccA", "ccB"], ["nd"])
-        scan(T.nr[:], T.nc[:], T.nd[:], OP.mult, OP.add, ["nc", "nd"], ["nr"])
-        tt(T.Y2[:, 8:16, :], T.Y2[:, 0:8, :], T.nr[:], OP.max, ["Y2", "nr"], ["Y2.f"])
-        for h, src in ((0, "VA"), (1, VB)):
-            tt(T.E0[:, 8 * h:8 * h + 8, :], T.TG[:, 8 * h:8 * h + 8, 0::2], T[src][:, :, 0::2], OP.add, ["TG", src], ["E0"])
-            tt(T.Y1[:, 8 * h:8 * h + 8, 0:16], T.TG[:, 8 * h:8 * h + 8, 1::2], T[src][:, :, 1::2], OP.add, ["TG", src], ["Y1"])
+            act(T.zd[:], part("Y0", 256, 128), AF.Abs, ["Y0", "pn"], ["zd"], bias=NE_)
+            dma("S", T.yz[:], T.zd[:], ["zd"], [])
+        for h, src, bk in ((0, "VA", "TG"), (1, VB, "Y2")):
+            tt(T.E0[:, 8 * h:8 * h + 8, :], T[bk][:, 0:8, 0::2], T[src][:, :, 0::2], OP.add, [bk, src], ["E0"])
+            tt(T.Y1[:, 8 * h:8 * h + 8, 0:16], T[bk][:, 0:8, 1::2], T[src][:, :, 1::2], OP.add, [bk, src], ["Y1"])
+        fill = T.Y2[:, 8:16, :]
+        mm(fill, T.ones[0:1, 0:128], T.topf[0:1, :], True, False, ["ones", "topf"], ["Y2"])
+        for e in range(2):
+            mm(T.Y2[:, 8:16, e::2], T.fbf[:, 128 * e:128 * e + 128], T.IDN[:], False, False, ["fbf", "IDN"], ["Y2"])
+        if not last:
+            make_u(0)
+            sums(2 * t)
+            make_u(1)
+        for e in range(2):
+            mm(T.Y2[:, 8:16, e::2], T.gf[:, 128 * e:128 * e + 128], ident("-1/128"), False, False, ["gf", "ID.-1/128"], ["Y2"])
+        mm(fill, ident("1"), T.nr[:], False, True, ["ID.1", "nr"], ["Y2"])
+        if not last:
+            turn_init(OWN, 0)
+            sums(2 * t + 1)
         for s in range(4):
             ei, eo = ("E0", "E1") if s % 2 == 0 else ("E1", "E0")
             ki, ko = ("Y1", "TG") if s % 2 == 0 else ("TG", "Y1")
@@ -586,19 +718,17 @@ def rank_program(g, core, T, topo):
         for hi, alu in ((0, OP.min), (1, OP.max)):
             tt(T.AP[:, :, 16 * hi:16 * hi + 16], T.E0[:, 0:8, :], T.Y1[:, 0:8, 0:16], alu, ["E0", "Y1"], ["AP"])
             tt(T.TG[:, 0:8, 16 * hi:16 * hi + 16], T.E0[:, 8:16, :], T.Y1[:, 8:16, 0:16], alu, ["E0", "Y1"], ["TG"])
-        if not last:
-            half_init(T.Y2, "Y2", 1)
         tt(T.v1[:], T.AP[:], T.TG[:, 0:8, :], OP.min, ["AP", "TG"], ["v1"])
         if not last:
-            half_init(T.TG, "TG", 1)
-            tt(T.VA[:], T.v1[:], T.Y2[:, 8:16, :], OP.min, ["v1", "Y2.f"], ["VA"])
+            tt(T.VA[:], T.v1[:], fill, OP.min, ["v1", "Y2"], ["VA"])
             send(0, t + 1, "VA", "VB%d" % (t + 1))
-            turn_hash_halves()
+            turn_own()
         else:
-            turn_init(T.TG, "TG", 0, "1")
             for b in range(2):
-                tt(T.VL[:, 128 * b:128 * b + 128], T.v1[:, :, 16 * b:16 * b + 16], T.Y2[:, 8:16, 16 * b:16 * b + 16], OP.min, ["v1", "Y2.f"], ["VL.%d" % b])
-                mm(T.TG[:, 4 * b:4 * b + 4, :], T.VL[:, 128 * b:128 * b + 128], T.IU[:], False, b == 1, ["VL.%d" % b, "IU"], ["TG"])
-            cp(T.amf[:], T.TG[:, 0:8, :], ["TG"], ["amf"])
+                mm(part("OB", 256 + 128 * b, 128), T.TP[:, 4 + b, :], T.ones[:, 0:128], b == 0, False, ["TP.a%d" % (4 + b), "TP.b%d" % (4 + b)], ["OB"])
+            for b in range(2):
+                tt(T.VL[:, 128 * b:128 * b + 128], T.v1[:, :, 16 * b:16 * b + 16], T.Y2[:, 8:16, 16 * b:16 * b + 16], OP.min, ["v1", "Y2"], ["VL.%d" % b])
+                mm(part("OB", 256 + 128 * b, 128), T.VL[:, 128 * b:128 * b + 128], T.IU[:], False, b == 1, ["VL.%d" % b, "IU"], ["OB"])
+            cp(T.amf[:], part("OB", 256, 256), ["OB"], ["amf"])
             dma("S", T.ya[:], T.amf[:], ["amf"], [])
     plan["emit"](g, T)

@@ -6,11 +6,14 @@ AF = ActivationFunctionType
 RO = 3
 BIG1 = 2.0 ** 90
 BIG2 = 2.0 ** 98
+HUGE = 2.0 ** 99
 DOWN = 2.0 ** -20
 UP = 2.0 ** 20
 MAGIC = 1.5 * 2.0 ** 23
-SPLIT = [(64, 72), (64, 56)]
+SPLIT = (64, 56)
 NENG = 8
+APART = 1
+LISTS = [[1], [0]]
 
 F, B, I, U = "float32", "bfloat16", "int32", "uint16"
 
@@ -19,17 +22,17 @@ def _s(shape, d):
     return ("sbuf", [128] + list(shape), d)
 
 
-IDS = {"1": 1.0, "big": BIG2, "-1": -1.0, "1/2": 0.5, "-1024": -1024.0, "g1": -96.0 / 128, "g2": -48.0 / 128, "g3": -24.0 / 128,
-       "g4": -12.0 / 128, "g5": -7.0 / 128, "-1/128": -1.0 / 128, "-2/128": -2.0 / 128, "-64": -64.0}
-OS = {"1": 1.0, "1/2": 0.5}
-LS = {"1": 1.0, "-1": -1.0}
+IDS = {"1": 1.0, "big": BIG2, "1/2": 0.5, "-1024": -1024.0, "-64": -64.0, "-1/128": -1.0 / 128,
+       "g1": -96.0 / 128, "g2": -48.0 / 128, "g3": -24.0 / 128, "g4": -12.0 / 128, "g5": -7.0 / 128}
+OS = {"1/2": 0.5, "-1/2": -0.5}
+LS = ["own", "got"]
 BDS = {"-1/16": -1.0 / 16, "big": -BIG1 / 16}
-ROWS = {"own": -16, "got": -1, "len": 0}
+ROWS = {"own": (1, 0), "len": (-1, 48)}
 TOPS = [(0, -4096.0), (1, -4096.0), (0, 32.0), (1, 32.0), (0, 0.0), (1, 0.0)]
 
 SCRATCH = {
     "X": _s([8192], B), "xg": _s([4096], B), "yg": _s([4096], B), "S": _s([2048], F),
-    "ami": _s([256], I), "amf": _s([256], F), "Z": _s([128], B), "wi": _s([8], I), "wf": _s([8], F),
+    "ami": _s([256], I), "amf": _s([256], F), "Z": _s([128], B), "ZC": _s([128], B), "wi": _s([8], I), "wf": _s([8], F),
     "VA": _s([8, 32], F), "VL": _s([256], F), "VB0": _s([8, 32], F), "VB1": _s([8, 32], F), "VB2": _s([8, 32], F),
     "LT": _s([256], B), "LB0": _s([256], B), "LB1": _s([256], B), "LB2": _s([256], B),
     "J": _s([8], U), "JB0": _s([8], U), "JB1": _s([8], U), "JB2": _s([8], U),
@@ -38,20 +41,18 @@ SCRATCH = {
     "cm": _s([128], F), "Dm": _s([128], F), "u32": _s([128], F), "gu": _s([128], B),
     "NV": _s([1536], F), "si": _s([8], I), "sj": _s([8], I), "sk": _s([8], F), "offX": _s([8], U),
     "w": _s([256], F), "r0": _s([256], B), "rA": _s([256], B), "rB": _s([256], B), "lt": _s([256], B),
-    "KF": _s([256], F), "HB": _s([136], F), "HS": _s([136], F), "hold": _s([128], F), "inc": _s([256], F), "B16": _s([128], B), "M": _s([128], B), "y0": _s([128], B), "ge": _s([128], B),
+    "KF": _s([256], F), "HB": _s([136], F), "HS": _s([136], F), "hold": _s([128], F), "inc": _s([256], F),
+    "M": _s([128], B), "y0": _s([128], B), "ge": _s([128], B),
     "fr": _s([128], B), "nf": _s([128], B), "mm": _s([128], B), "LTt": _s([256], B), "KA": _s([256], B), "KB": _s([256], B), "s2": _s([256], B),
     "sl": _s([8], F), "offS": _s([8], U), "xd": _s([128], F), "xp": _s([128], F),
     "cA": _s([1536], B), "cY": _s([1536], B), "DA": _s([256], B), "DB": _s([256], B), "nr": _s([256], B),
     "G1": _s([512], B), "G2": _s([512], B), "G3": _s([512], B), "G4": _s([512], B), "G5": _s([512], B),
     "E0": _s([16, 16], F), "E1": _s([16, 16], F), "AP": _s([8, 32], F), "v1": _s([8, 32], F),
-    "zd": _s([128], F),
-    "rs": _s([8], F), "kc": _s([8], F),
-    "ones": _s([512], B), "onesf": _s([128], F), "ID": _s([len(IDS), 128], B), "IU": _s([128], F), "IDN": _s([128], F),
+    "zd": _s([128], F), "rs": _s([8], F), "kc": _s([8], F),
+    "ones": _s([128], B), "zero": _s([256], B), "onesf": _s([128], F), "ID": _s([len(IDS), 128], B), "IU": _s([128], F), "IDN": _s([128], F),
     "OM": _s([len(OS), 128], B), "LM": _s([len(LS), 128], B), "OT": _s([2, 128], B), "tri": _s([128], B), "dia": _s([128], B),
-    "pc": _s([16], I), "pf": _s([24], F), "io1": _s([8], F), "io3": _s([128], F), "io4": _s([6], F), "io5": _s([128], F),
-    "io2": _s([128], F), "io6": _s([8], F), "zero": _s([128], B),
-    "vtmp": _s([6], F), "WN": _s([48], B), "WR": _s([48, 32], B), "NE": _s([128], B),
-    "BD": _s([len(BDS), 8, 32], B), "BW": _s([128], B), "WZ": _s([144], B),
+    "pc": _s([16], I), "pf": _s([24], F), "io1": _s([8], F), "io2": _s([128], F), "io3": _s([128], F), "io5": _s([128], F), "io6": _s([8], F),
+    "W": _s([48], B), "WR": _s([48, 32], B), "B16": _s([128], B), "BD": _s([len(BDS), 8, 32], B), "BW": _s([128], B), "WZ": _s([144], B),
     "br": _s([8, 32], B), "TP": _s([len(TOPS), 128], B), "CT": _s([256], B),
     "topl": _s([256], B), "topf": _s([256], B), "rows": _s([len(ROWS), 256], B), "urow": _s([128], B),
     "dp": _s([8], F), "dn": _s([8], F), "jb": _s([8], F), "cx": _s([8], F), "cs": _s([8], F),
@@ -173,8 +174,8 @@ def rank_program(g, core, T, topo):
     def ms(o, c, W, R=()):
         op("V", lambda: v.memset(o, c), R, W)
 
-    def scan(o, x, y, o0, o1, R, W):
-        op("V", lambda: v.tensor_tensor_scan(o, x, y, 0.0, o0, o1), R, W)
+    def scan(o, x, y, first, o0, o1, R, W):
+        op("V", lambda: v.tensor_tensor_scan(o, x, y, first, o0, o1), R, W)
 
     def act(o, x, f, R, W, bias=0.0, scale=1.0, acc=None):
         if acc is not None:
@@ -199,7 +200,10 @@ def rank_program(g, core, T, topo):
         else:
             op("G", lambda: g.iota(o, pat, base, ch), (), W)
 
-    def send(k, t, src, dst):
+    def select(o, x, pat, alu, fill, base, ch, R, W):
+        op("G", lambda: g.affine_select(o, x, pat, alu, fill, base, ch), R, W)
+
+    def send(k, t, src, dst, R=None):
         to = T.cores[(rank + 1 + t % (N - 1)) % N]
         fr = T.cores[(rank - 1 - t % (N - 1)) % N]
         eng = topo.engines(core, to)[:NENG]
@@ -207,10 +211,11 @@ def rank_program(g, core, T, topo):
         rid, pid = topo.addr(to)[:2]
         n = 3 * t + k
         op("G", lambda: g.remote_dma(T[dst][:], T[src][:], T.sem["a%d" % n], T.sem["l%d" % n], pid, rid, mask),
-           [src], [], sem="l%d" % n, inc=len(eng))
+           R or [src], [], sem="l%d" % n, inc=len(eng))
         op("G", None, [], [dst], sem="a%d" % n, inc=len(topo.engines(fr, core)[:NENG]))
 
     XB, YB = [T.X0, T.X1, T.X2], [T.Y0, T.Y1, T.Y2]
+    VK = ["VA.0", "VA.1"]
 
     def lev(l):
         return XB[l % 3][:, (l // 3) * 256:(l // 3) * 256 + 256]
@@ -220,9 +225,6 @@ def rank_program(g, core, T, topo):
 
     def ident(name):
         return pick("ID", IDS, name)
-
-    def row(name):
-        return T.rows[0:1, list(ROWS).index(name), :]
 
     def part(bk, c0, n):
         if bk in ("X0", "X1", "X2", "OB"):
@@ -239,74 +241,63 @@ def rank_program(g, core, T, topo):
     dma("A", T.X[:, 4096:8192], T.xt[:, 4096:8192], [], ["X.b"])
     XK = ["X.a", "X.b"]
 
-    ms(T.ones[:], 1.0, ["ones"])
-    iota(T.pc[:, 0:1], [[0, 1]], 0, 1, ["pc0"], flt=False)
-    ms(T.zero[:], 0.0, ["zero"])
-
     def diagonals(which):
         for n_ in which:
-            op("G", lambda n_=n_: g.affine_select(ident(n_), T.zero[:], [[-1, 128]], OP.not_equal, IDS[n_], 0, 1), ["zero"], ["ID." + n_])
-    diagonals(["1"])
-    iota(T.io3[:], [[1, 8], [0, 16]], 0, 0, ["io3"])
-    iota(T.io1[:], [[1, 8]], 0, 0, ["io1"])
-    iota(T.io4[:], [[3, 6]], 2, 0, ["io4"])
-    diagonals(["-1024"])
-    ms(T.WN[:], 0.0, ["WN"])
+            select(ident(n_), T.zero[:, 0:128], [[-1, 128]], OP.not_equal, IDS[n_], 0, 1, ["zero"], ["ID." + n_])
 
     def key_weights(rows):
         for p in rows:
             l = p // 3
             c0 = 16 * (l % 3) + 8 * (l // 3)
-            op("G", lambda p=p, l=l, c0=c0: g.affine_select(T.WN[:, c0:c0 + 8], T.WN[:, c0:c0 + 8], [[-16, 8]], OP.not_equal,
-                                                            -2.0 ** (48 - 25 * l + 8 * (2 - p % 3)), -p, 1), ["WN.%d" % l, "WN"], ["WN.%d" % l])
-
-    def scaled(buf, names, which):
-        first = list(names)[0]
-        for n_ in which:
-            act(pick(buf, names, n_), pick(buf, names, first), AF.Identity, ["%s.%s" % (buf, first)], ["%s.%s" % (buf, n_)],
-                scale=names[n_] / names[first])
-    key_weights([0, 3, 6, 9, 12, 15, 1])
-    ms(T.br[:, :, 0:1], 0.0, ["br"])
-    ms(T.TP[:], 0.0, ["TP"])
-    fills = [(T.urow[0:1, :], 192.0 * 1024, "urow"), (T.kc[:, 0:1], 4096.0 * 33 - 2.0 ** 23, "kc"), (T.WZ[:], 0.0, "WZ"),
-             (T.w[:, 255:256], 0.0, "w"), (T.OB[:, 255:256], 0.0, "OB")]
-    for s in range(5):
-        ts(T.br[:, :, 2 ** s:2 ** (s + 1)], T.br[:, :, 0:2 ** s], float(4 * 2 ** (4 - s)), None, OP.add, None, ["br"], ["br"])
-        ms(fills[s][0], fills[s][1], [fills[s][2]])
-    act(T.IDN[:], ident("1"), AF.Identity, ["ID.1"], ["IDN"], scale=DOWN)
-    act(T.topl[0:1, :], T.br[0:1, :, :], AF.Identity, ["br"], ["topl"], scale=2.0 ** -7)
-    act(T.IU[:], ident("1"), AF.Identity, ["ID.1"], ["IU"], scale=UP)
+            select(T.W[:, c0:c0 + 8], T.W[:, c0:c0 + 8], [[-16, 8]], OP.not_equal, 2.0 ** (48 - 25 * l + 8 * (2 - p % 3)), -p, 1,
+                   ["W.%d" % l, "W"], ["W.%d" % l])
 
     def tops(which):
         for n_ in which:
             e, c = TOPS[n_]
-            act(T.TP[0:1, n_, :], T.br[0:1, :, 0::2] if c else T.br[0:1, :, 0:16], AF.Identity, ["br", "TP"], ["TP.a%d" % n_], scale=-8192.0)
-            if e:
-                ms(T.TP[32:33, n_, :], (-64.0 if c else -4.0) * 8192, ["TP.b%d" % n_])
-            if c:
-                ms(T.TP[64:65, n_, :], c, ["TP.b%d" % n_])
-    tops([0, 1, 2, 3])
-    ts(T.pc[:, 1:2], T.pc[:, 0:1], 15, None, OP.bitwise_and, None, ["pc0"], ["pc1"])
-    ts(T.pc[:, 2:3], T.pc[:, 0:1], 4, None, OP.arith_shift_right, None, ["pc0"], ["pc1"])
-    ts(T.pc[:, 3:4], T.pc[:, 0:1], 31, None, OP.bitwise_and, None, ["pc0"], ["pc1"])
-    ts(T.pc[:, 4:5], T.pc[:, 0:1], 5, None, OP.arith_shift_right, None, ["pc0"], ["pc1"])
+            act(T.TP[0:1, n_, :], T.br[0:1, :, 0::2] if c else T.br[0:1, :, 0:16], AF.Identity, ["br", "TP"], ["TP.%d" % n_], scale=-8192.0)
+
+    ms(T.zero[:], 0.0, ["zero"])
+    iota(T.pc[:, 0:1], [[0, 1]], 0, 1, ["pc0"], flt=False)
+    iota(T.io1[:], [[1, 8]], 0, 0, ["io1"])
+    diagonals(["1"])
+    iota(T.io3[:], [[1, 8], [0, 16]], 0, 0, ["io3"])
+    ms(T.br[:, :, 0:1], 0.0, ["br"])
+    ms(T.W[:], 0.0, ["W"])
+    key_weights([0, 3, 6, 9, 12, 15, 1, 4, 7, 10])
+    between = [lambda: ms(T.ones[:], 1.0, ["ones"]),
+               lambda: ts(T.pc[:, 1:2], T.pc[:, 0:1], 15, None, OP.bitwise_and, None, ["pc0"], ["pc1"]),
+               lambda: ts(T.pc[:, 2:3], T.pc[:, 0:1], 4, None, OP.arith_shift_right, None, ["pc0"], ["pc1"]),
+               lambda: ts(T.pc[:, 3:4], T.pc[:, 0:1], 31, None, OP.bitwise_and, None, ["pc0"], ["pc1"]),
+               lambda: ts(T.pc[:, 4:5], T.pc[:, 0:1], 5, None, OP.arith_shift_right, None, ["pc0"], ["pc1"])]
+    for s in range(5):
+        ts(T.br[:, :, 2 ** s:2 ** (s + 1)], T.br[:, :, 0:2 ** s], float(4 * 2 ** (4 - s)), None, OP.add, None, ["br"], ["br"])
+        between[s]()
+    ms(T.TP[:], 0.0, ["TP"])
     cp(T.pf[:, 1:5], T.pc[:, 1:5], ["pc1"], ["pf"])
     P_, G_, K_, Q_ = T.pf[:, 1:2], T.pf[:, 2:3], T.pf[:, 3:4], T.pf[:, 4:5]
+    act(T.IDN[:], ident("1"), AF.Identity, ["ID.1"], ["IDN"], scale=DOWN)
+    act(T.IU[:], ident("1"), AF.Identity, ["ID.1"], ["IU"], scale=UP)
+    act(T.topl[0:1, :], T.br[0:1, :, :], AF.Identity, ["br"], ["topl"], scale=2.0 ** -7)
+    act(ident("-1024"), ident("1"), AF.Identity, ["ID.1"], ["ID.-1024"], scale=-1024.0)
+    tops([1, 0])
+    ms(T.urow[0:1, :], 192.0 * 1024, ["urow"])
+    ms(T.kc[:, 0:1], 4096.0 * 33 - 2.0 ** 23, ["kc"])
     cp(T.amf[:], T.ami[:], ["ami"], ["amf"])
-    mm(T.TG[:, 0:8, :], T.ones[0:1, 0:128], T.topl[0:1, :], True, False, ["ones", "topl"], ["TG"])
+    cp(T.wf[:, 0:1], T.wi[:, 0:1], ["wi"], ["wf"])
+    ms(T.TP[32:33, 1:4:2, :], -64.0 * 8192, ["TP.c"], ["TP"])
+    ts(T.BW[:], T.io3[:], G_, T.wf[:, 0:1], OP.is_equal, OP.mult, ["io3", "pf", "wf"], ["BW"])
+    ms(T.TP[64:65, 0:2, :], -4096.0, ["TP.c"])
+    mm(T.TG[:, 0:8, :], T.ones[0:1, :], T.topl[0:1, :], True, False, ["ones", "topl"], ["TG"])
     for b in range(2):
         mm(T.TG[:, 0:8, 16 * b:16 * b + 16], T.amf[:, 128 * b:128 * b + 128], T.IDN[:], False, b == 1, ["amf", "IDN"], ["TG"])
-    cp(T.wf[:, 0:1], T.wi[:, 0:1], ["wi"], ["wf"])
-    ts(T.BW[:], T.io3[:], G_, T.wf[:, 0:1], OP.is_equal, OP.mult, ["io3", "pf", "wf"], ["BW"])
+    ms(T.TP[64:65, 2:4, :], 32.0, ["TP.c"])
+    ms(T.WZ[:], 0.0, ["WZ"])
+    cp(T.VA[:], T.TG[:, 0:8, :], ["TG"], VK)
     ts(T.WZ[:, 16::16], T.io1[:], G_, T.wf[:, 0:1], OP.is_equal, OP.mult, ["io1", "pf", "wf", "WZ"], ["WZ"])
-    cp(T.VA[:], T.TG[:, 0:8, :], ["TG"], ["VA"])
-    send(0, 0, "VA", "VB0")
-    key_weights([4, 7, 10, 13, 2, 5, 8, 11, 14])
-    iota(T.io5[:], [[1, 4], [0, 32]], 0, 0, ["io5"])
-    iota(T.io2[:], [[0, 8], [1, 16]], 0, 0, ["io2"])
-    iota(T.io6[:], [[0, 4], [1024, 2]], 0, 0, ["io6"])
-    diagonals(["big"])
-    E_, NE_ = T.pf[:, 15:16], T.pf[:, 16:17]
+    send(0, 0, "VA", "VB0", VK)
+    key_weights([13, 2, 5, 8, 11, 14])
+    WK = ["W.%d" % l for l in range(6)]
 
     def make_u(step):
         raw, big, small = part("Y0", 0, 128), part("Y0", 256, 128), T.Y0[:, 4, 0:8]
@@ -314,12 +305,13 @@ def rank_program(g, core, T, topo):
             mm(raw, T.BW[:], T.Z[:], True, True, ["BW", "Z"], ["Y0"])
             act(T.gu[:], raw, AF.Identity, ["Y0"], ["gu"], bias=192.0 - 0.5 + 2.0 ** -11, scale=2.0 ** -10)
         if step == 1:
-            mm(big, T.urow[0:1, :], T.ones[0:1, 0:128], True, False, ["urow", "ones"], ["Y0"])
+            mm(big, T.urow[0:1, :], T.ones[0:1, :], True, False, ["urow", "ones"], ["Y0"])
             mm(big, T.BW[:], T.Z[:], False, False, ["BW", "Z"], ["Y0"])
             mm(big, ident("-1024"), T.gu[:], False, True, ["ID.-1024", "gu"], ["Y0"])
             act(T.cm[:], big, AF.Identity, ["Y0"], ["cm"], bias=33.0, scale=2.0)
             act(T.Dm[:], big, AF.Identity, ["Y0", "kc"], ["Dm"], bias=T.kc[:, 0:1], scale=8192.0)
             act(T.u32[:], big, AF.Identity, ["Y0"], ["u32"], scale=1.0 / 32)
+            act(T.ZC[:], T.Z[:], AF.Identity, ["Z"], ["ZC"], bias=255.0, scale=-1.0)
         if step == 2:
             for r in range(16):
                 mm(small, T.WZ[:, 16 - r:144 - r], T.Z[:, r::16], r == 0, r == 15, ["WZ", "Z"], ["Y0"])
@@ -343,12 +335,12 @@ def rank_program(g, core, T, topo):
     def turn_init(where, top, es=(1, 0)):
         for e in es:
             bk, c0 = where[e]
-            mm(part(bk, c0, 128), T.TP[:, top + e, :], T.ones[:, 0:128], True, False, ["TP", "TP.a%d" % (top + e), "TP.b%d" % (top + e), "ones"], [bk])
+            mm(part(bk, c0, 128), T.TP[:, top + e, :], T.ones[:], True, False, ["TP", "TP.c", "TP.%d" % (top + e), "ones"], [bk])
 
     def turn(where, src, es=(1, 0)):
         for e in es:
             bk, c0 = where[e]
-            mm(part(bk, c0, 128), T[src][:, :, e::2], T.IU[:], False, True, [src, "IU"], [bk])
+            mm(part(bk, c0, 128), T[src][:, :, e::2], T.IU[:], False, True, ["VA.%d" % e if src == "VA" else src, "IU"], [bk])
 
     def hash_step(where, off, step, e):
         bk, c0 = where[e]
@@ -376,36 +368,28 @@ def rank_program(g, core, T, topo):
                 hash_step(OWN, "offA", step, e)
 
     def gather(eng, dst, off, e, i0, i1):
-        if i0 == i1:
-            return
         c0, c1 = 128 * e + i0, 128 * e + i1
         o, x = T[dst][:, 16 * c0:16 * c1], T.X[:, 0:8192].indirect(T[off][:, c0:c1])
         key = "%s.%d%s" % (dst, e, eng)
         if eng == "V":
-            cp(o, x, XK + ["%s.%d" % (off, e)], [key])
+            ts(o, x, -1.0, 255.0, OP.mult, OP.add, XK + ["%s.%d" % (off, e)], [key])
         else:
-            act(o, x, AF.Copy, XK + ["%s.%d" % (off, e)], [key])
+            act(o, x, AF.Identity, XK + ["%s.%d" % (off, e)], [key], bias=255.0, scale=-1.0)
 
     def allkeys(dst):
         return ["%s.%d%s" % (dst, e, q) for e in range(2) for q in "VA"]
 
-    def key_init(j):
-        mm(XB[j][:], T.NE[:], T.WR[:, 16 * j:16 * j + 16, :], True, False, ["NE", "WR"], ["X%d" % j])
-
     def keys(dst, name, e, j, stop=False):
         for r in range(16):
             k = 2 * r + e
-            mm(YB[j][:, :, k] if name == "Y" else XB[j][:, k::32], T[dst][:, 2048 * e + r:2048 * e + 2048:16], T.WN[:, 16 * j:16 * j + 16],
-               name == "Y" and e == 1 and r == 0, stop and r == 15, ["%s.%dV" % (dst, e), "%s.%dA" % (dst, e)] + WK, ["%s%d" % (name, j)])
-
-    def start_row(bk, name):
-        mm(part(bk, 0, 256), T.ones[0:1, 0:128], row(name), True, False, ["ones", "rows"], [bk])
+            mm(YB[j][:, :, k] if name == "Y" else XB[j][:, k::32], T[dst][:, 2048 * e + r:2048 * e + 2048:16], T.W[:, 16 * j:16 * j + 16],
+               e == 1 and r == 0, stop and r == 15, ["%s.%dV" % (dst, e), "%s.%dA" % (dst, e)] + WK, ["%s%d" % (name, j)])
 
     def blocks(bk, c0, terms, stop, start=False):
         for n_, (src, buf, names, name) in enumerate(terms):
             for h in range(2):
-                mm(part(bk, c0 + 128 * h, 128), half(src, h), pick(buf, names, name), start and h == 0 and n_ == 0, stop and h == 1 and n_ == len(terms) - 1,
-                   [src, "%s.%s" % (buf, name)], [bk])
+                mm(part(bk, c0 + 128 * h, 128), half(src, h), pick(buf, names, name), start and h == 0 and n_ == 0,
+                   stop and h == 1 and n_ == len(terms) - 1, [src, "%s.%s" % (buf, name)], [bk])
 
     def sign_marks(bk, c0, marks):
         for h in range(2):
@@ -421,20 +405,19 @@ def rank_program(g, core, T, topo):
                 mm(part(bk, c0 + 128 * h, 128), T[src][:, 256 * c + 128 * h:256 * c + 128 * h + 128], ident("1"), False,
                    stop and c % 2 == 1 and h == 1, ["%s.%d" % (src, j), "ID.1"], [bk])
 
-    WK = ["WN.%d" % l for l in range(6)]
-    turn_init(OWN, 0)
     make_u(0)
+    turn_init(OWN, 0)
     make_u(1)
-    ts(T.vtmp[:], T.io4[:], 15.0, P_, OP.min, OP.is_equal, ["io4", "pf"], ["vtmp"])
-    ms(T.r0[:], 1.0, ["r0"])
-    op("V", lambda: v.tensor_reduce(T.pf[:, 15:16], T.vtmp[:], AxisListType.X, OP.add), ["vtmp"], ["pe"])
-    ms(T.r0[:, 31::32], 0.0, ["r0"], ["r0"])
-    ts(T.pf[:, 16:17], T.pf[:, 15:16], -1.0, None, OP.mult, None, ["pe"], ["pn"])
+    tops([2, 3])
     turn_own()
-    act(T.NE[:], T.ones[:, 0:128], AF.Identity, ["ones", "pn"], ["NE"], scale=NE_)
-    act(T.WR[:, :, 0:1], T.WN[:], AF.Identity, WK, ["WR"], scale=-1.0)
-    for s in range(5):
+
+    act(T.WR[:, :, 0:1], T.W[:], AF.Identity, WK, ["WR"], scale=-1.0)
+    for s in range(4):
         act(T.WR[:, :, 2 ** s:2 ** (s + 1)], T.WR[:, :, 0:2 ** s], AF.Copy, ["WR"], ["WR"])
+    ms(T.r0[:], 0.0, ["r0"])
+    ms(T.w[:, 255:256], HUGE, ["w"])
+    ms(T.OB[:, 255:256], HUGE, ["OB"])
+    ms(T.r0[:, 31::32], HUGE, ["r0"], ["r0"])
     fill0 = -131072.0 - 31.0 / 64
     ts(T.pf[:, 8:9], P_, 74.0, fill0, OP.mult, OP.add, ["pf"], ["pf8"])
     ts(T.pf[:, 9:10], P_, 74.0, fill0 + 37, OP.mult, OP.add, ["pf"], ["pf8"])
@@ -444,41 +427,60 @@ def rank_program(g, core, T, topo):
     ts(T.dn[:], T.io1[:], G_, -1.0, OP.is_equal, OP.mult, ["io1", "pf"], ["dn"])
     ts(T.jb[:], T.io1[:], 256.0 * DOWN, T.pf[:, 11:12], OP.mult, OP.add, ["io1", "pf10"], ["jb"])
     ts(T.cx[:], T.io1[:], 1024.0, T.pf[:, 12:13], OP.mult, OP.add, ["io1", "pf12"], ["cx"])
-    for b in range(2):
-        ts(T.BD[:, 0, :, 16 * b:16 * b + 16], T.io3[:], G_, -1.0 / 16, OP.is_equal, OP.mult, ["io3", "pf"], ["BD.-1/16"])
     ts(T.B16[:], T.io3[:], G_, None, OP.is_equal, None, ["io3", "pf"], ["B16"])
-    for h in range(2):
-        ts(T.OT[:, h, :], T.io3[:], float(-4 * h), Q_, OP.add, OP.is_equal, ["io3", "pf"], ["OT"])
-    ms(T.HB[:], 0.0, ["HB"])
-    ms(T.HS[:, 128:136], 0.0, ["HS"])
-    ms(T.CT[:], 0.0, ["CT"])
-    ts(T.dia[:], ident("1"), K_, None, OP.mult, None, ["ID.1", "pf"], ["dia"])
-    ms(T.CT[0:1, :], 280.0, ["CT"], ["CT"])
-    ms(T.CT[32:33, :], 66.0 / 128, ["CT"])
-    ts(T.CT[64:65, :], T.br[64:65, :, :], -1.0 / 128, None, OP.mult, None, ["br"], ["CT"])
-    ts(T.topf[0:1, :], T.br[0:1, :, :], 2.0 ** -7, 1.5, OP.mult, OP.add, ["br"], ["topf"])
-    ts(pick("OM", OS, "1"), T.io5[:], Q_, None, OP.is_equal, None, ["io5", "pf"], ["OM.1"])
+    ts(T.dia[:], ident("1"), K_, 0.5, OP.mult, OP.mult, ["ID.1", "pf"], ["dia"])
+    iota(T.io5[:], [[1, 4], [0, 32]], 0, 0, ["io5"])
     ts(pick("OM", OS, "1/2"), T.io5[:], Q_, 0.5, OP.is_equal, OP.mult, ["io5", "pf"], ["OM.1/2"])
-    ts(T.hold[:], T.io2[:], P_, None, OP.is_le, None, ["io2", "pf"], ["hold"])
-    ts(T.cs[:], T.io6[:], T.pf[:, 12:13], None, OP.add, None, ["io6", "pf12"], ["cs"])
-    ms(T.hold[:, 0::16], 0.0, ["hold"], ["hold"])
-    op("G", lambda: g.affine_select(T.tri[:], pick("OM", OS, "1"), [[1, 128]], OP.is_ge, 0.0, 0, -1), ["OM.1"], ["tri"])
+    diagonals(["1/2", "-64"])
+    select(T.tri[:], pick("OM", OS, "1/2"), [[1, 128]], OP.is_ge, 0.0, 0, -1, ["OM.1/2"], ["tri"])
+    diagonals(["big"])
+    iota(T.io2[:], [[0, 8], [1, 16]], 0, 0, ["io2"])
+    iota(T.io6[:], [[0, 4], [1024, 2]], 0, 0, ["io6"])
     iota(T.inc[:], [[0, 128], [-4095, 2]], 2048, 0, ["inc"])
-    diagonals(["-64", "1/2", "-2/128", "g1", "g2", "g3", "g4", "g5", "-1", "-1/128"])
-    for k, (n_, c) in enumerate(ROWS.items()):
-        iota(T.rows[:, k, :], [[0, 8], [1 if n_ == "own" else -1, 32]], c, 0, ["rows"])
+    iota(T.HB[:], [[0, 136]], 0, 0, ["HB"])
+    iota(T.HS[:, 128:136], [[0, 8]], 0, 0, ["HS"])
+    iota(T.CT[:], [[0, 256]], 0, 0, ["CT"])
+    diagonals(["g1", "g2", "g3", "g4", "g5", "-1/128"])
+    for n_, (sign, c) in enumerate(ROWS.values()):
+        iota(T.rows[:, n_, :], [[0, 8], [sign, 32]], c, 0, ["rows"])
     iota(T.onesf[:], [[0, 128]], 32, 0, ["onesf"])
+    first_spare = [
+        lambda: ts(pick("LM", LS, "own"), part("Y1", 0, 128), -2.0, None, OP.mult, None, ["Y1"], ["LM.own"]),
+        lambda: ts(pick("LM", LS, "got"), part("Y1", 128, 128), -1.0, None, OP.mult, None, ["Y1"], ["LM.got"]),
+        lambda: ts(T.hold[:], T.io2[:], P_, None, OP.is_le, None, ["io2", "pf"], ["hold"]),
+        lambda: ts(T.cs[:], T.io6[:], T.pf[:, 12:13], None, OP.add, None, ["io6", "pf12"], ["cs"]),
+        lambda: ms(T.hold[:, 0::16], 0.0, ["hold"], ["hold"]),
+        lambda: ts(T.OT[:, 0, :], T.io3[:], 0.0, Q_, OP.add, OP.is_equal, ["io3", "pf"], ["OT"]),
+        lambda: ts(T.OT[:, 1, :], T.io3[:], -4.0, Q_, OP.add, OP.is_equal, ["io3", "pf"], ["OT"])]
 
-    def late_constants():
-        scaled("BD", BDS, ["big"])
-        act(T.OT[:], T.OT[:], AF.Identity, ["OT"], ["OT"], scale=-1.0)
-        scaled("LM", LS, ["-1"])
-        tops([4, 5])
+    def late_constants(k):
+        if k == 0:
+            for n_ in range(2):
+                o = part("Y1", 128 * n_, 128)
+                mm(o, ident("1"), T.tri[:], n_ == 0, False, ["ID.1", "tri"], ["Y1"])
+                mm(o, ident("1"), T.dia[:], False, False, ["ID.1", "dia"], ["Y1"])
+            mm(part("Y1", 128, 128), ident("-64"), ident("1/2"), False, True, ["ID.-64", "ID.1/2"], ["Y1"])
+        if k == 1:
+            act(T.WR[:, :, 16:32], T.WR[:, :, 0:16], AF.Copy, ["WR"], ["WR"])
+            for n_, (name, c) in enumerate(BDS.items()):
+                for b in range(2):
+                    act(T.BD[:, n_, :, 16 * b:16 * b + 16], T.B16[:], AF.Identity, ["B16"], ["BD." + name], scale=c)
+        if k == 2:
+            act(T.OT[:], T.OT[:], AF.Identity, ["OT"], ["OT"], scale=-1.0)
+            act(pick("OM", OS, "-1/2"), pick("OM", OS, "1/2"), AF.Identity, ["OM.1/2"], ["OM.-1/2"], scale=-1.0)
+            act(T.CT[0:1, :], T.zero[0:1, :], AF.Identity, ["zero", "CT"], ["CT.c"], bias=280.0)
+            act(T.CT[32:33, :], T.br[32:33, :, :], AF.Identity, ["br", "CT"], ["CT.c"], bias=0.5, scale=-1.0 / 128)
+        if k == 3:
+            act(T.topf[0:1, :], T.br[0:1, :, :], AF.Identity, ["br"], ["topf"], bias=1.5, scale=2.0 ** -7)
+            tops([4, 5])
+            ms(T.TP[32:33, 5, :], -4.0 * 8192, ["TP.c"])
 
-    def sums(j):
+    def sums(j, bk):
         for q in range(4):
-            mm(T.X0[:], ident("1"), T.X[:, 2048 * q + 512 * j:2048 * q + 512 * j + 512], q == 0, q == 3, ["ID.1"] + XK, ["X0"])
-        act(T.S[:, 512 * j:512 * j + 512], T.X0[:], AF.Copy, ["X0"], ["S.%d" % (j // 2)])
+            mm(T[bk][:], ident("1"), T.X[:, 2048 * q + 512 * j:2048 * q + 512 * j + 512], q == 0, q == 3, ["ID.1"] + XK, [bk])
+
+    def keep_sums(j, bk):
+        act(T.S[:, 512 * j:512 * j + 512], T[bk][:], AF.Copy, [bk], ["S.%d" % (j // 2)])
 
     def patch(t, k):
         if t == 0:
@@ -492,53 +494,59 @@ def rank_program(g, core, T, topo):
         else:
             cp(win, T.xp[:, c], ["xp", "offS"], SK)
 
-    off = [192.0 - 0.5 + 2.0 ** -(s + 1) for s in range(6)]
-
-    def quot(eng, s, h, src, key):
-        o = T["G%d" % s][:, 256 * h:256 * h + 256]
+    def quot(eng, s, h, src):
+        o, off = T["G%d" % s][:, 256 * h:256 * h + 256], 192.0 - 0.5 + 2.0 ** -(s + 1)
         if eng == "V":
-            ts(o, src, 2.0 ** -s, off[s], OP.mult, OP.add, [key], ["G%d.%d" % (s, h)])
+            ts(o, T[src][:], 2.0 ** -s, off, OP.mult, OP.add, [src], ["G%d.%d" % (s, h)])
         else:
-            act(o, src, AF.Identity, [key], ["G%d.%d" % (s, h)], bias=off[s], scale=2.0 ** -s)
+            act(o, T[src][:], AF.Identity, [src], ["G%d.%d" % (s, h)], bias=off, scale=2.0 ** -s)
 
     def quot_add(bk, s, h, stop=False):
         mm(part(bk, 0, 256), ident("g%d" % s), T["G%d" % s][:, 256 * h:256 * h + 256], False, stop, ["ID.g%d" % s, "G%d.%d" % (s, h)], [bk])
 
+    def stage(s, hs):
+        ei, eo = ("E0", "E1") if s % 2 == 0 else ("E1", "E0")
+        ki, ko = ("Y1", "TG") if s % 2 == 0 else ("TG", "Y1")
+        c = slice(8 * hs[0], 8 * hs[-1] + 8)
+        for hi, alu in ((0, OP.min), (1, OP.max)):
+            for par in range(2):
+                ok = eo if par == 0 else ko
+                tt(T[ok][:, c, 8 * hi:8 * hi + 8], T[ei][:, c, par::2], T[ki][:, c, par:16:2], alu,
+                   ["%s.%d" % (x, h) for x in (ei, ki) for h in hs], ["%s.%d" % (ok, h) for h in hs])
+
     for t in range(RO):
         last = t == RO - 1
         VB, LB, JB = "VB%d" % t, "LB%d" % t, "JB%d" % t
-        s1, s0 = SPLIT[min(t, 1)]
+
+        def early(k):
+            if last:
+                patch(t, k)
+
+        def late(k):
+            if not last:
+                patch(t, k)
+        s1, s0 = SPLIT
         gather("A", "xg", "offA", 1, s1, 128)
         gather("A", "xg", "offA", 0, s0, 128)
         turn_init(GOT, 0)
-        if t > 0:
-            for j in range(3):
-                key_init(j)
         turn(GOT, VB)
-        spare = [lambda k=k: columns(k) for k in range(1, 6 if t > 0 else 4)]
-        if t > 0:
-            gather("V", "xg", "offA", 1, 0, s1)
-            gather("V", "xg", "offA", 0, 0, s0)
-            for step, other in enumerate((lambda: fill_product(0), lambda: fill_product(1), lambda: columns(0), None)):
-                hash_step(GOT, "offB", step, 1)
-                if other:
-                    other()
-            spare = [lambda k=k: hash_step(GOT, "offB", k, 0) for k in range(4)] + spare
-        else:
-            for step in range(4):
-                for e in (1, 0):
-                    hash_step(GOT, "offB", step, e)
-            for j in range(3):
-                key_init(j)
-            fill_product(0)
-            fill_product(1)
-            columns(0)
-            gather("V", "xg", "offA", 1, 0, s1)
-            gather("V", "xg", "offA", 0, 0, s0)
-            spare.append(lambda: tt(pick("LM", LS, "1"), T.dia[:], T.tri[:], OP.add, ["dia", "tri"], ["LM.1"]))
+        gather("V", "xg", "offA", 1, 0, s1)
+        gather("V", "xg", "offA", 0, 0, s0)
+        for step, other in enumerate((lambda: fill_product(0), lambda: fill_product(1), lambda: columns(0), None)):
+            hash_step(GOT, "offB", step, 1)
+            if other:
+                other()
+        spare = [lambda k=k: hash_step(GOT, "offB", k, 0) for k in range(4)]
+        if t == 0:
+            spare += [lambda: [f() for f in first_spare[0:2]], first_spare[2]]
+        spare += [lambda k=k: columns(k) for k in range(1, 6 if t > 0 else 4)]
+        if t == 0:
+            spare += [lambda: [f() for f in first_spare[3:5]], lambda: [f() for f in first_spare[5:]]]
         gather("A", "yg", "offB", 1, 0, 128)
         for j in range(3):
             keys("xg", "X", 1, j)
+        if t == 0:
+            late_constants(0)
         keys("xg", "X", 0, 0, True)
         keys("xg", "X", 0, 1)
         r = "r0"
@@ -546,15 +554,17 @@ def rank_program(g, core, T, topo):
             if l < 3:
                 kx, kw = "X%d" % l, "w"
                 nv, w = lev(l), T.w[:]
-                scan(T.w[:, 254::-1], XB[l][:, 255:0:-1], T[r][:, 254::-1], OP.min, OP.mult, [kx, r], [kw])
+                scan(T.w[:, 254::-1], XB[l][:, 255:0:-1], T[r][:, 254::-1], HUGE, OP.min, OP.max, [kx, r], [kw])
             else:
                 c0, kx, kw = 512 * (l - 3) + 256, "NV.%d" % l, "OB"
                 nv, w = T.NV[:, c0:c0 + 256], T.OB[:, 0:256]
-                scan(T.OB[:, 254::-1], T.NV[:, c0 + 255:c0:-1], T[r][:, 254::-1], OP.min, OP.mult, [kx, r], [kw])
+                scan(T.OB[:, 254::-1], T.NV[:, c0 + 255:c0:-1], T[r][:, 254::-1], HUGE, OP.min, OP.max, [kx, r], [kw])
             if spare:
                 spare.pop(0)()
             if l == 2:
                 gather("A", "yg", "offB", 0, 0, 128)
+            if l == 3 and t == 0:
+                late_constants(1)
             if l < 5:
                 tt(T.lt[:], nv, w, OP.is_gt, [kx, kw], ["lt"])
                 if l < 2:
@@ -565,54 +575,57 @@ def rank_program(g, core, T, topo):
                     for j in range(3):
                         keys("yg", "Y", 1, j)
                 r = "rA" if l % 2 == 0 else "rB"
-                tt(T[r][:], nv, w, OP.is_ge, [kx, kw], [r])
+                tt(T[r][:], w, nv, OP.subtract, [kx, kw], [r])
                 if l >= 2:
                     tt(T.NV[:, 512 * (l - 2) + 256:512 * (l - 2) + 512], lev(l + 1), T.lt[:], OP.add, ["X%d" % (l - 2), "lt"], ["NV.%d" % (l + 1)])
+                if l == 2:
+                    keys("xg", "X", 1, 0)
+                    keys("xg", "X", 0, 0)
                 if spare:
                     spare.pop(0)()
                 if l == 4:
                     mm(T.TG[:, 8, 0:8], T.IU[:], T.jb[:], True, False, ["IU", "jb"], ["TG"])
                     for j in (2, 1, 0):
                         keys("yg", "Y", 0, j)
-                if l == 3:
-                    key_init(0)
-                    keys("xg", "X", 1, 0)
-                    keys("xg", "X", 0, 0)
             else:
                 tt(T.LT[:], nv, w, OP.is_gt, [kx, kw], ["LT"])
-        if t == 0:
-            late_constants()
         for l in (1, 2):
             act(T.NV[:, 512 * l:512 * l + 256], lev(l), AF.Copy, ["X%d" % l], ["NV.%d" % l])
-        for e in range(2):
-            act(T.f1[:, 128 * e:128 * e + 128], T.ft[:, 128 * e:128 * e + 128], AF.Identity, ["ft", "pf8"], ["f1"], bias=T.pf[:, 8 + e:9 + e])
-        act(T.ft[:], T.f1[:], AF.Identity, ["f1"], ["ft"], bias=MAGIC)
+
+        def fill_names(k):
+            if k == 0:
+                for e in range(2):
+                    act(T.f1[:, 128 * e:128 * e + 128], T.ft[:, 128 * e:128 * e + 128], AF.Identity, ["ft", "pf8"], ["f1"], bias=T.pf[:, 8 + e:9 + e])
+                act(T.ft[:], T.f1[:], AF.Identity, ["f1"], ["ft"], bias=MAGIC)
+            else:
+                act(T.fbf[:], T.ft[:], AF.Identity, ["ft"], ["fbf"], bias=-MAGIC)
+                act(T.gf[:], T.fbf[:], AF.Identity, ["fbf"], ["gf"], bias=192.0 - 0.5 + 2.0 ** -14, scale=2.0 ** -13)
+        if t > 0:
+            fill_names(0)
         send(2, t, "LT", LB)
-        scan(T.KF[:, ::-1], T.inc[:, ::-1], T.LT[:, ::-1], OP.add, OP.mult, ["inc", "LT"], ["KF"])
+        scan(T.KF[:, ::-1], T.inc[:, ::-1], T.LT[:, ::-1], 0.0, OP.add, OP.mult, ["inc", "LT"], ["KF"])
         for h in range(2):
             mm(part("OB", 256 + 128 * h, 128), half("LT", h), ident("1"), h == 0, h == 1, ["LT", "ID.1"], ["OB"])
         act(T.LTt[:], part("OB", 256, 256), AF.Identity, ["OB"], ["LTt", "rs"], acc=T.rs[:, 0:1])
-        act(T.fbf[:], T.ft[:], AF.Identity, ["ft"], ["fbf"], bias=-MAGIC)
-        act(T.gf[:], T.fbf[:], AF.Identity, ["fbf"], ["gf"], bias=192.0 - 0.5 + 2.0 ** -14, scale=2.0 ** -13)
+        if t > 0:
+            fill_names(1)
+        else:
+            late_constants(2)
         cp(T.HB[:, 0:128:16], T.KF[:, 0::32], ["KF"], ["HB"])
-        scan(T.HS[:, 0:128], T.hold[:], T.HB[:, 0:128], OP.mult, OP.add, ["hold", "HB"], ["HS"])
+        scan(T.HS[:, 0:128], T.hold[:], T.HB[:, 0:128], 0.0, OP.mult, OP.add, ["hold", "HB"], ["HS"])
         mm(T.TG[:, 8, 0:8], T.HB[:, 1:129], T.dp[:], False, False, ["HB", "dp"], ["TG"])
         mm(T.TG[:, 8, 0:8], T.HS[:, 0:128], T.dp[:], False, False, ["HS", "dp"], ["TG"])
         mm(T.TG[:, 8, 0:8], T.HS[:, 1:129], T.dn[:], False, True, ["HS", "dn"], ["TG"])
         cp(T.J[:], T.TG[:, 8, 0:8], ["TG"], ["J"])
         send(1, t, "J", JB)
         cp(T.M[:], T.xg[:, 0:4096].indirect(T.J[:, 0:8]), allkeys("xg") + ["J"], ["M"])
-        tt(T.ge[:], T.xg[:, 0:4096].indirect(T.J[:, 0:8]), T.Z[:], OP.is_le, allkeys("xg") + ["J", "Z"], ["ge"])
-        tt(T.h1[:, 0:128], T.X[:, 0:8192].indirect(T.offX[:, 0:8]), T.M[:], OP.add, XK + ["offX", "M"], ["h1.0"])
+        tt(T.ge[:], T.xg[:, 0:4096].indirect(T.J[:, 0:8]), T.ZC[:], OP.is_ge, allkeys("xg") + ["J", "ZC"], ["ge"])
+        tt(T.h1[:, 0:128], T.X[:, 0:8192].indirect(T.offX[:, 0:8]), T.M[:], OP.subtract, XK + ["offX", "M"], ["h1.0"])
         for j in (2, 1, 0):
             mm(YB[j][:], T.M[:], T.WR[:, 16 * j:16 * j + 16, :], False, True, ["M", "WR"], ["Y%d" % j])
             if j == 2:
                 mm(part("TG", 0, 128), T.B16[:], T.ge[:], True, True, ["ge", "B16"], ["TG"])
         act(T.cY[:, 1024:1536], T.Y2[:], AF.Copy, ["Y2"], ["cY.2"])
-        ts(T.h2[:, 0:128], T.h1[:, 0:128], 1, None, OP.arith_shift_right, None, ["h1.0"], ["h2.0"])
-        if t > 0:
-            tt(T.xd[:], T.X[:, 0:8192].indirect(T.offX[:, 0:8]), T.h2[:, 0:128], OP.subtract, XK + ["offX", "h2.0"], ["xd"])
-        patch(t, 0)
         cp(T.cY[:, 512:1024], T.Y1[:], ["Y1"], ["cY.1"])
         act(T.fr[:], part("TG", 0, 128), AF.Relu, ["TG"], ["fr"], bias=-6.0)
         act(T.cY[:, 0:512], T.Y0[:], AF.Copy, ["Y0"], ["cY.0"])
@@ -620,114 +633,127 @@ def rank_program(g, core, T, topo):
         sign_marks("OB", 256, LB)
         sign_levels("OB", 256, "cY", 2, False)
         sign_whole("OB", 256, "fr")
+        ts(T.h2[:, 0:128], T.h1[:, 0:128], 0.5, 127.25, OP.mult, OP.add, ["h1.0"], ["h2.0"])
+        cp(T.y0[:], T.yg[:, 0:4096].indirect(T[JB][:, 0:8]), allkeys("yg") + [JB], ["y0"])
         sign_levels("OB", 256, "cY", 1, False)
-        blocks("Y1", 0, [("LTt", "LM", LS, "-1")], False, True)
+        for j in (1, 2, 0):
+            mm(XB[j][:], T.y0[:], T.WR[:, 16 * j:16 * j + 16, :], j > 0, True, ["y0", "WR"], ["X%d" % j])
+            if j == 1:
+                sign_levels("OB", 256, "cY", 0, True)
+        if t > 0:
+            tt(T.xd[:], T.X[:, 0:8192].indirect(T.offX[:, 0:8]), T.h2[:, 0:128], OP.subtract, XK + ["offX", "h2.0"], ["xd"])
+        early(0)
+        act(T.KB[:], part("OB", 256, 256), AF.Sign, ["OB"], ["KB"], bias=-2.0 ** -70)
+        act(T.cA[:, 0:512], T.X0[:], AF.Copy, ["X0"], ["cA.0"])
+        act(T.s2[:], part("OB", 256, 256), AF.Sign, ["OB"], ["s2"], bias=BIG1 / 2)
         mm(part("Y2", 256, 128), ident("-64"), T.fr[:], True, False, ["ID.-64", "fr"], ["Y2"])
         for h in range(2):
             mm(part("Y2", 256, 128), T.OT[:, h, :], half("LTt", h), False, h == 1, ["OT", "LTt"], ["Y2"])
-        patch(t, 1)
-        ts(T.y0[:], T.yg[:, 0:4096].indirect(T[JB][:, 0:8]), E_, None, OP.add, None, allkeys("yg") + [JB, "pe"], ["y0"])
-        sign_levels("OB", 256, "cY", 0, True)
-        for j in (1, 2, 0):
-            mm(XB[j][:], T.y0[:], T.WR[:, 16 * j:16 * j + 16, :], j > 0, True, ["y0", "WR"], ["X%d" % j])
-        patch(t, 2)
-        patch(t, 3)
-        ts(T.KB[:], part("OB", 256, 256), 0.0, None, OP.is_le, None, ["OB"], ["KB"])
         act(T.mm[:], part("Y2", 256, 128), AF.Relu, ["Y2"], ["mm"], bias=32.0)
-        act(T.s2[:], part("OB", 256, 256), AF.Sign, ["OB"], ["s2"], bias=BIG1 / 2)
-        act(T.cA[:, 0:512], T.X0[:], AF.Copy, ["X0"], ["cA.0"])
         sign_marks("Y0", 0, "LT")
-        blocks("Y1", 0, [("KB", "OM", OS, "1"), ("s2", "OM", OS, "1/2")], True)
         sign_whole("Y0", 0, "nf")
         for j in (1, 2):
             tt(T.cA[:, 512 * j:512 * j + 512], XB[j][:], T.NV[:, 512 * j:512 * j + 512], OP.add, ["X%d" % j, "NV.%d" % j, "NV.%d" % (j + 3)], ["cA.%d" % j])
-            patch(t, 3 + j)
-        sign_levels("Y0", 0, "cA", 1, False)
-        sign_levels("Y0", 0, "cA", 0, False)
-        sign_levels("Y0", 0, "cA", 2, True)
-        mm(part("X1", 0, 256), T.mm[:], T.BD[:, 0, :, :], True, False, ["mm", "BD.-1/16"], ["X1"])
-        blocks("X1", 0, [("KB", "LM", LS, "1")], False)
-        tt(T.DA[:], part("Y1", 0, 256), T.rows[:, 0, :], OP.add, ["Y1", "rows"], ["DA"])
-        for s in (5, 4):
-            quot("A", s, 0, T.DA[:], "DA")
+            early(j)
+        for j in (1, 2, 0):
+            sign_levels("Y0", 0, "cA", j, j == 0)
+        blocks("X1", 0, [("KB", "LM", LS, "got")], False, True)
         if not last:
-            cp(T.X[:, 0:8192].indirect(T.offX[:, 0:8]), T.h2[:, 0:128], ["h2.0", "offX"], XK)
-        patch(t, 6)
-        patch(t, 7)
+            cp(T.X[:, 0:8192].indirect(T.offX[:, 0:8]), T.h2[:, 0:128], ["h2.0", "offX", "xd"], XK)
+        early(3)
+        early(4)
+        ts(T.KA[:], part("Y0", 0, 256), 0.0, -2.0, OP.is_gt, OP.mult, ["Y0"], ["KA"])
+        early(5)
+        blocks("Y1", 0, [("LTt", "LM", LS, "own"), ("KB", "OM", OS, "-1/2"), ("s2", "OM", OS, "1/2")], True, True)
+        mm(part("X1", 0, 256), T.mm[:], T.BD[:, 0, :, :], False, False, ["mm", "BD.-1/16"], ["X1"])
+        blocks("X1", 0, [("KA", "OM", OS, "1/2")], True)
+        tt(T.DA[:], part("Y1", 0, 256), T.rows[:, 0, :], OP.add, ["Y1", "rows"], ["DA"])
+        for s in (5, 4, 3):
+            quot("A", s, 0, "DA")
+        mm(part("Y2", 0, 256), T.ones[:], T.CT[:], True, False, ["ones", "CT.c"], ["Y2"])
+        ts(T.DB[:], part("X1", 0, 256), 63.5, None, OP.add, None, ["X1"], ["DB"])
+        early(6)
+        mm(part("X0", 0, 256), T.ones[:], T.CT[:], True, False, ["ones", "CT.c"], ["X0"])
+        blocks("X0", 0, [("KA", "ID", IDS, "-1/128")], False)
+        for s in range(1, 6):
+            quot("V", s, 1, "DB")
+        early(7)
         if last:
             dma("S", T.yx[:], T.S[:], ["S.0", "S.1"], [])
-        ts(T.KA[:], part("Y0", 0, 256), 0.0, None, OP.is_le, None, ["Y0"], ["KA"])
-        mm(part("TG", 0, 256), T.ones[:, 0:128], T.CT[:], True, False, ["ones", "CT"], ["TG"])
-        blocks("X1", 0, [("KA", "OM", OS, "1")], True)
-        quot("V", 1, 0, T.DA[:], "DA")
-        tt(T.DB[:], part("X1", 0, 256), T.rows[:, 1, :], OP.add, ["X1", "rows"], ["DB"])
-        for s in (2, 3):
-            quot("V", s, 0, T.DA[:], "DA")
-        for s in (5, 4):
-            quot("A", s, 1, T.DB[:], "DB")
-        mm(part("TG", 0, 256), ident("1/2"), T.DA[:], False, False, ["ID.1/2", "DA"], ["TG"])
-        blocks("TG", 0, [("KA", "ID", IDS, "-2/128")], False)
-        for s in (5, 1, 4):
-            quot_add("TG", s, 0)
-        mm(part("Y2", 0, 256), T.ones[:, 0:128], T.CT[:], True, False, ["ones", "CT"], ["Y2"])
-        for s in (2, 3):
-            quot_add("TG", s, 0, s == 3)
-        for s in (1, 2, 3):
-            quot("V", s, 1, T.DB[:], "DB")
-        blocks("Y2", 0, [("KB", "ID", IDS, "-2/128")], False)
+        for s in (1, 2):
+            quot("V", s, 0, "DA")
         mm(part("Y2", 0, 256), ident("1/2"), T.DB[:], False, False, ["ID.1/2", "DB"], ["Y2"])
-        for s in (1, 5, 2, 3, 4):
-            quot_add("Y2", s, 1, s == 4)
-        start_row("X2", "len")
-        blocks("X2", 0, [("KB", "OM", OS, "1"), ("KA", "OM", OS, "1")], True)
+        for s in range(1, 6):
+            quot_add("Y2", s, 1, s == 5)
+        mm(part("X0", 0, 256), ident("1/2"), T.DA[:], False, False, ["ID.1/2", "DA"], ["X0"])
+        for s in (5, 4, 1, 2, 3):
+            quot_add("X0", s, 0, s == 3)
+        if t == 0:
+            fill_names(0)
+            late_constants(3)
+            fill_names(1)
         mm(part("Y0", 256, 128), ident("1"), T.y0[:], True, False, ["ID.1", "y0"], ["Y0"])
-        mm(part("Y0", 256, 128), ident("-1"), T.Z[:], False, True, ["ID.-1", "Z"], ["Y0"])
+        mm(part("Y0", 256, 128), ident("1"), T.Z[:], False, True, ["ID.1", "Z"], ["Y0"])
+        mm(part("X2", 0, 256), T.ones[0:1, :], T.rows[0:1, 1, :], True, False, ["ones", "rows"], ["X2"])
+        blocks("X2", 0, [("KB", "OM", OS, "-1/2"), ("KA", "OM", OS, "1/2")], True)
         if not last:
-            act(T.Z[:], part("Y0", 256, 128), AF.Abs, ["Y0", "pn"], ["Z"], bias=NE_)
+            act(T.Z[:], part("Y0", 256, 128), AF.Abs, ["Y0"], ["Z"], bias=-255.0)
         act(T.nr[:], part("X2", 0, 256), AF.Relu, ["X2"], ["nr"])
         if not last:
+            sums(2 * t, "X1")
             mm(T.Y0[:, 12, 0:1], T.onesf[:], T.rs[:, 0:1], True, True, ["onesf", "rs"], ["Y0"])
             act(T.kc[:, 0:1], T.Y0[:, 12, 0:1], AF.Identity, ["Y0"], ["kc"], bias=4096.0 * 33 - 2.0 ** 23)
         else:
-            act(T.zd[:], part("Y0", 256, 128), AF.Abs, ["Y0", "pn"], ["zd"], bias=NE_)
+            act(T.zd[:], part("Y0", 256, 128), AF.Abs, ["Y0"], ["zd"], bias=-255.0)
             dma("S", T.yz[:], T.zd[:], ["zd"], [])
-        for h, src, bk in ((0, "VA", "TG"), (1, VB, "Y2")):
-            tt(T.E0[:, 8 * h:8 * h + 8, :], T[bk][:, 0:8, 0::2], T[src][:, :, 0::2], OP.add, [bk, src], ["E0"])
-            tt(T.Y1[:, 8 * h:8 * h + 8, 0:16], T[bk][:, 0:8, 1::2], T[src][:, :, 1::2], OP.add, [bk, src], ["Y1"])
+        for h, src, R, even, odd, bk in ((1, VB, [VB], T.Y2[:, 0:8, 0::2], T.Y2[:, 0:8, 1::2], "Y2"),
+                                         (0, "VA", VK, T.X0[:, 0:256:2], T.X0[:, 1:256:2], "X0")):
+            tt(T.E0[:, 8 * h:8 * h + 8, :], even, T[src][:, :, 0::2], OP.add, [bk] + R, ["E0.%d" % h])
+            tt(T.Y1[:, 8 * h:8 * h + 8, 0:16], odd, T[src][:, :, 1::2], OP.add, [bk] + R, ["Y1.%d" % h])
+            late(1 - h)
+            for s in range(APART):
+                stage(s, [h])
         fill = T.Y2[:, 8:16, :]
-        mm(fill, T.ones[0:1, 0:128], T.topf[0:1, :], True, False, ["ones", "topf"], ["Y2"])
+        mm(fill, T.ones[0:1, :], T.topf[0:1, :], True, False, ["ones", "topf"], ["Y2"])
         for e in range(2):
             mm(T.Y2[:, 8:16, e::2], T.fbf[:, 128 * e:128 * e + 128], T.IDN[:], False, False, ["fbf", "IDN"], ["Y2"])
         if not last:
             make_u(0)
-            sums(2 * t)
-            make_u(1)
+            keep_sums(2 * t, "X1")
         for e in range(2):
             mm(T.Y2[:, 8:16, e::2], T.gf[:, 128 * e:128 * e + 128], ident("-1/128"), False, False, ["gf", "ID.-1/128"], ["Y2"])
         mm(fill, ident("1"), T.nr[:], False, True, ["ID.1", "nr"], ["Y2"])
         if not last:
+            make_u(1)
+            sums(2 * t + 1, "X0")
+            keep_sums(2 * t + 1, "X0")
             turn_init(OWN, 0)
-            sums(2 * t + 1)
         for s in range(4):
-            ei, eo = ("E0", "E1") if s % 2 == 0 else ("E1", "E0")
-            ki, ko = ("Y1", "TG") if s % 2 == 0 else ("TG", "Y1")
-            for hi, alu in ((0, OP.min), (1, OP.max)):
-                for par in range(2):
-                    o, ok = (T[eo], eo) if par == 0 else (T[ko], ko)
-                    tt(o[:, :, 8 * hi:8 * hi + 8], T[ei][:, :, par::2], T[ki][:, :, par:16:2], alu, [ei, ki], [ok])
+            if s >= APART:
+                for hs in LISTS:
+                    stage(s, hs)
+            late(2 + s)
         for hi, alu in ((0, OP.min), (1, OP.max)):
-            tt(T.AP[:, :, 16 * hi:16 * hi + 16], T.E0[:, 0:8, :], T.Y1[:, 0:8, 0:16], alu, ["E0", "Y1"], ["AP"])
-            tt(T.TG[:, 0:8, 16 * hi:16 * hi + 16], T.E0[:, 8:16, :], T.Y1[:, 8:16, 0:16], alu, ["E0", "Y1"], ["TG"])
-        tt(T.v1[:], T.AP[:], T.TG[:, 0:8, :], OP.min, ["AP", "TG"], ["v1"])
+            tt(T.AP[:, :, 16 * hi:16 * hi + 16], T.E0[:, 0:8, :], T.Y1[:, 0:8, 0:16], alu, ["E0.0", "Y1.0"], ["AP"])
+            tt(T.TG[:, 0:8, 16 * hi:16 * hi + 16], T.E0[:, 8:16, :], T.Y1[:, 8:16, 0:16], alu, ["E0.1", "Y1.1"], ["TG"])
+        late(6)
         if not last:
-            tt(T.VA[:], T.v1[:], fill, OP.min, ["v1", "Y2"], ["VA"])
-            send(0, t + 1, "VA", "VB%d" % (t + 1))
+            for e in (1, 0):
+                tt(T.v1[:, :, e::2], T.AP[:, :, e::2], T.TG[:, 0:8, e::2], OP.min, ["AP", "TG"], ["v1.%d" % e])
+            late(7)
+            for e in (1, 0):
+                tt(T.VA[:, :, e::2], T.v1[:, :, e::2], T.Y2[:, 8:16, e::2], OP.min, ["v1.%d" % e, "Y2"], ["VA.%d" % e])
+            send(0, t + 1, "VA", "VB%d" % (t + 1), VK)
             turn_own()
         else:
             for b in range(2):
-                mm(part("OB", 256 + 128 * b, 128), T.TP[:, 4 + b, :], T.ones[:, 0:128], b == 0, False, ["TP.a%d" % (4 + b), "TP.b%d" % (4 + b)], ["OB"])
+                mm(part("OB", 256 + 128 * b, 128), T.TP[:, 4 + b, :], T.ones[:], b == 0, False, ["TP.c", "TP.%d" % (4 + b)], ["OB"])
             for b in range(2):
-                tt(T.VL[:, 128 * b:128 * b + 128], T.v1[:, :, 16 * b:16 * b + 16], T.Y2[:, 8:16, 16 * b:16 * b + 16], OP.min, ["v1", "Y2"], ["VL.%d" % b])
+                c = slice(16 * b, 16 * b + 16)
+                tt(T.v1[:, :, c], T.AP[:, :, c], T.TG[:, 0:8, c], OP.min, ["AP", "TG"], ["v1.%d" % b])
+            for b in range(2):
+                c = slice(16 * b, 16 * b + 16)
+                tt(T.VL[:, 128 * b:128 * b + 128], T.v1[:, :, c], T.Y2[:, 8:16, c], OP.min, ["v1.%d" % b, "Y2"], ["VL.%d" % b])
                 mm(part("OB", 256 + 128 * b, 128), T.VL[:, 128 * b:128 * b + 128], T.IU[:], False, b == 1, ["VL.%d" % b, "IU"], ["OB"])
             cp(T.amf[:], part("OB", 256, 256), ["OB"], ["amf"])
             dma("S", T.ya[:], T.amf[:], ["amf"], [])

@@ -12,8 +12,6 @@ UP = 2.0 ** 20
 MAGIC = 1.5 * 2.0 ** 23
 SPLIT = (64, 56)
 NENG = 8
-APART = 1
-LISTS = [[1], [0]]
 
 F, B, I, U = "float32", "bfloat16", "int32", "uint16"
 
@@ -33,7 +31,7 @@ TOPS = [(0, -4096.0), (1, -4096.0), (0, 32.0), (1, 32.0), (0, 0.0), (1, 0.0)]
 SCRATCH = {
     "X": _s([8192], B), "xg": _s([4096], B), "yg": _s([4096], B), "S": _s([2048], F),
     "ami": _s([256], I), "amf": _s([256], F), "Z": _s([128], B), "ZC": _s([128], B), "wi": _s([8], I), "wf": _s([8], F),
-    "VA": _s([8, 32], F), "VL": _s([256], F), "VB0": _s([8, 32], F), "VB1": _s([8, 32], F), "VB2": _s([8, 32], F),
+    "VA": _s([2, 128], F), "VL": _s([256], F), "VB0": _s([2, 128], F), "VB1": _s([2, 128], F), "VB2": _s([2, 128], F),
     "LT": _s([256], B), "LB0": _s([256], B), "LB1": _s([256], B), "LB2": _s([256], B),
     "J": _s([8], U), "JB0": _s([8], U), "JB1": _s([8], U), "JB2": _s([8], U),
     "h1": _s([256], I), "h2": _s([256], I), "offA": _s([256], U), "offB": _s([256], U),
@@ -44,7 +42,7 @@ SCRATCH = {
     "KF": _s([256], F), "HB": _s([136], F), "HS": _s([136], F), "hold": _s([128], F), "inc": _s([256], F),
     "M": _s([128], B), "y0": _s([128], B), "ge": _s([128], B),
     "fr": _s([128], B), "nf": _s([128], B), "mm": _s([128], B), "LTt": _s([256], B), "KA": _s([256], B), "KB": _s([256], B), "s2": _s([256], B),
-    "sl": _s([8], F), "offS": _s([8], U), "xd": _s([128], F), "xp": _s([128], F),
+    "sl": _s([8], F), "offS": _s([8], U), "xs": _s([128], B), "xh": _s([128], I), "xd": _s([128], F), "BP": _s([8, 32], F), "xp": _s([128], F),
     "cA": _s([1536], B), "cY": _s([1536], B), "DA": _s([256], B), "DB": _s([256], B), "nr": _s([256], B),
     "G1": _s([512], B), "G2": _s([512], B), "G3": _s([512], B), "G4": _s([512], B), "G5": _s([512], B),
     "E0": _s([16, 16], F), "E1": _s([16, 16], F), "AP": _s([8, 32], F), "v1": _s([8, 32], F),
@@ -61,7 +59,7 @@ SCRATCH = {
     "TG": ("psum", [128, 16, 32], F), "OB": ("psum", [128, 512], F),
 }
 PSUM = ("X0", "X1", "X2", "Y0", "Y1", "Y2", "TG", "OB")
-SEMAPHORES = ["eV", "eA", "eP", "eG"] + ["d%d" % k for k in range(16)] + ["l%d" % k for k in range(9)] + ["a%d" % k for k in range(9)]
+SEMAPHORES = ["eV", "eA", "eP", "eG"] + ["d%d" % k for k in range(16)] + ["l%d" % k for k in range(12)] + ["a%d" % k for k in range(12)]
 
 
 def make_plan():
@@ -203,19 +201,20 @@ def rank_program(g, core, T, topo):
     def select(o, x, pat, alu, fill, base, ch, R, W):
         op("G", lambda: g.affine_select(o, x, pat, alu, fill, base, ch), R, W)
 
-    def send(k, t, src, dst, R=None):
+    def send(k, t, src, dst, R, W):
         to = T.cores[(rank + 1 + t % (N - 1)) % N]
         fr = T.cores[(rank - 1 - t % (N - 1)) % N]
         eng = topo.engines(core, to)[:NENG]
         mask = sum(1 << e for e in eng)
         rid, pid = topo.addr(to)[:2]
-        n = 3 * t + k
-        op("G", lambda: g.remote_dma(T[dst][:], T[src][:], T.sem["a%d" % n], T.sem["l%d" % n], pid, rid, mask),
-           R or [src], [], sem="l%d" % n, inc=len(eng))
-        op("G", None, [], [dst], sem="a%d" % n, inc=len(topo.engines(fr, core)[:NENG]))
+        n = 4 * t + k
+        op("G", lambda: g.remote_dma(dst, src, T.sem["a%d" % n], T.sem["l%d" % n], pid, rid, mask), R, [], sem="l%d" % n, inc=len(eng))
+        op("G", None, [], W, sem="a%d" % n, inc=len(topo.engines(fr, core)[:NENG]))
+
+    def send_names(t, e):
+        send(e, t, T.VA[:, e, :], T["VB%d" % t][:, e, :], ["VA.%d" % e], ["VB%d.%d" % (t, e)])
 
     XB, YB = [T.X0, T.X1, T.X2], [T.Y0, T.Y1, T.Y2]
-    VK = ["VA.0", "VA.1"]
 
     def lev(l):
         return XB[l % 3][:, (l // 3) * 256:(l // 3) * 256 + 256]
@@ -233,6 +232,12 @@ def rank_program(g, core, T, topo):
 
     def half(name, h):
         return T[name][:, 128 * h:128 * h + 128]
+
+    def quarter(name, h):
+        return T[name][:, 64 * h:64 * h + 64]
+
+    def four(name):
+        return ["%s%d" % (name, h) for h in range(4)]
 
     dma("S", T.ami[:], T.am[:], [], ["ami"])
     dma("A", T.Z[:], T.zv[:], [], ["Z"])
@@ -293,9 +298,11 @@ def rank_program(g, core, T, topo):
         mm(T.TG[:, 0:8, 16 * b:16 * b + 16], T.amf[:, 128 * b:128 * b + 128], T.IDN[:], False, b == 1, ["amf", "IDN"], ["TG"])
     ms(T.TP[64:65, 2:4, :], 32.0, ["TP.c"])
     ms(T.WZ[:], 0.0, ["WZ"])
-    cp(T.VA[:], T.TG[:, 0:8, :], ["TG"], VK)
+    for e in (1, 0):
+        cp(T.VA[:, e, :], T.TG[:, 0:8, e::2], ["TG"], ["VA.%d" % e])
     ts(T.WZ[:, 16::16], T.io1[:], G_, T.wf[:, 0:1], OP.is_equal, OP.mult, ["io1", "pf", "wf", "WZ"], ["WZ"])
-    send(0, 0, "VA", "VB0", VK)
+    for e in (1, 0):
+        send_names(0, e)
     key_weights([13, 2, 5, 8, 11, 14])
     WK = ["W.%d" % l for l in range(6)]
 
@@ -340,19 +347,19 @@ def rank_program(g, core, T, topo):
     def turn(where, src, es=(1, 0)):
         for e in es:
             bk, c0 = where[e]
-            mm(part(bk, c0, 128), T[src][:, :, e::2], T.IU[:], False, True, ["VA.%d" % e if src == "VA" else src, "IU"], [bk])
+            mm(part(bk, c0, 128), T[src][:, e, :], T.IU[:], False, True, ["%s.%d" % (src, e), "IU"], [bk])
 
-    def hash_step(where, off, step, e):
+    def hash_step(where, off, step, e, q):
         bk, c0 = where[e]
-        c = slice(128 * e, 128 * e + 128)
+        c, ln, key = slice(128 * e + 64 * q, 128 * e + 64 * q + 64), slice(64 * q, 64 * q + 64), "%d%d" % (e, q)
         if step == 0:
-            tt(part(bk, c0, 128), part(bk, c0, 128), T.cm[:], OP.mult, [bk, "cm"], [bk])
+            tt(part(bk, c0 + 64 * q, 64), part(bk, c0 + 64 * q, 64), T.cm[:, ln], OP.mult, [bk, "cm"], [bk + ".p" + key])
         if step == 1:
-            tt(T.h1[:, c], part(bk, c0, 128), T.Dm[:], OP.add, [bk, "Dm"], ["h1.%d" % e])
+            tt(T.h1[:, c], part(bk, c0 + 64 * q, 64), T.Dm[:, ln], OP.add, [bk + ".p" + key, "Dm"], ["h1." + key])
         if step == 2:
-            ts(T.h2[:, c], T.h1[:, c], 5, 8191, OP.arith_shift_right, OP.bitwise_and, ["h1.%d" % e], ["h2.%d" % e])
+            ts(T.h2[:, c], T.h1[:, c], 5, 8191, OP.arith_shift_right, OP.bitwise_and, ["h1." + key], ["h2." + key])
         if step == 3:
-            cp(T[off][:, c], T.h2[:, c], ["h2.%d" % e], ["%s.%d" % (off, e)])
+            cp(T[off][:, c], T.h2[:, c], ["h2." + key], ["%s.%s" % (off, key)])
 
     def fill_product(e):
         tt(T.ft[:, 128 * e:128 * e + 128], part("Y2", 128 * e, 128), T.u32[:], OP.mult, ["Y2", "u32"], ["ft"])
@@ -365,16 +372,17 @@ def rank_program(g, core, T, topo):
         make_u(2)
         for step in range(4):
             for e in (1, 0):
-                hash_step(OWN, "offA", step, e)
+                for q in (1, 0):
+                    hash_step(OWN, "offA", step, e, q)
 
     def gather(eng, dst, off, e, i0, i1):
         c0, c1 = 128 * e + i0, 128 * e + i1
         o, x = T[dst][:, 16 * c0:16 * c1], T.X[:, 0:8192].indirect(T[off][:, c0:c1])
-        key = "%s.%d%s" % (dst, e, eng)
+        key, R = "%s.%d%s" % (dst, e, eng), XK + ["%s.%d%d" % (off, e, q) for q in range(i0 // 64, (i1 - 1) // 64 + 1)]
         if eng == "V":
-            ts(o, x, -1.0, 255.0, OP.mult, OP.add, XK + ["%s.%d" % (off, e)], [key])
+            ts(o, x, -1.0, 255.0, OP.mult, OP.add, R, [key])
         else:
-            act(o, x, AF.Identity, XK + ["%s.%d" % (off, e)], [key], bias=255.0, scale=-1.0)
+            act(o, x, AF.Identity, R, [key], bias=255.0, scale=-1.0)
 
     def allkeys(dst):
         return ["%s.%d%s" % (dst, e, q) for e in range(2) for q in "VA"]
@@ -393,7 +401,7 @@ def rank_program(g, core, T, topo):
 
     def sign_marks(bk, c0, marks):
         for h in range(2):
-            mm(part(bk, c0 + 128 * h, 128), half(marks, h), ident("big"), h == 0, False, [marks, "ID.big"], [bk])
+            mm(part(bk, c0 + 128 * h, 128), half(marks, h), ident("big"), h == 0, False, [marks, "ID.big"] + four(marks + "."), [bk])
 
     def sign_whole(bk, c0, flag):
         for h in range(2):
@@ -415,8 +423,8 @@ def rank_program(g, core, T, topo):
     for s in range(4):
         act(T.WR[:, :, 2 ** s:2 ** (s + 1)], T.WR[:, :, 0:2 ** s], AF.Copy, ["WR"], ["WR"])
     ms(T.r0[:], 0.0, ["r0"])
-    ms(T.w[:, 255:256], HUGE, ["w"])
-    ms(T.OB[:, 255:256], HUGE, ["OB"])
+    ms(T.w[:, 63::64], HUGE, four("w."))
+    ms(T.OB[:, 63:256:64], HUGE, four("OB.w"))
     ms(T.r0[:, 31::32], HUGE, ["r0"], ["r0"])
     fill0 = -131072.0 - 31.0 / 64
     ts(T.pf[:, 8:9], P_, 74.0, fill0, OP.mult, OP.add, ["pf"], ["pf8"])
@@ -480,19 +488,15 @@ def rank_program(g, core, T, topo):
             mm(T[bk][:], ident("1"), T.X[:, 2048 * q + 512 * j:2048 * q + 512 * j + 512], q == 0, q == 3, ["ID.1"] + XK, [bk])
 
     def keep_sums(j, bk):
-        act(T.S[:, 512 * j:512 * j + 512], T[bk][:], AF.Copy, [bk], ["S.%d" % (j // 2)])
+        act(T.S[:, 512 * j:512 * j + 512], T[bk][:], AF.Copy, [bk], ["S"])
 
-    def patch(t, k):
-        if t == 0:
-            return
-        q, n = k // 2, t
-        win = T.S[:, 0:1024 * n].indirect(T.offS[:, 2 * q:2 * q + n])
-        c = slice(32 * q, 32 * q + 16 * n)
-        SK = ["S.%d" % j for j in range(n)]
+    def patch(k):
+        q = k // 2
+        win, c = T.S[:, 0:2048].indirect(T.offS[:, 2 * q:2 * q + 2]), slice(32 * q, 32 * q + 32)
         if k % 2 == 0:
-            tt(T.xp[:, c], win, T.xd[:, c], OP.subtract, SK + ["offS", "xd"], ["xp"])
+            tt(T.xp[:, c], win, T.xd[:, c], OP.subtract, ["S", "offS", "xd"], ["xp"])
         else:
-            cp(win, T.xp[:, c], ["xp", "offS"], SK)
+            cp(win, T.xp[:, c], ["xp", "offS"], ["S"])
 
     def quot(eng, s, h, src):
         o, off = T["G%d" % s][:, 256 * h:256 * h + 256], 192.0 - 0.5 + 2.0 ** -(s + 1)
@@ -504,15 +508,15 @@ def rank_program(g, core, T, topo):
     def quot_add(bk, s, h, stop=False):
         mm(part(bk, 0, 256), ident("g%d" % s), T["G%d" % s][:, 256 * h:256 * h + 256], False, stop, ["ID.g%d" % s, "G%d.%d" % (s, h)], [bk])
 
-    def stage(s, hs):
+    def stage(s, h):
         ei, eo = ("E0", "E1") if s % 2 == 0 else ("E1", "E0")
         ki, ko = ("Y1", "TG") if s % 2 == 0 else ("TG", "Y1")
-        c = slice(8 * hs[0], 8 * hs[-1] + 8)
+        c = slice(8 * h, 8 * h + 8)
         for hi, alu in ((0, OP.min), (1, OP.max)):
             for par in range(2):
                 ok = eo if par == 0 else ko
                 tt(T[ok][:, c, 8 * hi:8 * hi + 8], T[ei][:, c, par::2], T[ki][:, c, par:16:2], alu,
-                   ["%s.%d" % (x, h) for x in (ei, ki) for h in hs], ["%s.%d" % (ok, h) for h in hs])
+                   ["%s.%d" % (ei, h), "%s.%d" % (ki, h)], ["%s.%d" % (ok, h)])
 
     for t in range(RO):
         last = t == RO - 1
@@ -520,28 +524,34 @@ def rank_program(g, core, T, topo):
 
         def early(k):
             if last:
-                patch(t, k)
-
-        def late(k):
-            if not last:
-                patch(t, k)
+                patch(k)
         s1, s0 = SPLIT
         gather("A", "xg", "offA", 1, s1, 128)
         gather("A", "xg", "offA", 0, s0, 128)
         turn_init(GOT, 0)
-        turn(GOT, VB)
+        columns(0)
+        if last:
+            sums(2, "Y1")
+            keep_sums(2, "Y1")
+        turn(GOT, VB, (1,))
         gather("V", "xg", "offA", 1, 0, s1)
-        gather("V", "xg", "offA", 0, 0, s0)
-        for step, other in enumerate((lambda: fill_product(0), lambda: fill_product(1), lambda: columns(0), None)):
-            hash_step(GOT, "offB", step, 1)
-            if other:
-                other()
-        spare = [lambda k=k: hash_step(GOT, "offB", k, 0) for k in range(4)]
+        turn(GOT, VB, (0,))
+        cuts = [0, 16, 32, s0]
+        for step in range(6):
+            for e, k in ((1, step), (0, step - 2)):
+                if 0 <= k < 4:
+                    for q in range(2):
+                        hash_step(GOT, "offB", k, e, q)
+            if step < 3:
+                gather("V", "xg", "offA", 0, cuts[step], cuts[step + 1])
+            elif step < 5:
+                fill_product(step - 3)
+        spare = [lambda: columns(1)]
         if t == 0:
             spare += [lambda: [f() for f in first_spare[0:2]], first_spare[2]]
-        spare += [lambda k=k: columns(k) for k in range(1, 6 if t > 0 else 4)]
+        spare += [lambda k=k: columns(k) for k in range(2, 6 if last else 4)]
         if t == 0:
-            spare += [lambda: [f() for f in first_spare[3:5]], lambda: [f() for f in first_spare[5:]]]
+            spare += first_spare[3:]
         gather("A", "yg", "offB", 1, 0, 128)
         for j in range(3):
             keys("xg", "X", 1, j)
@@ -551,14 +561,15 @@ def rank_program(g, core, T, topo):
         keys("xg", "X", 0, 1)
         r = "r0"
         for l in range(6):
-            if l < 3:
-                kx, kw = "X%d" % l, "w"
-                nv, w = lev(l), T.w[:]
-                scan(T.w[:, 254::-1], XB[l][:, 255:0:-1], T[r][:, 254::-1], HUGE, OP.min, OP.max, [kx, r], [kw])
-            else:
-                c0, kx, kw = 512 * (l - 3) + 256, "NV.%d" % l, "OB"
-                nv, w = T.NV[:, c0:c0 + 256], T.OB[:, 0:256]
-                scan(T.OB[:, 254::-1], T.NV[:, c0 + 255:c0:-1], T[r][:, 254::-1], HUGE, OP.min, OP.max, [kx, r], [kw])
+            src, c0, wb = (XB[l], 0, T.w) if l < 3 else (T.NV, 512 * (l - 3) + 256, T.OB)
+            kx = ["X%d" % l] * 4 if l < 3 else ["NV.%d%d" % (l, h) for h in range(4)]
+            kw = ["w.%d" % h if l < 3 else "OB.w%d" % h for h in range(4)]
+            nv = [src[:, c0 + 64 * h:c0 + 64 * h + 64] for h in range(4)]
+            w = [wb[:, 64 * h:64 * h + 64] for h in range(4)]
+            for h in range(4):
+                back = slice(64 * h + 62, 64 * h - 1 if h else None, -1)
+                scan(wb[:, back], src[:, c0 + 64 * h + 63:c0 + 64 * h:-1], T[r][:, back], HUGE, OP.min, OP.max,
+                     [kx[h], r if l == 0 else "%s.%d" % (r, h)], [kw[h]])
             if spare:
                 spare.pop(0)()
             if l == 2:
@@ -566,18 +577,24 @@ def rank_program(g, core, T, topo):
             if l == 3 and t == 0:
                 late_constants(1)
             if l < 5:
-                tt(T.lt[:], nv, w, OP.is_gt, [kx, kw], ["lt"])
-                if l < 2:
-                    mm(lev(l + 1), ident("big"), T.lt[:], False, True, ["ID.big", "lt"], ["X%d" % (l + 1)])
+                for h in range(4):
+                    tt(quarter("lt", h), nv[h], w[h], OP.is_gt, [kx[h], kw[h]], ["lt.%d" % h])
+                    if l < 2 and h % 2:
+                        mm(XB[l + 1][:, 64 * h - 64:64 * h + 64], ident("big"), half("lt", h // 2), False, h == 3,
+                           ["ID.big", "lt.%d" % (h - 1), "lt.%d" % h], ["X%d" % (l + 1)])
                 if l == 0:
                     keys("xg", "X", 0, 2)
                 if l == 2:
                     for j in range(3):
                         keys("yg", "Y", 1, j)
                 r = "rA" if l % 2 == 0 else "rB"
-                tt(T[r][:], w, nv, OP.subtract, [kx, kw], [r])
+                for h in range(4):
+                    tt(quarter(r, h), w[h], nv[h], OP.subtract, [kx[h], kw[h]], ["%s.%d" % (r, h)])
                 if l >= 2:
-                    tt(T.NV[:, 512 * (l - 2) + 256:512 * (l - 2) + 512], lev(l + 1), T.lt[:], OP.add, ["X%d" % (l - 2), "lt"], ["NV.%d" % (l + 1)])
+                    for h in range(4):
+                        c1 = 256 + 64 * h
+                        tt(T.NV[:, 512 * (l - 2) + c1:512 * (l - 2) + c1 + 64], XB[l - 2][:, c1:c1 + 64], quarter("lt", h), OP.add,
+                           ["X%d" % (l - 2), "lt.%d" % h], ["NV.%d%d" % (l + 1, h)])
                 if l == 2:
                     keys("xg", "X", 1, 0)
                     keys("xg", "X", 0, 0)
@@ -585,10 +602,11 @@ def rank_program(g, core, T, topo):
                     spare.pop(0)()
                 if l == 4:
                     mm(T.TG[:, 8, 0:8], T.IU[:], T.jb[:], True, False, ["IU", "jb"], ["TG"])
-                    for j in (2, 1, 0):
+                    for j in (2, 1):
                         keys("yg", "Y", 0, j)
             else:
-                tt(T.LT[:], nv, w, OP.is_gt, [kx, kw], ["LT"])
+                for h in range(4):
+                    tt(quarter("LT", h), nv[h], w[h], OP.is_gt, [kx[h], kw[h]], ["LT.%d" % h])
         for l in (1, 2):
             act(T.NV[:, 512 * l:512 * l + 256], lev(l), AF.Copy, ["X%d" % l], ["NV.%d" % l])
 
@@ -602,91 +620,104 @@ def rank_program(g, core, T, topo):
                 act(T.gf[:], T.fbf[:], AF.Identity, ["fbf"], ["gf"], bias=192.0 - 0.5 + 2.0 ** -14, scale=2.0 ** -13)
         if t > 0:
             fill_names(0)
-        send(2, t, "LT", LB)
-        scan(T.KF[:, ::-1], T.inc[:, ::-1], T.LT[:, ::-1], 0.0, OP.add, OP.mult, ["inc", "LT"], ["KF"])
+        send(2, t, T.LT[:], T[LB][:], four("LT."), [LB])
+        for h in range(4):
+            back = slice(64 * h + 63, 64 * h - 1 if h else None, -1)
+            scan(T.KF[:, back], T.inc[:, back], T.LT[:, back], 0.0, OP.add, OP.mult, ["inc", "LT.%d" % h], ["KF.%d" % h])
         for h in range(2):
-            mm(part("OB", 256 + 128 * h, 128), half("LT", h), ident("1"), h == 0, h == 1, ["LT", "ID.1"], ["OB"])
+            mm(part("OB", 256 + 128 * h, 128), half("LT", h), ident("1"), h == 0, h == 1, four("LT.") + ["ID.1"], ["OB"])
         act(T.LTt[:], part("OB", 256, 256), AF.Identity, ["OB"], ["LTt", "rs"], acc=T.rs[:, 0:1])
         if t > 0:
             fill_names(1)
-        else:
+        while spare:
+            spare.pop(0)()
+        if t == 0:
             late_constants(2)
-        cp(T.HB[:, 0:128:16], T.KF[:, 0::32], ["KF"], ["HB"])
-        scan(T.HS[:, 0:128], T.hold[:], T.HB[:, 0:128], 0.0, OP.mult, OP.add, ["hold", "HB"], ["HS"])
-        mm(T.TG[:, 8, 0:8], T.HB[:, 1:129], T.dp[:], False, False, ["HB", "dp"], ["TG"])
-        mm(T.TG[:, 8, 0:8], T.HS[:, 0:128], T.dp[:], False, False, ["HS", "dp"], ["TG"])
-        mm(T.TG[:, 8, 0:8], T.HS[:, 1:129], T.dn[:], False, True, ["HS", "dn"], ["TG"])
+        for h in range(4):
+            cp(T.HB[:, 32 * h:32 * h + 32:16], T.KF[:, 64 * h:64 * h + 64:32], ["KF.%d" % h, "HB"], ["HB.%d" % h])
+        for h in range(4):
+            c = slice(32 * h, 32 * h + 32)
+            scan(T.HS[:, c], T.hold[:, c], T.HB[:, c], 0.0, OP.mult, OP.add, ["hold", "HB.%d" % h], ["HS.%d" % h])
+        mm(T.TG[:, 8, 0:8], T.HB[:, 1:129], T.dp[:], False, False, four("HB.") + ["dp"], ["TG"])
+        mm(T.TG[:, 8, 0:8], T.HS[:, 0:128], T.dp[:], False, False, four("HS.") + ["dp"], ["TG"])
+        mm(T.TG[:, 8, 0:8], T.HS[:, 1:129], T.dn[:], False, True, four("HS.") + ["HS", "dn"], ["TG"])
         cp(T.J[:], T.TG[:, 8, 0:8], ["TG"], ["J"])
-        send(1, t, "J", JB)
+        keys("yg", "Y", 0, 0)
+        if last:
+            sums(3, "X2")
+            keep_sums(3, "X2")
+        send(3, t, T.J[:], T[JB][:], ["J"], [JB])
         cp(T.M[:], T.xg[:, 0:4096].indirect(T.J[:, 0:8]), allkeys("xg") + ["J"], ["M"])
         tt(T.ge[:], T.xg[:, 0:4096].indirect(T.J[:, 0:8]), T.ZC[:], OP.is_ge, allkeys("xg") + ["J", "ZC"], ["ge"])
-        tt(T.h1[:, 0:128], T.X[:, 0:8192].indirect(T.offX[:, 0:8]), T.M[:], OP.subtract, XK + ["offX", "M"], ["h1.0"])
+        tt(T.xs[:], T.X[:, 0:8192].indirect(T.offX[:, 0:8]), T.M[:], OP.subtract, XK + ["offX", "M"], ["xs"])
         for j in (2, 1, 0):
             mm(YB[j][:], T.M[:], T.WR[:, 16 * j:16 * j + 16, :], False, True, ["M", "WR"], ["Y%d" % j])
             if j == 2:
                 mm(part("TG", 0, 128), T.B16[:], T.ge[:], True, True, ["ge", "B16"], ["TG"])
-        act(T.cY[:, 1024:1536], T.Y2[:], AF.Copy, ["Y2"], ["cY.2"])
-        cp(T.cY[:, 512:1024], T.Y1[:], ["Y1"], ["cY.1"])
+        cp(T.cY[:, 1024:1536], T.Y2[:], ["Y2"], ["cY.2"])
         act(T.fr[:], part("TG", 0, 128), AF.Relu, ["TG"], ["fr"], bias=-6.0)
-        act(T.cY[:, 0:512], T.Y0[:], AF.Copy, ["Y0"], ["cY.0"])
+        act(T.cY[:, 512:1024], T.Y1[:], AF.Copy, ["Y1"], ["cY.1"])
         act(T.nf[:], part("TG", 0, 128), AF.Relu, ["TG"], ["nf"], bias=7.0, scale=-1.0)
+        cp(T.cY[:, 0:512], T.Y0[:], ["Y0"], ["cY.0"])
         sign_marks("OB", 256, LB)
-        sign_levels("OB", 256, "cY", 2, False)
         sign_whole("OB", 256, "fr")
-        ts(T.h2[:, 0:128], T.h1[:, 0:128], 0.5, 127.25, OP.mult, OP.add, ["h1.0"], ["h2.0"])
-        cp(T.y0[:], T.yg[:, 0:4096].indirect(T[JB][:, 0:8]), allkeys("yg") + [JB], ["y0"])
-        sign_levels("OB", 256, "cY", 1, False)
-        for j in (1, 2, 0):
-            mm(XB[j][:], T.y0[:], T.WR[:, 16 * j:16 * j + 16, :], j > 0, True, ["y0", "WR"], ["X%d" % j])
-            if j == 1:
-                sign_levels("OB", 256, "cY", 0, True)
-        if t > 0:
-            tt(T.xd[:], T.X[:, 0:8192].indirect(T.offX[:, 0:8]), T.h2[:, 0:128], OP.subtract, XK + ["offX", "h2.0"], ["xd"])
-        early(0)
-        act(T.KB[:], part("OB", 256, 256), AF.Sign, ["OB"], ["KB"], bias=-2.0 ** -70)
-        act(T.cA[:, 0:512], T.X0[:], AF.Copy, ["X0"], ["cA.0"])
-        act(T.s2[:], part("OB", 256, 256), AF.Sign, ["OB"], ["s2"], bias=BIG1 / 2)
+        sign_levels("OB", 256, "cY", 2, False)
         mm(part("Y2", 256, 128), ident("-64"), T.fr[:], True, False, ["ID.-64", "fr"], ["Y2"])
         for h in range(2):
             mm(part("Y2", 256, 128), T.OT[:, h, :], half("LTt", h), False, h == 1, ["OT", "LTt"], ["Y2"])
         act(T.mm[:], part("Y2", 256, 128), AF.Relu, ["Y2"], ["mm"], bias=32.0)
+        cp(T.y0[:], T.yg[:, 0:4096].indirect(T[JB][:, 0:8]), allkeys("yg") + [JB], ["y0"])
+        sign_levels("OB", 256, "cY", 1, False)
+        sign_levels("OB", 256, "cY", 0, True)
+        for j in (1, 0, 2):
+            mm(XB[j][:], T.y0[:], T.WR[:, 16 * j:16 * j + 16, :], j > 0, True, ["y0", "WR"], ["X%d" % j])
+        ts(T.xh[:], T.xs[:], 0.5, 127.25, OP.mult, OP.add, ["xs"], ["xh"])
+        if last:
+            tt(T.xd[:], T.X[:, 0:8192].indirect(T.offX[:, 0:8]), T.xh[:], OP.subtract, XK + ["offX", "xh"], ["xd"])
+        act(T.KB[:], part("OB", 256, 256), AF.Sign, ["OB"], ["KB"], bias=-2.0 ** -70)
+        act(T.cA[:, 0:512], T.X0[:], AF.Copy, ["X0"], ["cA.0"])
+        act(T.s2[:], part("OB", 256, 256), AF.Sign, ["OB"], ["s2"], bias=BIG1 / 2)
         sign_marks("Y0", 0, "LT")
         sign_whole("Y0", 0, "nf")
+        blocks("Y1", 0, [("LTt", "LM", LS, "own")], False, True)
         for j in (1, 2):
-            tt(T.cA[:, 512 * j:512 * j + 512], XB[j][:], T.NV[:, 512 * j:512 * j + 512], OP.add, ["X%d" % j, "NV.%d" % j, "NV.%d" % (j + 3)], ["cA.%d" % j])
-            early(j)
-        for j in (1, 2, 0):
-            sign_levels("Y0", 0, "cA", j, j == 0)
-        blocks("X1", 0, [("KB", "LM", LS, "got")], False, True)
+            tt(T.cA[:, 512 * j:512 * j + 512], XB[j][:], T.NV[:, 512 * j:512 * j + 512], OP.add,
+               ["X%d" % j, "NV.%d" % j] + four("NV.%d" % (j + 3)), ["cA.%d" % j])
+            early(j - 1)
+        sign_levels("Y0", 0, "cA", 1, False)
+        mm(part("X1", 0, 256), T.mm[:], T.BD[:, 0, :, :], True, False, ["mm", "BD.-1/16"], ["X1"])
+        sign_levels("Y0", 0, "cA", 0, False)
+        sign_levels("Y0", 0, "cA", 2, True)
+        blocks("Y1", 0, [("KB", "OM", OS, "-1/2"), ("s2", "OM", OS, "1/2")], True)
+        blocks("X1", 0, [("KB", "LM", LS, "got")], False)
         if not last:
-            cp(T.X[:, 0:8192].indirect(T.offX[:, 0:8]), T.h2[:, 0:128], ["h2.0", "offX", "xd"], XK)
+            cp(T.X[:, 0:8192].indirect(T.offX[:, 0:8]), T.xh[:], ["xh", "offX"], XK)
+        early(2)
         early(3)
-        early(4)
         ts(T.KA[:], part("Y0", 0, 256), 0.0, -2.0, OP.is_gt, OP.mult, ["Y0"], ["KA"])
-        early(5)
-        blocks("Y1", 0, [("LTt", "LM", LS, "own"), ("KB", "OM", OS, "-1/2"), ("s2", "OM", OS, "1/2")], True, True)
-        mm(part("X1", 0, 256), T.mm[:], T.BD[:, 0, :, :], False, False, ["mm", "BD.-1/16"], ["X1"])
         blocks("X1", 0, [("KA", "OM", OS, "1/2")], True)
         tt(T.DA[:], part("Y1", 0, 256), T.rows[:, 0, :], OP.add, ["Y1", "rows"], ["DA"])
+        early(4)
         for s in (5, 4, 3):
             quot("A", s, 0, "DA")
         mm(part("Y2", 0, 256), T.ones[:], T.CT[:], True, False, ["ones", "CT.c"], ["Y2"])
         ts(T.DB[:], part("X1", 0, 256), 63.5, None, OP.add, None, ["X1"], ["DB"])
-        early(6)
+        early(5)
         mm(part("X0", 0, 256), T.ones[:], T.CT[:], True, False, ["ones", "CT.c"], ["X0"])
         blocks("X0", 0, [("KA", "ID", IDS, "-1/128")], False)
+        mm(part("X0", 0, 256), ident("1/2"), T.DA[:], False, False, ["ID.1/2", "DA"], ["X0"])
+        quot("V", 1, 0, "DA")
         for s in range(1, 6):
             quot("V", s, 1, "DB")
+        early(6)
+        quot("V", 2, 0, "DA")
         early(7)
         if last:
-            dma("S", T.yx[:], T.S[:], ["S.0", "S.1"], [])
-        for s in (1, 2):
-            quot("V", s, 0, "DA")
+            dma("S", T.yx[:], T.S[:], ["S"], [])
         mm(part("Y2", 0, 256), ident("1/2"), T.DB[:], False, False, ["ID.1/2", "DB"], ["Y2"])
         for s in range(1, 6):
             quot_add("Y2", s, 1, s == 5)
-        mm(part("X0", 0, 256), ident("1/2"), T.DA[:], False, False, ["ID.1/2", "DA"], ["X0"])
-        for s in (5, 4, 1, 2, 3):
+        for s in (1, 5, 4, 2, 3):
             quot_add("X0", s, 0, s == 3)
         if t == 0:
             fill_names(0)
@@ -700,61 +731,59 @@ def rank_program(g, core, T, topo):
             act(T.Z[:], part("Y0", 256, 128), AF.Abs, ["Y0"], ["Z"], bias=-255.0)
         act(T.nr[:], part("X2", 0, 256), AF.Relu, ["X2"], ["nr"])
         if not last:
-            sums(2 * t, "X1")
-            mm(T.Y0[:, 12, 0:1], T.onesf[:], T.rs[:, 0:1], True, True, ["onesf", "rs"], ["Y0"])
-            act(T.kc[:, 0:1], T.Y0[:, 12, 0:1], AF.Identity, ["Y0"], ["kc"], bias=4096.0 * 33 - 2.0 ** 23)
+            make_u(0)
+            mm(T.X1[:, 256:257], T.onesf[:], T.rs[:, 0:1], True, True, ["onesf", "rs"], ["X1"])
+            act(T.kc[:, 0:1], T.X1[:, 256:257], AF.Identity, ["X1"], ["kc"], bias=4096.0 * 33 - 2.0 ** 23)
         else:
             act(T.zd[:], part("Y0", 256, 128), AF.Abs, ["Y0"], ["zd"], bias=-255.0)
             dma("S", T.yz[:], T.zd[:], ["zd"], [])
-        for h, src, R, even, odd, bk in ((1, VB, [VB], T.Y2[:, 0:8, 0::2], T.Y2[:, 0:8, 1::2], "Y2"),
-                                         (0, "VA", VK, T.X0[:, 0:256:2], T.X0[:, 1:256:2], "X0")):
-            tt(T.E0[:, 8 * h:8 * h + 8, :], even, T[src][:, :, 0::2], OP.add, [bk] + R, ["E0.%d" % h])
-            tt(T.Y1[:, 8 * h:8 * h + 8, 0:16], odd, T[src][:, :, 1::2], OP.add, [bk] + R, ["Y1.%d" % h])
-            late(1 - h)
-            for s in range(APART):
-                stage(s, [h])
+
+        def step(h, s):
+            if s < 0:
+                src, bk, even, odd = (("VA", "X0", T.X0[:, 0:256:2], T.X0[:, 1:256:2]), (VB, "Y2", T.Y2[:, 0:8, 0::2], T.Y2[:, 0:8, 1::2]))[h]
+                tt(T.E0[:, 8 * h:8 * h + 8, :], even, T[src][:, 0, :], OP.add, [bk, src + ".0"], ["E0.%d" % h])
+                tt(T.Y1[:, 8 * h:8 * h + 8, 0:16], odd, T[src][:, 1, :], OP.add, [bk, src + ".1"], ["Y1.%d" % h])
+            elif s < 4:
+                stage(s, h)
+            else:
+                o, key = ((T.TG, "TG"), (T.BP, "BP"))[h]
+                for hi, alu in ((0, OP.min), (1, OP.max)):
+                    tt(o[:, 0:8, 16 * hi:16 * hi + 16], T.E0[:, 8 * h:8 * h + 8, :], T.Y1[:, 8 * h:8 * h + 8, 0:16], alu,
+                       ["E0.%d" % h, "Y1.%d" % h], [key])
+        step(1, -1)
         fill = T.Y2[:, 8:16, :]
         mm(fill, T.ones[0:1, :], T.topf[0:1, :], True, False, ["ones", "topf"], ["Y2"])
         for e in range(2):
             mm(T.Y2[:, 8:16, e::2], T.fbf[:, 128 * e:128 * e + 128], T.IDN[:], False, False, ["fbf", "IDN"], ["Y2"])
         if not last:
-            make_u(0)
-            keep_sums(2 * t, "X1")
+            make_u(1)
         for e in range(2):
             mm(T.Y2[:, 8:16, e::2], T.gf[:, 128 * e:128 * e + 128], ident("-1/128"), False, False, ["gf", "ID.-1/128"], ["Y2"])
         mm(fill, ident("1"), T.nr[:], False, True, ["ID.1", "nr"], ["Y2"])
+        for s in range(5):
+            step(1, s)
+            step(0, s - 1)
+            if s == 0 and not last:
+                turn_init(OWN, 0)
+            if s == 0 and t == RO - 2:
+                for j, bk in enumerate(("X0", "Y0")):
+                    sums(j, bk)
+                    keep_sums(j, bk)
+        halves = [slice(1, 32, 2), slice(0, 32, 2)] if not last else [slice(0, 16), slice(16, 32)]
+        tt(T.v1[:, :, halves[0]], T.BP[:, :, halves[0]], T.Y2[:, 8:16, halves[0]], OP.min, ["BP", "Y2"], ["v1.0"])
+        step(0, 4)
+        tt(T.v1[:, :, halves[1]], T.BP[:, :, halves[1]], T.Y2[:, 8:16, halves[1]], OP.min, ["BP", "Y2"], ["v1.1"])
         if not last:
-            make_u(1)
-            sums(2 * t + 1, "X0")
-            keep_sums(2 * t + 1, "X0")
-            turn_init(OWN, 0)
-        for s in range(4):
-            if s >= APART:
-                for hs in LISTS:
-                    stage(s, hs)
-            late(2 + s)
-        for hi, alu in ((0, OP.min), (1, OP.max)):
-            tt(T.AP[:, :, 16 * hi:16 * hi + 16], T.E0[:, 0:8, :], T.Y1[:, 0:8, 0:16], alu, ["E0.0", "Y1.0"], ["AP"])
-            tt(T.TG[:, 0:8, 16 * hi:16 * hi + 16], T.E0[:, 8:16, :], T.Y1[:, 8:16, 0:16], alu, ["E0.1", "Y1.1"], ["TG"])
-        late(6)
-        if not last:
-            for e in (1, 0):
-                tt(T.v1[:, :, e::2], T.AP[:, :, e::2], T.TG[:, 0:8, e::2], OP.min, ["AP", "TG"], ["v1.%d" % e])
-            late(7)
-            for e in (1, 0):
-                tt(T.VA[:, :, e::2], T.v1[:, :, e::2], T.Y2[:, 8:16, e::2], OP.min, ["v1.%d" % e, "Y2"], ["VA.%d" % e])
-            send(0, t + 1, "VA", "VB%d" % (t + 1), VK)
+            for b, e in enumerate((1, 0)):
+                tt(T.VA[:, e, :], T.v1[:, :, halves[b]], T.TG[:, 0:8, halves[b]], OP.min, ["v1.%d" % b, "TG"], ["VA.%d" % e])
+                send_names(t + 1, e)
             turn_own()
         else:
+            turn_init(OWN, 4, (0, 1))
             for b in range(2):
-                mm(part("OB", 256 + 128 * b, 128), T.TP[:, 4 + b, :], T.ones[:], b == 0, False, ["TP.c", "TP.%d" % (4 + b)], ["OB"])
-            for b in range(2):
-                c = slice(16 * b, 16 * b + 16)
-                tt(T.v1[:, :, c], T.AP[:, :, c], T.TG[:, 0:8, c], OP.min, ["AP", "TG"], ["v1.%d" % b])
-            for b in range(2):
-                c = slice(16 * b, 16 * b + 16)
-                tt(T.VL[:, 128 * b:128 * b + 128], T.v1[:, :, c], T.Y2[:, 8:16, c], OP.min, ["v1.%d" % b, "Y2"], ["VL.%d" % b])
-                mm(part("OB", 256 + 128 * b, 128), T.VL[:, 128 * b:128 * b + 128], T.IU[:], False, b == 1, ["VL.%d" % b, "IU"], ["OB"])
-            cp(T.amf[:], part("OB", 256, 256), ["OB"], ["amf"])
-            dma("S", T.ya[:], T.amf[:], ["amf"], [])
+                tt(T.VL[:, 128 * b:128 * b + 128], T.v1[:, :, halves[b]], T.TG[:, 0:8, halves[b]], OP.min, ["v1.%d" % b, "TG"], ["VL.%d" % b])
+                mm(part(OWN[b][0], 0, 128), T.VL[:, 128 * b:128 * b + 128], T.IU[:], False, True, ["VL.%d" % b, "IU"], [OWN[b][0]])
+            act(half("amf", 0), part(OWN[0][0], 0, 128), AF.Copy, [OWN[0][0]], ["amf.0"])
+            cp(half("amf", 1), part(OWN[1][0], 0, 128), [OWN[1][0]], ["amf.1"])
+            dma("S", T.ya[:], T.amf[:], ["amf.0", "amf.1"], [])
     plan["emit"](g, T)

@@ -10,7 +10,8 @@ HUGE = 2.0 ** 99
 DOWN = 2.0 ** -20
 UP = 2.0 ** 20
 MAGIC = 1.5 * 2.0 ** 23
-SPLIT = (64, 56)
+SPLIT = (64, 52)
+SHARE = 10
 NENG = 8
 
 F, B, I, U = "float32", "bfloat16", "int32", "uint16"
@@ -31,7 +32,7 @@ TOPS = [(0, -4096.0), (1, -4096.0), (0, 32.0), (1, 32.0), (0, 0.0), (1, 0.0)]
 SCRATCH = {
     "X": _s([8192], B), "xg": _s([4096], B), "yg": _s([4096], B), "S": _s([2048], F),
     "ami": _s([256], I), "amf": _s([256], F), "Z": _s([128], B), "ZC": _s([128], B), "wi": _s([8], I), "wf": _s([8], F),
-    "VA": _s([2, 128], F), "VL": _s([256], F), "VB0": _s([2, 128], F), "VB1": _s([2, 128], F), "VB2": _s([2, 128], F),
+    "VA": _s([2, 8, 16], F), "VL": _s([256], F), "VB0": _s([2, 8, 16], F), "VB1": _s([2, 8, 16], F), "VB2": _s([2, 8, 16], F),
     "LT": _s([256], B), "LB0": _s([256], B), "LB1": _s([256], B), "LB2": _s([256], B),
     "J": _s([8], U), "JB0": _s([8], U), "JB1": _s([8], U), "JB2": _s([8], U),
     "h1": _s([256], I), "h2": _s([256], I), "offA": _s([256], U), "offB": _s([256], U),
@@ -39,13 +40,12 @@ SCRATCH = {
     "cm": _s([128], F), "Dm": _s([128], F), "u32": _s([128], F), "gu": _s([128], B),
     "NV": _s([1536], F), "si": _s([8], I), "sj": _s([8], I), "sk": _s([8], F), "offX": _s([8], U),
     "w": _s([256], F), "r0": _s([256], B), "rA": _s([256], B), "rB": _s([256], B), "lt": _s([256], B),
-    "KF": _s([256], F), "HB": _s([136], F), "HS": _s([136], F), "hold": _s([128], F), "inc": _s([256], F),
+    "LX": _s([8, 48], B), "KF": _s([8, 48], F), "inc": _s([8, 48], F), "HS": _s([128], F), "mine": _s([128], F),
     "M": _s([128], B), "y0": _s([128], B), "ge": _s([128], B),
     "fr": _s([128], B), "nf": _s([128], B), "mm": _s([128], B), "LTt": _s([256], B), "KA": _s([256], B), "KB": _s([256], B), "s2": _s([256], B),
     "sl": _s([8], F), "offS": _s([8], U), "xs": _s([128], B), "xh": _s([128], I), "xd": _s([128], F), "BP": _s([8, 32], F), "xp": _s([128], F),
     "cA": _s([1536], B), "cY": _s([1536], B), "DA": _s([256], B), "DB": _s([256], B), "nr": _s([256], B),
-    "G1": _s([512], B), "G2": _s([512], B), "G3": _s([512], B), "G4": _s([512], B), "G5": _s([512], B),
-    "E0": _s([16, 16], F), "E1": _s([16, 16], F), "AP": _s([8, 32], F), "v1": _s([8, 32], F),
+    "GA": _s([5, 256], B), "GB": _s([5, 256], B), "E0": _s([16, 16], F), "E1": _s([16, 16], F), "v1": _s([8, 32], F),
     "zd": _s([128], F), "rs": _s([8], F), "kc": _s([8], F),
     "ones": _s([128], B), "zero": _s([256], B), "onesf": _s([128], F), "ID": _s([len(IDS), 128], B), "IU": _s([128], F), "IDN": _s([128], F),
     "OM": _s([len(OS), 128], B), "LM": _s([len(LS), 128], B), "OT": _s([2, 128], B), "tri": _s([128], B), "dia": _s([128], B),
@@ -53,7 +53,7 @@ SCRATCH = {
     "W": _s([48], B), "WR": _s([48, 32], B), "B16": _s([128], B), "BD": _s([len(BDS), 8, 32], B), "BW": _s([128], B), "WZ": _s([144], B),
     "br": _s([8, 32], B), "TP": _s([len(TOPS), 128], B), "CT": _s([256], B),
     "topl": _s([256], B), "topf": _s([256], B), "rows": _s([len(ROWS), 256], B), "urow": _s([128], B),
-    "dp": _s([8], F), "dn": _s([8], F), "jb": _s([8], F), "cx": _s([8], F), "cs": _s([8], F),
+    "dp": _s([8], F), "jb": _s([8], F), "cx": _s([8], F), "cs": _s([8], F),
     "X0": ("psum", [128, 512], F), "X1": ("psum", [128, 512], F), "X2": ("psum", [128, 512], F),
     "Y0": ("psum", [128, 16, 32], F), "Y1": ("psum", [128, 16, 32], F), "Y2": ("psum", [128, 16, 32], F),
     "TG": ("psum", [128, 16, 32], F), "OB": ("psum", [128, 512], F),
@@ -177,7 +177,7 @@ def rank_program(g, core, T, topo):
 
     def act(o, x, f, R, W, bias=0.0, scale=1.0, acc=None):
         if acc is not None:
-            op("A", lambda: a.activation(o, x, f, accum_out=acc), R, W)
+            op("A", lambda: a.activation(o, x, f, scale=scale, accum_out=acc), R, W)
         elif f == AF.Copy:
             op("A", lambda: a.activation(o, x, f), R, W)
         else:
@@ -269,7 +269,8 @@ def rank_program(g, core, T, topo):
     iota(T.io3[:], [[1, 8], [0, 16]], 0, 0, ["io3"])
     ms(T.br[:, :, 0:1], 0.0, ["br"])
     ms(T.W[:], 0.0, ["W"])
-    key_weights([0, 3, 6, 9, 12, 15, 1, 4, 7, 10])
+    key_weights([0, 3, 6, 9, 12, 15, 1, 4, 7, 10, 13, 2, 5, 8, 11, 14])
+    iota(T.io5[:], [[1, 4], [0, 32]], 0, 0, ["io5"])
     between = [lambda: ms(T.ones[:], 1.0, ["ones"]),
                lambda: ts(T.pc[:, 1:2], T.pc[:, 0:1], 15, None, OP.bitwise_and, None, ["pc0"], ["pc1"]),
                lambda: ts(T.pc[:, 2:3], T.pc[:, 0:1], 4, None, OP.arith_shift_right, None, ["pc0"], ["pc1"]),
@@ -297,27 +298,28 @@ def rank_program(g, core, T, topo):
     for b in range(2):
         mm(T.TG[:, 0:8, 16 * b:16 * b + 16], T.amf[:, 128 * b:128 * b + 128], T.IDN[:], False, b == 1, ["amf", "IDN"], ["TG"])
     ms(T.TP[64:65, 2:4, :], 32.0, ["TP.c"])
+    ms(T.TP[32:33, 5, :], -4.0 * 8192, ["TP.c"])
+    ms(T.CT[:], 0.0, ["CT"])
     ms(T.WZ[:], 0.0, ["WZ"])
     for e in (1, 0):
         cp(T.VA[:, e, :], T.TG[:, 0:8, e::2], ["TG"], ["VA.%d" % e])
     ts(T.WZ[:, 16::16], T.io1[:], G_, T.wf[:, 0:1], OP.is_equal, OP.mult, ["io1", "pf", "wf", "WZ"], ["WZ"])
     for e in (1, 0):
         send_names(0, e)
-    key_weights([13, 2, 5, 8, 11, 14])
     WK = ["W.%d" % l for l in range(6)]
 
     def make_u(step):
-        raw, big, small = part("Y0", 0, 128), part("Y0", 256, 128), T.Y0[:, 4, 0:8]
+        raw, big, small = part("X0", 0, 128), part("X0", 256, 128), T.Y0[:, 4, 0:8]
         if step == 0:
-            mm(raw, T.BW[:], T.Z[:], True, True, ["BW", "Z"], ["Y0"])
-            act(T.gu[:], raw, AF.Identity, ["Y0"], ["gu"], bias=192.0 - 0.5 + 2.0 ** -11, scale=2.0 ** -10)
+            mm(raw, T.BW[:], T.Z[:], True, True, ["BW", "Z"], ["X0"])
+            act(T.gu[:], raw, AF.Identity, ["X0"], ["gu"], bias=192.0 - 0.5 + 2.0 ** -11, scale=2.0 ** -10)
         if step == 1:
-            mm(big, T.urow[0:1, :], T.ones[0:1, :], True, False, ["urow", "ones"], ["Y0"])
-            mm(big, T.BW[:], T.Z[:], False, False, ["BW", "Z"], ["Y0"])
-            mm(big, ident("-1024"), T.gu[:], False, True, ["ID.-1024", "gu"], ["Y0"])
-            act(T.cm[:], big, AF.Identity, ["Y0"], ["cm"], bias=33.0, scale=2.0)
-            act(T.Dm[:], big, AF.Identity, ["Y0", "kc"], ["Dm"], bias=T.kc[:, 0:1], scale=8192.0)
-            act(T.u32[:], big, AF.Identity, ["Y0"], ["u32"], scale=1.0 / 32)
+            mm(big, T.urow[0:1, :], T.ones[0:1, :], True, False, ["urow", "ones"], ["X0"])
+            mm(big, T.BW[:], T.Z[:], False, False, ["BW", "Z"], ["X0"])
+            mm(big, ident("-1024"), T.gu[:], False, True, ["ID.-1024", "gu"], ["X0"])
+            act(T.cm[:], big, AF.Identity, ["X0"], ["cm"], bias=33.0, scale=2.0)
+            act(T.Dm[:], big, AF.Identity, ["X0", "kc"], ["Dm"], bias=T.kc[:, 0:1], scale=8192.0)
+            act(T.u32[:], big, AF.Identity, ["X0"], ["u32"], scale=1.0 / 32)
             act(T.ZC[:], T.Z[:], AF.Identity, ["Z"], ["ZC"], bias=255.0, scale=-1.0)
         if step == 2:
             for r in range(16):
@@ -397,31 +399,35 @@ def rank_program(g, core, T, topo):
         for n_, (src, buf, names, name) in enumerate(terms):
             for h in range(2):
                 mm(part(bk, c0 + 128 * h, 128), half(src, h), pick(buf, names, name), start and h == 0 and n_ == 0,
-                   stop and h == 1 and n_ == len(terms) - 1, [src, "%s.%s" % (buf, name)], [bk])
+                   stop and h == 1 and n_ == len(terms) - 1, [src, "%s.%d" % (src, h), "%s.%s" % (buf, name)], [bk])
 
     def sign_marks(bk, c0, marks):
         for h in range(2):
-            mm(part(bk, c0 + 128 * h, 128), half(marks, h), ident("big"), h == 0, False, [marks, "ID.big"] + four(marks + "."), [bk])
+            mm(part(bk, c0 + 128 * h, 128), half(marks, h), ident("big"), False, False, [marks, "ID.big"], [bk])
 
     def sign_whole(bk, c0, flag):
         for h in range(2):
-            mm(part(bk, c0 + 128 * h, 128), T.BD[:, 1, 4 * h:4 * h + 4, :], T[flag][:], False, False, ["BD.big", flag], [bk])
+            mm(part(bk, c0 + 128 * h, 128), T.BD[:, 1, 4 * h:4 * h + 4, :], T[flag][:], h == 0, False, ["BD.big", flag], [bk])
 
-    def sign_levels(bk, c0, src, j, stop):
-        for c in (2 * j, 2 * j + 1):
+    def sign_levels(bk, c0, src, which, stop, start=False):
+        for c in which:
             for h in range(2):
-                mm(part(bk, c0 + 128 * h, 128), T[src][:, 256 * c + 128 * h:256 * c + 128 * h + 128], ident("1"), False,
-                   stop and c % 2 == 1 and h == 1, ["%s.%d" % (src, j), "ID.1"], [bk])
+                mm(part(bk, c0 + 128 * h, 128), T[src][:, 256 * c + 128 * h:256 * c + 128 * h + 128], ident("1"), start and c == which[0] and h == 0,
+                   stop and c == which[-1] and h == 1, ["%s.%d" % (src, c), "ID.1"], [bk])
 
     make_u(0)
     turn_init(OWN, 0)
     make_u(1)
-    tops([2, 3])
-    turn_own()
 
-    act(T.WR[:, :, 0:1], T.W[:], AF.Identity, WK, ["WR"], scale=-1.0)
-    for s in range(4):
+    def widen(s):
         act(T.WR[:, :, 2 ** s:2 ** (s + 1)], T.WR[:, :, 0:2 ** s], AF.Copy, ["WR"], ["WR"])
+    act(T.WR[:, :, 0:1], T.W[:], AF.Identity, WK, ["WR"], scale=-1.0)
+    tops([2, 3])
+    widen(0)
+    act(T.CT[0:1, :], T.zero[0:1, :], AF.Identity, ["zero", "CT"], ["CT.c"], bias=280.0)
+    widen(1)
+    act(T.CT[32:33, :], T.br[32:33, :, :], AF.Identity, ["br", "CT"], ["CT.c"], bias=0.5, scale=-1.0 / 128)
+    widen(2)
     ms(T.r0[:], 0.0, ["r0"])
     ms(T.w[:, 63::64], HUGE, four("w."))
     ms(T.OB[:, 63:256:64], HUGE, four("OB.w"))
@@ -432,34 +438,32 @@ def rank_program(g, core, T, topo):
     ts(T.pf[:, 11:12], P_, 16.0 * DOWN, None, OP.mult, None, ["pf"], ["pf10"])
     ts(T.pf[:, 12:13], P_, 64.0, None, OP.mult, None, ["pf"], ["pf12"])
     ts(T.dp[:], T.io1[:], G_, None, OP.is_equal, None, ["io1", "pf"], ["dp"])
-    ts(T.dn[:], T.io1[:], G_, -1.0, OP.is_equal, OP.mult, ["io1", "pf"], ["dn"])
     ts(T.jb[:], T.io1[:], 256.0 * DOWN, T.pf[:, 11:12], OP.mult, OP.add, ["io1", "pf10"], ["jb"])
     ts(T.cx[:], T.io1[:], 1024.0, T.pf[:, 12:13], OP.mult, OP.add, ["io1", "pf12"], ["cx"])
     ts(T.B16[:], T.io3[:], G_, None, OP.is_equal, None, ["io3", "pf"], ["B16"])
+    turn_own()
     ts(T.dia[:], ident("1"), K_, 0.5, OP.mult, OP.mult, ["ID.1", "pf"], ["dia"])
-    iota(T.io5[:], [[1, 4], [0, 32]], 0, 0, ["io5"])
-    ts(pick("OM", OS, "1/2"), T.io5[:], Q_, 0.5, OP.is_equal, OP.mult, ["io5", "pf"], ["OM.1/2"])
+    for n_, c in OS.items():
+        ts(pick("OM", OS, n_), T.io5[:], Q_, c, OP.is_equal, OP.mult, ["io5", "pf"], ["OM." + n_])
     diagonals(["1/2", "-64"])
     select(T.tri[:], pick("OM", OS, "1/2"), [[1, 128]], OP.is_ge, 0.0, 0, -1, ["OM.1/2"], ["tri"])
     diagonals(["big"])
     iota(T.io2[:], [[0, 8], [1, 16]], 0, 0, ["io2"])
     iota(T.io6[:], [[0, 4], [1024, 2]], 0, 0, ["io6"])
-    iota(T.inc[:], [[0, 128], [-4095, 2]], 2048, 0, ["inc"])
-    iota(T.HB[:], [[0, 136]], 0, 0, ["HB"])
-    iota(T.HS[:, 128:136], [[0, 8]], 0, 0, ["HS"])
-    iota(T.CT[:], [[0, 256]], 0, 0, ["CT"])
+    iota(T.inc[:, :, 16:48], [[0, 128], [-4095, 2]], 2048, 0, ["inc"])
+    iota(T.inc[:, :, 0:16], [[0, 128]], 0, 0, ["inc"])
+    iota(T.LX[:, :, 0:16], [[0, 128]], 1, 0, ["LX"])
+    select(T.OT[:], T.zero[:], [[-128, 2], [32, 8], [0, 16]], OP.is_ge, 1.0, -1, -1, ["zero"], ["OT"])
+    select(T.OT[:], T.OT[:], [[-128, 2], [32, 8], [0, 16]], OP.is_ge, 0.0, 31, -1, ["OT"], ["OT"])
     diagonals(["g1", "g2", "g3", "g4", "g5", "-1/128"])
     for n_, (sign, c) in enumerate(ROWS.values()):
         iota(T.rows[:, n_, :], [[0, 8], [sign, 32]], c, 0, ["rows"])
-    iota(T.onesf[:], [[0, 128]], 32, 0, ["onesf"])
+    iota(T.onesf[:], [[0, 128]], -32, 0, ["onesf"])
     first_spare = [
-        lambda: ts(pick("LM", LS, "own"), part("Y1", 0, 128), -2.0, None, OP.mult, None, ["Y1"], ["LM.own"]),
+        lambda: ts(pick("LM", LS, "own"), part("Y1", 0, 128), 2.0, None, OP.mult, None, ["Y1"], ["LM.own"]),
         lambda: ts(pick("LM", LS, "got"), part("Y1", 128, 128), -1.0, None, OP.mult, None, ["Y1"], ["LM.got"]),
-        lambda: ts(T.hold[:], T.io2[:], P_, None, OP.is_le, None, ["io2", "pf"], ["hold"]),
-        lambda: ts(T.cs[:], T.io6[:], T.pf[:, 12:13], None, OP.add, None, ["io6", "pf12"], ["cs"]),
-        lambda: ms(T.hold[:, 0::16], 0.0, ["hold"], ["hold"]),
-        lambda: ts(T.OT[:, 0, :], T.io3[:], 0.0, Q_, OP.add, OP.is_equal, ["io3", "pf"], ["OT"]),
-        lambda: ts(T.OT[:, 1, :], T.io3[:], -4.0, Q_, OP.add, OP.is_equal, ["io3", "pf"], ["OT"])]
+        lambda: ts(T.mine[:], T.io2[:], P_, None, OP.is_equal, None, ["io2", "pf"], ["mine"]),
+        lambda: ts(T.cs[:], T.io6[:], T.pf[:, 12:13], None, OP.add, None, ["io6", "pf12"], ["cs"])]
 
     def late_constants(k):
         if k == 0:
@@ -469,19 +473,9 @@ def rank_program(g, core, T, topo):
                 mm(o, ident("1"), T.dia[:], False, False, ["ID.1", "dia"], ["Y1"])
             mm(part("Y1", 128, 128), ident("-64"), ident("1/2"), False, True, ["ID.-64", "ID.1/2"], ["Y1"])
         if k == 1:
-            act(T.WR[:, :, 16:32], T.WR[:, :, 0:16], AF.Copy, ["WR"], ["WR"])
             for n_, (name, c) in enumerate(BDS.items()):
                 for b in range(2):
                     act(T.BD[:, n_, :, 16 * b:16 * b + 16], T.B16[:], AF.Identity, ["B16"], ["BD." + name], scale=c)
-        if k == 2:
-            act(T.OT[:], T.OT[:], AF.Identity, ["OT"], ["OT"], scale=-1.0)
-            act(pick("OM", OS, "-1/2"), pick("OM", OS, "1/2"), AF.Identity, ["OM.1/2"], ["OM.-1/2"], scale=-1.0)
-            act(T.CT[0:1, :], T.zero[0:1, :], AF.Identity, ["zero", "CT"], ["CT.c"], bias=280.0)
-            act(T.CT[32:33, :], T.br[32:33, :, :], AF.Identity, ["br", "CT"], ["CT.c"], bias=0.5, scale=-1.0 / 128)
-        if k == 3:
-            act(T.topf[0:1, :], T.br[0:1, :, :], AF.Identity, ["br"], ["topf"], bias=1.5, scale=2.0 ** -7)
-            tops([4, 5])
-            ms(T.TP[32:33, 5, :], -4.0 * 8192, ["TP.c"])
 
     def sums(j, bk):
         for q in range(4):
@@ -498,15 +492,25 @@ def rank_program(g, core, T, topo):
         else:
             cp(win, T.xp[:, c], ["xp", "offS"], ["S"])
 
-    def quot(eng, s, h, src):
-        o, off = T["G%d" % s][:, 256 * h:256 * h + 256], 192.0 - 0.5 + 2.0 ** -(s + 1)
-        if eng == "V":
-            ts(o, T[src][:], 2.0 ** -s, off, OP.mult, OP.add, [src], ["G%d.%d" % (s, h)])
-        else:
-            act(o, T[src][:], AF.Identity, [src], ["G%d.%d" % (s, h)], bias=off, scale=2.0 ** -s)
+    def span(h):
+        return (0, 256, (0, 1)) if h is None else (128 * h, 128, (h,))
 
-    def quot_add(bk, s, h, stop=False):
-        mm(part(bk, 0, 256), ident("g%d" % s), T["G%d" % s][:, 256 * h:256 * h + 256], False, stop, ["ID.g%d" % s, "G%d.%d" % (s, h)], [bk])
+    def quot(eng, s, lst, h=None):
+        c0, n, hs = span(h)
+        o, x, off = T["G" + lst][:, s - 1, c0:c0 + n], T["D" + lst][:, c0:c0 + n], 192.0 - 0.5 + 2.0 ** -(s + 1)
+        R, W = ["D%s.%d" % (lst, k) for k in hs], ["G%s%d.%d" % (lst, s, k) for k in hs]
+        if eng == "V":
+            ts(o, x, 2.0 ** -s, off, OP.mult, OP.add, R, W)
+        else:
+            act(o, x, AF.Identity, R, W, bias=off, scale=2.0 ** -s)
+
+    def quot_add(bk, lst, h, which, stop=False):
+        c0, n, hs = span(h)
+        for s in which:
+            name = "g%d" % s if s else "1/2"
+            x = T["G" + lst][:, s - 1, c0:c0 + n] if s else T["D" + lst][:, c0:c0 + n]
+            mm(part(bk, c0, n), ident(name), x, False, stop and s == which[-1],
+               ["ID." + name] + [("G%s%d.%d" % (lst, s, k) if s else "D%s.%d" % (lst, k)) for k in hs], [bk])
 
     def stage(s, h):
         ei, eo = ("E0", "E1") if s % 2 == 0 else ("E1", "E0")
@@ -522,6 +526,11 @@ def rank_program(g, core, T, topo):
         last = t == RO - 1
         VB, LB, JB = "VB%d" % t, "LB%d" % t, "JB%d" % t
 
+        def new_columns(h):
+            c = (slice(0, 6), slice(6, 8))[h]
+            if not last:
+                cp(T.X[:, 0:8192].indirect(T.offX[:, c]), T.xh[:, 16 * c.start:16 * c.stop], ["xh", "offX"], XK)
+
         def early(k):
             if last:
                 patch(k)
@@ -529,36 +538,41 @@ def rank_program(g, core, T, topo):
         gather("A", "xg", "offA", 1, s1, 128)
         gather("A", "xg", "offA", 0, s0, 128)
         turn_init(GOT, 0)
-        columns(0)
+        if t == 0:
+            widen(3)
+            act(T.topf[0:1, :], T.br[0:1, :, :], AF.Identity, ["br"], ["topf"], bias=1.5, scale=2.0 ** -7)
+        if t == 1:
+            tops([4, 5])
         if last:
             sums(2, "Y1")
             keep_sums(2, "Y1")
         turn(GOT, VB, (1,))
         gather("V", "xg", "offA", 1, 0, s1)
         turn(GOT, VB, (0,))
-        cuts = [0, 16, 32, s0]
-        for step in range(6):
-            for e, k in ((1, step), (0, step - 2)):
+        gather("V", "xg", "offA", 0, 0, s0 // 2)
+        for step in range(5):
+            for e, k in ((1, step), (0, step - 1)):
                 if 0 <= k < 4:
                     for q in range(2):
                         hash_step(GOT, "offB", k, e, q)
-            if step < 3:
-                gather("V", "xg", "offA", 0, cuts[step], cuts[step + 1])
-            elif step < 5:
-                fill_product(step - 3)
-        spare = [lambda: columns(1)]
-        if t == 0:
-            spare += [lambda: [f() for f in first_spare[0:2]], first_spare[2]]
+            if step == 0:
+                gather("V", "xg", "offA", 0, s0 // 2, s0)
+            if step == 3:
+                columns(0)
+                fill_product(0)
+        fill_product(1)
+        spare = [lambda: columns(1), lambda: gather("V", "yg", "offB", 0, 128 - SHARE, 128), lambda: [f() for f in first_spare[0:3] if t == 0],
+                 lambda: gather("V", "yg", "offB", 0, 128 - 2 * SHARE, 128 - SHARE)]
         spare += [lambda k=k: columns(k) for k in range(2, 6 if last else 4)]
         if t == 0:
             spare += first_spare[3:]
         gather("A", "yg", "offB", 1, 0, 128)
         for j in range(3):
             keys("xg", "X", 1, j)
-        if t == 0:
-            late_constants(0)
         keys("xg", "X", 0, 0, True)
         keys("xg", "X", 0, 1)
+        if t == 0:
+            late_constants(0)
         r = "r0"
         for l in range(6):
             src, c0, wb = (XB[l], 0, T.w) if l < 3 else (T.NV, 512 * (l - 3) + 256, T.OB)
@@ -573,9 +587,9 @@ def rank_program(g, core, T, topo):
             if spare:
                 spare.pop(0)()
             if l == 2:
-                gather("A", "yg", "offB", 0, 0, 128)
+                gather("A", "yg", "offB", 0, 0, 128 - 2 * SHARE)
             if l == 3 and t == 0:
-                late_constants(1)
+                widen(4)
             if l < 5:
                 for h in range(4):
                     tt(quarter("lt", h), nv[h], w[h], OP.is_gt, [kx[h], kw[h]], ["lt.%d" % h])
@@ -584,12 +598,15 @@ def rank_program(g, core, T, topo):
                            ["ID.big", "lt.%d" % (h - 1), "lt.%d" % h], ["X%d" % (l + 1)])
                 if l == 0:
                     keys("xg", "X", 0, 2)
+                if l == 1 and last:
+                    sums(3, "TG")
                 if l == 2:
+                    if last:
+                        keep_sums(3, "TG")
                     for j in range(3):
                         keys("yg", "Y", 1, j)
                 r = "rA" if l % 2 == 0 else "rB"
-                for h in range(4):
-                    tt(quarter(r, h), w[h], nv[h], OP.subtract, [kx[h], kw[h]], ["%s.%d" % (r, h)])
+                tt(T[r][:], wb[:, 0:256], src[:, c0:c0 + 256], OP.subtract, kx + kw, four(r + "."))
                 if l >= 2:
                     for h in range(4):
                         c1 = 256 + 64 * h
@@ -601,189 +618,179 @@ def rank_program(g, core, T, topo):
                 if spare:
                     spare.pop(0)()
                 if l == 4:
-                    mm(T.TG[:, 8, 0:8], T.IU[:], T.jb[:], True, False, ["IU", "jb"], ["TG"])
-                    for j in (2, 1):
-                        keys("yg", "Y", 0, j)
+                    for j in (None, 2, 1) if not last else (2, 1, None):
+                        if j is None:
+                            mm(T.TG[:, 8, 0:8], T.IU[:], T.jb[:], True, False, ["IU", "jb"], ["TG"])
+                        else:
+                            keys("yg", "Y", 0, j)
             else:
                 for h in range(4):
-                    tt(quarter("LT", h), nv[h], w[h], OP.is_gt, [kx[h], kw[h]], ["LT.%d" % h])
+                    tt(T.LX[:, 2 * h:2 * h + 2, 16:48], nv[h], w[h], OP.is_gt, [kx[h], kw[h]], ["LX.%d" % h])
         for l in (1, 2):
             act(T.NV[:, 512 * l:512 * l + 256], lev(l), AF.Copy, ["X%d" % l], ["NV.%d" % l])
+            if l == 1:
+                act(T.LT[:], T.LX[:, :, 16:48], AF.Copy, four("LX."), ["LT"])
 
         def fill_names(k):
             if k == 0:
                 for e in range(2):
-                    act(T.f1[:, 128 * e:128 * e + 128], T.ft[:, 128 * e:128 * e + 128], AF.Identity, ["ft", "pf8"], ["f1"], bias=T.pf[:, 8 + e:9 + e])
-                act(T.ft[:], T.f1[:], AF.Identity, ["f1"], ["ft"], bias=MAGIC)
+                    ts(half("f1", e), half("ft", e), T.pf[:, 8 + e:9 + e], MAGIC, OP.add, OP.add, ["ft", "pf8"], ["f1"])
+            elif k == 1:
+                ts(T.fbf[:], T.f1[:], -MAGIC, None, OP.add, None, ["f1"], ["fbf"])
             else:
-                act(T.fbf[:], T.ft[:], AF.Identity, ["ft"], ["fbf"], bias=-MAGIC)
                 act(T.gf[:], T.fbf[:], AF.Identity, ["fbf"], ["gf"], bias=192.0 - 0.5 + 2.0 ** -14, scale=2.0 ** -13)
-        if t > 0:
-            fill_names(0)
-        send(2, t, T.LT[:], T[LB][:], four("LT."), [LB])
-        for h in range(4):
-            back = slice(64 * h + 63, 64 * h - 1 if h else None, -1)
-            scan(T.KF[:, back], T.inc[:, back], T.LT[:, back], 0.0, OP.add, OP.mult, ["inc", "LT.%d" % h], ["KF.%d" % h])
-        for h in range(2):
-            mm(part("OB", 256 + 128 * h, 128), half("LT", h), ident("1"), h == 0, h == 1, four("LT.") + ["ID.1"], ["OB"])
-        act(T.LTt[:], part("OB", 256, 256), AF.Identity, ["OB"], ["LTt", "rs"], acc=T.rs[:, 0:1])
-        if t > 0:
-            fill_names(1)
+        send(2, t, T.LT[:], T[LB][:], ["LT"], [LB])
+        for gq in range(8):
+            scan(T.KF[:, gq, ::-1], T.inc[:, gq, ::-1], T.LX[:, gq, ::-1], 0.0, OP.add, OP.mult, ["inc", "LX", "LX.%d" % (gq // 2)], ["KF.%d" % (gq // 2)])
         while spare:
             spare.pop(0)()
-        if t == 0:
-            late_constants(2)
-        for h in range(4):
-            cp(T.HB[:, 32 * h:32 * h + 32:16], T.KF[:, 64 * h:64 * h + 64:32], ["KF.%d" % h, "HB"], ["HB.%d" % h])
         for h in range(4):
             c = slice(32 * h, 32 * h + 32)
-            scan(T.HS[:, c], T.hold[:, c], T.HB[:, c], 0.0, OP.mult, OP.add, ["hold", "HB.%d" % h], ["HS.%d" % h])
-        mm(T.TG[:, 8, 0:8], T.HB[:, 1:129], T.dp[:], False, False, four("HB.") + ["dp"], ["TG"])
-        mm(T.TG[:, 8, 0:8], T.HS[:, 0:128], T.dp[:], False, False, four("HS.") + ["dp"], ["TG"])
-        mm(T.TG[:, 8, 0:8], T.HS[:, 1:129], T.dn[:], False, True, four("HS.") + ["HS", "dn"], ["TG"])
+            tt(T.HS[:, c], T.KF[:, 2 * h:2 * h + 2, 0:16], T.mine[:, c], OP.mult, ["mine", "KF.%d" % h], ["HS.%d" % h])
+        mm(T.TG[:, 8, 0:8], T.HS[:], T.dp[:], False, True, four("HS.") + ["dp"], ["TG"])
+        for h in range(2):
+            mm(part("OB", 256 + 128 * h, 128), half("LT", h), ident("1"), h == 0, h == 1, ["LT", "ID.1"], ["OB"])
+        act(T.LTt[:], part("OB", 256, 256), AF.Identity, ["OB"], ["LTt", "rs"], scale=-1.0, acc=T.rs[:, 0:1])
+        if t == 0:
+            late_constants(1)
+        fill_names(0)
         cp(T.J[:], T.TG[:, 8, 0:8], ["TG"], ["J"])
+        fill_names(1)
         keys("yg", "Y", 0, 0)
-        if last:
-            sums(3, "X2")
-            keep_sums(3, "X2")
         send(3, t, T.J[:], T[JB][:], ["J"], [JB])
+        mm(part("X0", 0, 256), ident("big"), T.LT[:], False, False, ["LT", "ID.big"], ["X0"])
+        mm(part("TG", 0, 256), T.ones[:], T.CT[:], True, False, ["ones", "CT.c"], ["TG"])
         cp(T.M[:], T.xg[:, 0:4096].indirect(T.J[:, 0:8]), allkeys("xg") + ["J"], ["M"])
         tt(T.ge[:], T.xg[:, 0:4096].indirect(T.J[:, 0:8]), T.ZC[:], OP.is_ge, allkeys("xg") + ["J", "ZC"], ["ge"])
         tt(T.xs[:], T.X[:, 0:8192].indirect(T.offX[:, 0:8]), T.M[:], OP.subtract, XK + ["offX", "M"], ["xs"])
         for j in (2, 1, 0):
             mm(YB[j][:], T.M[:], T.WR[:, 16 * j:16 * j + 16, :], False, True, ["M", "WR"], ["Y%d" % j])
             if j == 2:
-                mm(part("TG", 0, 128), T.B16[:], T.ge[:], True, True, ["ge", "B16"], ["TG"])
-        cp(T.cY[:, 1024:1536], T.Y2[:], ["Y2"], ["cY.2"])
-        act(T.fr[:], part("TG", 0, 128), AF.Relu, ["TG"], ["fr"], bias=-6.0)
-        act(T.cY[:, 512:1024], T.Y1[:], AF.Copy, ["Y1"], ["cY.1"])
-        act(T.nf[:], part("TG", 0, 128), AF.Relu, ["TG"], ["nf"], bias=7.0, scale=-1.0)
-        cp(T.cY[:, 0:512], T.Y0[:], ["Y0"], ["cY.0"])
-        sign_marks("OB", 256, LB)
-        sign_whole("OB", 256, "fr")
-        sign_levels("OB", 256, "cY", 2, False)
-        mm(part("Y2", 256, 128), ident("-64"), T.fr[:], True, False, ["ID.-64", "fr"], ["Y2"])
-        for h in range(2):
-            mm(part("Y2", 256, 128), T.OT[:, h, :], half("LTt", h), False, h == 1, ["OT", "LTt"], ["Y2"])
-        act(T.mm[:], part("Y2", 256, 128), AF.Relu, ["Y2"], ["mm"], bias=32.0)
-        cp(T.y0[:], T.yg[:, 0:4096].indirect(T[JB][:, 0:8]), allkeys("yg") + [JB], ["y0"])
-        sign_levels("OB", 256, "cY", 1, False)
-        sign_levels("OB", 256, "cY", 0, True)
-        for j in (1, 0, 2):
-            mm(XB[j][:], T.y0[:], T.WR[:, 16 * j:16 * j + 16, :], j > 0, True, ["y0", "WR"], ["X%d" % j])
+                mm(part("X2", 0, 128), T.B16[:], T.ge[:], True, True, ["ge", "B16"], ["X2"])
         ts(T.xh[:], T.xs[:], 0.5, 127.25, OP.mult, OP.add, ["xs"], ["xh"])
+        cp(T.cY[:, 1024:1536], T.Y2[:], ["Y2"], ["cY.4", "cY.5"])
         if last:
             tt(T.xd[:], T.X[:, 0:8192].indirect(T.offX[:, 0:8]), T.xh[:], OP.subtract, XK + ["offX", "xh"], ["xd"])
-        act(T.KB[:], part("OB", 256, 256), AF.Sign, ["OB"], ["KB"], bias=-2.0 ** -70)
-        act(T.cA[:, 0:512], T.X0[:], AF.Copy, ["X0"], ["cA.0"])
-        act(T.s2[:], part("OB", 256, 256), AF.Sign, ["OB"], ["s2"], bias=BIG1 / 2)
-        sign_marks("Y0", 0, "LT")
-        sign_whole("Y0", 0, "nf")
-        blocks("Y1", 0, [("LTt", "LM", LS, "own")], False, True)
-        for j in (1, 2):
-            tt(T.cA[:, 512 * j:512 * j + 512], XB[j][:], T.NV[:, 512 * j:512 * j + 512], OP.add,
-               ["X%d" % j, "NV.%d" % j] + four("NV.%d" % (j + 3)), ["cA.%d" % j])
-            early(j - 1)
-        sign_levels("Y0", 0, "cA", 1, False)
-        mm(part("X1", 0, 256), T.mm[:], T.BD[:, 0, :, :], True, False, ["mm", "BD.-1/16"], ["X1"])
-        sign_levels("Y0", 0, "cA", 0, False)
-        sign_levels("Y0", 0, "cA", 2, True)
-        blocks("Y1", 0, [("KB", "OM", OS, "-1/2"), ("s2", "OM", OS, "1/2")], True)
-        blocks("X1", 0, [("KB", "LM", LS, "got")], False)
-        if not last:
-            cp(T.X[:, 0:8192].indirect(T.offX[:, 0:8]), T.xh[:], ["xh", "offX"], XK)
-        early(2)
-        early(3)
-        ts(T.KA[:], part("Y0", 0, 256), 0.0, -2.0, OP.is_gt, OP.mult, ["Y0"], ["KA"])
-        blocks("X1", 0, [("KA", "OM", OS, "1/2")], True)
-        tt(T.DA[:], part("Y1", 0, 256), T.rows[:, 0, :], OP.add, ["Y1", "rows"], ["DA"])
-        early(4)
-        for s in (5, 4, 3):
-            quot("A", s, 0, "DA")
+        early(0)
+        act(T.fr[:], part("X2", 0, 128), AF.Relu, ["X2"], ["fr"], bias=-6.0)
+        act(T.nf[:], part("X2", 0, 128), AF.Relu, ["X2"], ["nf"], bias=7.0 * 256, scale=-256.0)
+        act(T.cY[:, 512:1024], T.Y1[:], AF.Copy, ["Y1"], ["cY.2", "cY.3"])
+        sign_whole("OB", 256, "fr")
+        mm(part("X2", 0, 128), ident("-64"), T.fr[:], True, False, ["ID.-64", "fr"], ["X2"])
+        for h in range(2):
+            mm(part("X2", 0, 128), T.OT[:, h, :], half("LTt", h), False, h == 1, ["OT", "LTt"], ["X2"])
+        act(T.mm[:], part("X2", 0, 128), AF.Relu, ["X2"], ["mm"], bias=32.0)
+        act(T.cY[:, 0:512], T.Y0[:], AF.Copy, ["Y0"], ["cY.0", "cY.1"])
+        sign_levels("OB", 256, "cY", (4, 5), False)
         mm(part("Y2", 0, 256), T.ones[:], T.CT[:], True, False, ["ones", "CT.c"], ["Y2"])
-        ts(T.DB[:], part("X1", 0, 256), 63.5, None, OP.add, None, ["X1"], ["DB"])
-        early(5)
-        mm(part("X0", 0, 256), T.ones[:], T.CT[:], True, False, ["ones", "CT.c"], ["X0"])
-        blocks("X0", 0, [("KA", "ID", IDS, "-1/128")], False)
-        mm(part("X0", 0, 256), ident("1/2"), T.DA[:], False, False, ["ID.1/2", "DA"], ["X0"])
-        quot("V", 1, 0, "DA")
-        for s in range(1, 6):
-            quot("V", s, 1, "DB")
-        early(6)
-        quot("V", 2, 0, "DA")
+        tt(T.y0[:], T.yg[:, 0:4096].indirect(T[JB][:, 0:8]), T.nf[:], OP.add, allkeys("yg") + [JB, "nf"], ["y0"])
+        early(1)
+        tt(T.zd[:], T.yg[:, 0:4096].indirect(T[JB][:, 0:8]), T.Z[:], OP.add, allkeys("yg") + [JB, "Z"], ["zd"])
+        sign_levels("OB", 256, "cY", (2, 3), False)
+        blocks("Y1", 0, [("LTt", "LM", LS, "own")], False, True)
+        for j in (1, 0, 2):
+            mm(XB[j][:], T.y0[:], T.WR[:, 16 * j:16 * j + 16, :], j > 0, True, ["y0", "WR"], ["X%d" % j])
+        sign_marks("OB", 256, LB)
+        sign_levels("OB", 256, "cY", (0, 1), True)
+        for c in range(2):
+            act(T.cA[:, 256 * c:256 * c + 256], part("X0", 256 * c, 256), AF.Copy, ["X0"], ["cA.%d" % c])
+        act(T.KB[:], part("OB", 256, 256), AF.Sign, ["OB"], ["KB"], bias=-2.0 ** -70)
+        act(T.s2[:], part("OB", 256, 256), AF.Sign, ["OB"], ["s2"], bias=BIG1 / 2)
+        act(T.zd[:] if last else T.Z[:], T.zd[:], AF.Abs, ["zd"], ["zd" if last else "Z"], bias=-255.0)
+        if last:
+            dma("S", T.yz[:], T.zd[:], ["zd"], [])
+        early(2)
+        for c in range(2, 6):
+            j = c // 2
+            tt(T.cA[:, 256 * c:256 * c + 256], part("X%d" % j, 256 * (c % 2), 256), T.NV[:, 256 * c:256 * c + 256], OP.add,
+               ["X%d" % j, "NV.%d" % j] + four("NV.%d" % (j + 3)), ["cA.%d" % c])
+            early(c + 1)
         early(7)
         if last:
             dma("S", T.yx[:], T.S[:], ["S"], [])
-        mm(part("Y2", 0, 256), ident("1/2"), T.DB[:], False, False, ["ID.1/2", "DB"], ["Y2"])
-        for s in range(1, 6):
-            quot_add("Y2", s, 1, s == 5)
-        for s in (1, 5, 4, 2, 3):
-            quot_add("X0", s, 0, s == 3)
-        if t == 0:
-            fill_names(0)
-            late_constants(3)
-            fill_names(1)
-        mm(part("Y0", 256, 128), ident("1"), T.y0[:], True, False, ["ID.1", "y0"], ["Y0"])
-        mm(part("Y0", 256, 128), ident("1"), T.Z[:], False, True, ["ID.1", "Z"], ["Y0"])
-        mm(part("X2", 0, 256), T.ones[0:1, :], T.rows[0:1, 1, :], True, False, ["ones", "rows"], ["X2"])
-        blocks("X2", 0, [("KB", "OM", OS, "-1/2"), ("KA", "OM", OS, "1/2")], True)
-        if not last:
-            act(T.Z[:], part("Y0", 256, 128), AF.Abs, ["Y0"], ["Z"], bias=-255.0)
-        act(T.nr[:], part("X2", 0, 256), AF.Relu, ["X2"], ["nr"])
+        sign_levels("Y0", 0, "cA", (2, 0, 3, 4, 1, 5), True, True)
+        blocks("X1", 0, [("KB", "LM", LS, "got")], False, True)
+        mm(part("X1", 0, 256), T.mm[:], T.BD[:, 0, :, :], False, False, ["mm", "BD.-1/16"], ["X1"])
+        blocks("Y1", 0, [("KB", "OM", OS, "-1/2"), ("s2", "OM", OS, "1/2")], True)
+        new_columns(0)
+        for h in range(2):
+            ts(half("KA", h), part("Y0", 128 * h, 128), 0.0, -2.0, OP.is_gt, OP.mult, ["Y0"], ["KA.%d" % h])
+        blocks("X1", 0, [("KA", "OM", OS, "1/2")], True)
+        tt(T.DA[:], part("Y1", 0, 256), T.rows[:, 0, :], OP.add, ["Y1", "rows"], ["DA.0", "DA.1"])
+        for h in range(2):
+            ts(half("DB", h), part("X1", 128 * h, 128), 63.5, None, OP.add, None, ["X1"], ["DB.%d" % h])
+        blocks("Y2", 0, [("KA", "ID", IDS, "-1/128")], False)
         if not last:
             make_u(0)
-            mm(T.X1[:, 256:257], T.onesf[:], T.rs[:, 0:1], True, True, ["onesf", "rs"], ["X1"])
-            act(T.kc[:, 0:1], T.X1[:, 256:257], AF.Identity, ["X1"], ["kc"], bias=4096.0 * 33 - 2.0 ** 23)
-        else:
-            act(T.zd[:], part("Y0", 256, 128), AF.Abs, ["Y0"], ["zd"], bias=-255.0)
-            dma("S", T.yz[:], T.zd[:], ["zd"], [])
+        for lst, s in (("B", 5), ("A", 5), ("A", 4)):
+            quot("A", s, lst)
+        for h in range(2):
+            for s in range(1, 5):
+                quot("V", s, "B", h)
+        for s in (1, 2, 3):
+            quot("V", s, "A")
+        for h in range(2):
+            quot_add("TG", "B", h, (0, 1, 2, 3, 4))
+        quot_add("TG", "B", None, (5,), True)
+        quot_add("Y2", "A", None, (0, 1, 5, 2, 3, 4), True)
+        mm(part("X2", 0, 256), T.ones[0:1, :], T.rows[0:1, 1, :], True, False, ["ones", "rows"], ["X2"])
+        blocks("X2", 0, [("KB", "OM", OS, "-1/2"), ("KA", "OM", OS, "1/2")], True)
+        act(T.nr[:], part("X2", 0, 256), AF.Relu, ["X2"], ["nr"])
+        fill_names(2)
+        if not last:
+            mm(T.OB[:, 256:257], T.onesf[:], T.rs[:, 0:1], True, True, ["onesf", "rs"], ["OB"])
+            act(T.kc[:, 0:1], T.OB[:, 256:257], AF.Identity, ["OB"], ["kc"], bias=4096.0 * 33 - 2.0 ** 23)
+            make_u(1)
 
         def step(h, s):
             if s < 0:
-                src, bk, even, odd = (("VA", "X0", T.X0[:, 0:256:2], T.X0[:, 1:256:2]), (VB, "Y2", T.Y2[:, 0:8, 0::2], T.Y2[:, 0:8, 1::2]))[h]
-                tt(T.E0[:, 8 * h:8 * h + 8, :], even, T[src][:, 0, :], OP.add, [bk, src + ".0"], ["E0.%d" % h])
-                tt(T.Y1[:, 8 * h:8 * h + 8, 0:16], odd, T[src][:, 1, :], OP.add, [bk, src + ".1"], ["Y1.%d" % h])
+                src, bk = (("VA", "Y2"), (VB, "TG"))[h]
+                tt(T.E0[:, 8 * h:8 * h + 8, :], T[bk][:, 0:8, 0::2], T[src][:, 0], OP.add, [bk, src + ".0"], ["E0.%d" % h])
+                tt(T.Y1[:, 8 * h:8 * h + 8, 0:16], T[bk][:, 0:8, 1::2], T[src][:, 1], OP.add, [bk, src + ".1"], ["Y1.%d" % h])
             elif s < 4:
                 stage(s, h)
             else:
                 o, key = ((T.TG, "TG"), (T.BP, "BP"))[h]
                 for hi, alu in ((0, OP.min), (1, OP.max)):
                     tt(o[:, 0:8, 16 * hi:16 * hi + 16], T.E0[:, 8 * h:8 * h + 8, :], T.Y1[:, 8 * h:8 * h + 8, 0:16], alu,
-                       ["E0.%d" % h, "Y1.%d" % h], [key])
+                       ["E0.%d" % h, "Y1.%d" % h], ["%s.s%d" % (key, hi)])
         step(1, -1)
-        fill = T.Y2[:, 8:16, :]
-        mm(fill, T.ones[0:1, :], T.topf[0:1, :], True, False, ["ones", "topf"], ["Y2"])
+        new_columns(1)
+        fill = T.Y0[:, 8:16, :]
+        mm(fill, T.ones[0:1, :], T.topf[0:1, :], True, False, ["ones", "topf"], ["Y0"])
         for e in range(2):
-            mm(T.Y2[:, 8:16, e::2], T.fbf[:, 128 * e:128 * e + 128], T.IDN[:], False, False, ["fbf", "IDN"], ["Y2"])
-        if not last:
-            make_u(1)
+            mm(T.Y0[:, 8:16, e::2], T.fbf[:, 128 * e:128 * e + 128], T.IDN[:], False, False, ["fbf", "IDN"], ["Y0"])
         for e in range(2):
-            mm(T.Y2[:, 8:16, e::2], T.gf[:, 128 * e:128 * e + 128], ident("-1/128"), False, False, ["gf", "ID.-1/128"], ["Y2"])
-        mm(fill, ident("1"), T.nr[:], False, True, ["ID.1", "nr"], ["Y2"])
+            mm(T.Y0[:, 8:16, e::2], T.gf[:, 128 * e:128 * e + 128], ident("-1/128"), False, False, ["gf", "ID.-1/128"], ["Y0"])
+        mm(fill, ident("1"), T.nr[:], False, True, ["ID.1", "nr"], ["Y0"])
         for s in range(5):
             step(1, s)
             step(0, s - 1)
             if s == 0 and not last:
                 turn_init(OWN, 0)
             if s == 0 and t == RO - 2:
-                for j, bk in enumerate(("X0", "Y0")):
+                for j, bk in enumerate(("Y2", "X0")):
                     sums(j, bk)
                     keep_sums(j, bk)
-        halves = [slice(1, 32, 2), slice(0, 32, 2)] if not last else [slice(0, 16), slice(16, 32)]
-        tt(T.v1[:, :, halves[0]], T.BP[:, :, halves[0]], T.Y2[:, 8:16, halves[0]], OP.min, ["BP", "Y2"], ["v1.0"])
+        for hi in range(2):
+            c = slice(16 * hi, 16 * hi + 16)
+            tt(T.v1[:, :, c], T.BP[:, :, c], T.Y0[:, 8:16, c], OP.min, ["BP.s%d" % hi, "Y0"], ["v1.%d" % hi])
         step(0, 4)
-        tt(T.v1[:, :, halves[1]], T.BP[:, :, halves[1]], T.Y2[:, 8:16, halves[1]], OP.min, ["BP", "Y2"], ["v1.1"])
         if not last:
-            for b, e in enumerate((1, 0)):
-                tt(T.VA[:, e, :], T.v1[:, :, halves[b]], T.TG[:, 0:8, halves[b]], OP.min, ["v1.%d" % b, "TG"], ["VA.%d" % e])
+            for e, hi in ((1, 0), (1, 1), (0, 0), (0, 1)):
+                c = slice(16 * hi + e, 16 * hi + 16, 2)
+                tt(T.VA[:, e, :, 8 * hi:8 * hi + 8], T.v1[:, :, c], T.TG[:, 0:8, c], OP.min, ["v1.%d" % hi, "TG.s%d" % hi], ["VA.%d" % e])
+            for e in (1, 0):
                 send_names(t + 1, e)
             turn_own()
         else:
             turn_init(OWN, 4, (0, 1))
             for b in range(2):
-                tt(T.VL[:, 128 * b:128 * b + 128], T.v1[:, :, halves[b]], T.TG[:, 0:8, halves[b]], OP.min, ["v1.%d" % b, "TG"], ["VL.%d" % b])
+                c = slice(16 * b, 16 * b + 16)
+                tt(T.VL[:, 128 * b:128 * b + 128], T.v1[:, :, c], T.TG[:, 0:8, c], OP.min, ["v1.%d" % b, "TG.s%d" % b], ["VL.%d" % b])
                 mm(part(OWN[b][0], 0, 128), T.VL[:, 128 * b:128 * b + 128], T.IU[:], False, True, ["VL.%d" % b, "IU"], [OWN[b][0]])
             act(half("amf", 0), part(OWN[0][0], 0, 128), AF.Copy, [OWN[0][0]], ["amf.0"])
             cp(half("amf", 1), part(OWN[1][0], 0, 128), [OWN[1][0]], ["amf.1"])
-            dma("S", T.ya[:], T.amf[:], ["amf.0", "amf.1"], [])
+            dma("A", T.ya[:, 0:128], half("amf", 0), ["amf.0"], [])
+            dma("S", T.ya[:, 128:256], half("amf", 1), ["amf.1"], [])
     plan["emit"](g, T)

from concourse.bass import DstId, RemoteDMATransfer
from concourse.mybir import dt, AluOpType, AxisListType, ActivationFunctionType

OP = AluOpType
AF = ActivationFunctionType
RO = 3
BIG1 = 2.0 ** 90
BIG2 = 2.0 ** 98
HUGE = 2.0 ** 99
DOWN = 2.0 ** -20
UP = 2.0 ** 20
MAGIC = 1.5 * 2.0 ** 23
SPLIT = (64, 52)
SHARE = 10
NENG = 8

F, B, I, U = "float32", "bfloat16", "int32", "uint16"


def _s(shape, d):
    return ("sbuf", [128] + list(shape), d)


IDS = {"1": 1.0, "big": BIG2, "1/2": 0.5, "-1024": -1024.0, "-64": -64.0, "-1/128": -1.0 / 128,
       "g1": -96.0 / 128, "g2": -48.0 / 128, "g3": -24.0 / 128, "g4": -12.0 / 128, "g5": -7.0 / 128}
OS = {"1/2": 0.5, "-1/2": -0.5}
LS = ["own", "got"]
BDS = {"-1/16": -1.0 / 16, "big": -BIG1 / 16}
ROWS = {"own": (1, 0), "len": (-1, 48)}
TOPS = [(0, -4096.0), (1, -4096.0), (0, 32.0), (1, 32.0), (0, 0.0), (1, 0.0)]

SCRATCH = {
    "X": _s([8192], B), "xg": _s([4096], B), "yg": _s([4096], B), "S": _s([2048], F),
    "ami": _s([256], I), "amf": _s([256], F), "Z": _s([128], B), "ZC": _s([128], B), "wi": _s([8], I), "wf": _s([8], F),
    "VA": _s([2, 8, 16], F), "VL": _s([256], F), "VB0": _s([2, 8, 16], F), "VB1": _s([2, 8, 16], F), "VB2": _s([2, 8, 16], F),
    "LT": _s([256], B), "LB0": _s([256], B), "LB1": _s([256], B), "LB2": _s([256], B),
    "J": _s([8], U), "JB0": _s([8], U), "JB1": _s([8], U), "JB2": _s([8], U),
    "h1": _s([256], I), "h2": _s([256], I), "offA": _s([256], U), "offB": _s([256], U),
    "ft": _s([256], F), "f1": _s([256], F), "fbf": _s([256], F), "gf": _s([256], B),
    "cm": _s([128], F), "Dm": _s([128], F), "u32": _s([128], F), "gu": _s([128], B),
    "NV": _s([1536], F), "si": _s([8], I), "sj": _s([8], I), "sk": _s([8], F), "offX": _s([8], U),
    "w": _s([256], F), "r0": _s([256], B), "rA": _s([256], B), "rB": _s([256], B), "lt": _s([256], B),
    "LX": _s([8, 48], B), "KF": _s([8, 48], F), "inc": _s([8, 48], F), "HS": _s([128], F), "mine": _s([128], F),
    "M": _s([128], B), "y0": _s([128], B), "ge": _s([128], B),
    "fr": _s([128], B), "nf": _s([128], B), "mm": _s([128], B), "LTt": _s([256], B), "KA": _s([256], B), "KB": _s([256], B), "s2": _s([256], B),
    "sl": _s([8], F), "offS": _s([8], U), "xs": _s([128], B), "xh": _s([128], I), "xd": _s([128], F), "BP": _s([8, 32], F), "xp": _s([128], F),
    "cA": _s([1536], B), "cY": _s([1536], B), "DA": _s([256], B), "DB": _s([256], B), "nr": _s([256], B),
    "GA": _s([5, 256], B), "GB": _s([5, 256], B), "E0": _s([16, 16], F), "E1": _s([16, 16], F), "v1": _s([8, 32], F),
    "zd": _s([128], F), "rs": _s([8], F), "kc": _s([8], F),
    "ones": _s([128], B), "zero": _s([256], B), "onesf": _s([128], F), "ID": _s([len(IDS), 128], B), "IU": _s([128], F), "IDN": _s([128], F),
    "OM": _s([len(OS), 128], B), "LM": _s([len(LS), 128], B), "OT": _s([2, 128], B), "tri": _s([128], B), "dia": _s([128], B),
    "pc": _s([16], I), "pf": _s([24], F), "io1": _s([8], F), "io2": _s([128], F), "io3": _s([128], F), "io5": _s([128], F), "io6": _s([8], F),
    "W": _s([48], B), "WR": _s([48, 32], B), "B16": _s([128], B), "BD": _s([len(BDS), 8, 32], B), "BW": _s([128], B), "WZ": _s([144], B),
    "br": _s([8, 32], B), "TP": _s([len(TOPS), 128], B), "CT": _s([256], B),
    "topl": _s([256], B), "topf": _s([256], B), "rows": _s([len(ROWS), 256], B), "urow": _s([128], B),
    "dp": _s([8], F), "jb": _s([8], F), "cx": _s([8], F), "cs": _s([8], F),
    "X0": ("psum", [128, 512], F), "X1": ("psum", [128, 512], F), "X2": ("psum", [128, 512], F),
    "Y0": ("psum", [128, 16, 32], F), "Y1": ("psum", [128, 16, 32], F), "Y2": ("psum", [128, 16, 32], F),
    "TG": ("psum", [128, 16, 32], F), "OB": ("psum", [128, 512], F),
}
PSUM = ("X0", "X1", "X2", "Y0", "Y1", "Y2", "TG", "OB")
SEMAPHORES = ["eV", "eA", "eP", "eG"] + ["d%d" % k for k in range(16)] + ["l%d" % k for k in range(12)] + ["a%d" % k for k in range(12)]


def make_plan():
    ops, lastw, readers, bank, out = [], {}, {}, {}, {}

    def op(eng, fn, R=(), W=(), sem=None, inc=None):
        k = len(ops)
        own = sem is not None
        deps = set()

        def other(j):
            return own or ops[j]["sem"] is not None or ops[j]["eng"] != eng
        for r in R:
            j = lastw.get(r)
            if j is not None and (other(j) or eng != "P"):
                deps.add(j)
        for x in W:
            j = lastw.get(x)
            if j is not None and other(j):
                deps.add(j)
            for j in readers.get(x, ()):
                if other(j):
                    deps.add(j)
        for x in set(R) | set(W):
            b = x.split(".")[0]
            if b in PSUM:
                for e, j in bank.setdefault(b, {}).items():
                    if e != eng:
                        deps.add(j)
                bank[b][eng] = k
        for r in R:
            readers.setdefault(r, []).append(k)
        for x in W:
            lastw[x] = k
            readers[x] = []
        ops.append({"eng": eng, "fn": fn, "deps": deps, "sem": sem, "inc": inc})
        return k

    def emit(g, T):
        q = {"V": g.vector, "A": g.scalar, "P": g.tensor, "G": g, "S": g.sync}
        known = {e: {} for e in q}
        for k, o in enumerate(ops):
            o["key"] = o["sem"] if o["sem"] is not None else o["eng"]
            o["need"] = False
            if o["fn"] is None:
                o["clock"] = {o["key"]: k}
                o["waits"] = []
                continue
            kn = known[o["eng"]]
            waits = []
            for j in sorted(o["deps"], reverse=True):
                if kn.get(ops[j]["key"], -1) >= j:
                    continue
                waits.append(j)
                ops[j]["need"] = True
                for key, val in ops[j]["clock"].items():
                    if kn.get(key, -1) < val:
                        kn[key] = val
            o["waits"] = waits
            o["clock"] = dict(kn)
            o["clock"][o["key"]] = k
        count = {}
        for o in ops:
            if o["sem"] is not None:
                o["wait"] = (o["sem"], o["inc"])
                count[o["sem"]] = o["inc"]
            elif o["need"]:
                name = "e" + o["eng"]
                count[name] = count.get(name, 0) + 1
                o["wait"] = (name, count[name])
        for o in ops:
            if o["fn"] is None:
                continue
            for j in o["waits"]:
                q[o["eng"]].wait_ge(T.sem[ops[j]["wait"][0]], ops[j]["wait"][1])
            ins = o["fn"]()
            if o["sem"] is not None:
                if o["sem"][0] == "d":
                    ins.then_inc(T.sem[o["sem"]], 16)
            elif o["need"]:
                ins.then_inc(T.sem[o["wait"][0]], 1)
        for name, val in count.items():
            g.sync.wait_ge(T.sem[name], val)
    out["op"], out["emit"] = op, emit
    return out


def rank_program(g, core, T, topo):
    rank = T.rank_of(core)
    if rank is None:
        return
    N = len(T.cores)
    plan = make_plan()
    op = plan["op"]
    v, a, pe = g.vector, g.scalar, g.tensor
    nd = [0]

    def tt(o, x, y, alu, R, W):
        op("V", lambda: v.tensor_tensor(o, x, y, alu), R, W)

    def ts(o, x, s1, s2, o0, o1, R, W):
        if o1 is None:
            op("V", lambda: v.tensor_scalar(o, x, s1, None, o0), R, W)
        else:
            op("V", lambda: v.tensor_scalar(o, x, s1, s2, o0, o1), R, W)

    def cp(o, x, R, W):
        op("V", lambda: v.tensor_copy(o, x), R, W)

    def ms(o, c, W, R=()):
        op("V", lambda: v.memset(o, c), R, W)

    def scan(o, x, y, first, o0, o1, R, W):
        op("V", lambda: v.tensor_tensor_scan(o, x, y, first, o0, o1), R, W)

    def act(o, x, f, R, W, bias=0.0, scale=1.0, acc=None):
        if acc is not None:
            op("A", lambda: a.activation(o, x, f, scale=scale, accum_out=acc), R, W)
        elif f == AF.Copy:
            op("A", lambda: a.activation(o, x, f), R, W)
        else:
            op("A", lambda: a.activation(o, x, f, bias=bias, scale=scale), R, W)

    def mm(o, l, r, st, sp, R, W):
        op("P", lambda: pe.matmul(o, l, r, st, sp), R, W)

    def dma(eng, o, x, R, W):
        qq = {"S": g.sync, "A": g.scalar, "G": g}[eng]
        name = "d%d" % nd[0]
        nd[0] += 1
        op(eng, lambda: qq.dma_start(o, x), R, W, sem=name, inc=16)

    def iota(o, pat, base, ch, W, flt=True):
        if flt:
            op("G", lambda: g.iota(o, pat, base, ch, allow_small_or_imprecise_dtypes=True), (), W)
        else:
            op("G", lambda: g.iota(o, pat, base, ch), (), W)

    def select(o, x, pat, alu, fill, base, ch, R, W):
        op("G", lambda: g.affine_select(o, x, pat, alu, fill, base, ch), R, W)

    def send(k, t, src, dst, R, W):
        to = T.cores[(rank + 1 + t % (N - 1)) % N]
        fr = T.cores[(rank - 1 - t % (N - 1)) % N]
        eng = topo.engines(core, to)[:NENG]
        mask = sum(1 << e for e in eng)
        rid, pid = topo.addr(to)[:2]
        n = 4 * t + k
        op("G", lambda: g.remote_dma(dst, src, T.sem["a%d" % n], T.sem["l%d" % n], pid, rid, mask), R, [], sem="l%d" % n, inc=len(eng))
        op("G", None, [], W, sem="a%d" % n, inc=len(topo.engines(fr, core)[:NENG]))

    def send_names(t, e):
        send(e, t, T.VA[:, e, :], T["VB%d" % t][:, e, :], ["VA.%d" % e], ["VB%d.%d" % (t, e)])

    XB, YB = [T.X0, T.X1, T.X2], [T.Y0, T.Y1, T.Y2]

    def lev(l):
        return XB[l % 3][:, (l // 3) * 256:(l // 3) * 256 + 256]

    def pick(buf, names, name):
        return T[buf][:, list(names).index(name)]

    def ident(name):
        return pick("ID", IDS, name)

    def part(bk, c0, n):
        if bk in ("X0", "X1", "X2", "OB"):
            return T[bk][:, c0:c0 + n]
        return T[bk][:, c0 // 32:(c0 + n) // 32, :]

    def half(name, h):
        return T[name][:, 128 * h:128 * h + 128]

    def quarter(name, h):
        return T[name][:, 64 * h:64 * h + 64]

    def four(name):
        return ["%s%d" % (name, h) for h in range(4)]

    dma("S", T.ami[:], T.am[:], [], ["ami"])
    dma("A", T.Z[:], T.zv[:], [], ["Z"])
    dma("A", T.wi[:, 0:1], T.wt[:], [], ["wi"])
    dma("S", T.X[:, 0:4096], T.xt[:, 0:4096], [], ["X.a"])
    dma("A", T.X[:, 4096:8192], T.xt[:, 4096:8192], [], ["X.b"])
    XK = ["X.a", "X.b"]

    def diagonals(which):
        for n_ in which:
            select(ident(n_), T.zero[:, 0:128], [[-1, 128]], OP.not_equal, IDS[n_], 0, 1, ["zero"], ["ID." + n_])

    def key_weights(rows):
        for p in rows:
            l = p // 3
            c0 = 16 * (l % 3) + 8 * (l // 3)
            select(T.W[:, c0:c0 + 8], T.W[:, c0:c0 + 8], [[-16, 8]], OP.not_equal, 2.0 ** (48 - 25 * l + 8 * (2 - p % 3)), -p, 1,
                   ["W.%d" % l, "W"], ["W.%d" % l])

    def tops(which):
        for n_ in which:
            e, c = TOPS[n_]
            act(T.TP[0:1, n_, :], T.br[0:1, :, 0::2] if c else T.br[0:1, :, 0:16], AF.Identity, ["br", "TP"], ["TP.%d" % n_], scale=-8192.0)

    ms(T.zero[:], 0.0, ["zero"])
    iota(T.pc[:, 0:1], [[0, 1]], 0, 1, ["pc0"], flt=False)
    iota(T.io1[:], [[1, 8]], 0, 0, ["io1"])
    diagonals(["1"])
    iota(T.io3[:], [[1, 8], [0, 16]], 0, 0, ["io3"])
    ms(T.br[:, :, 0:1], 0.0, ["br"])
    ms(T.W[:], 0.0, ["W"])
    key_weights([0, 3, 6, 9, 12, 15, 1, 4, 7, 10, 13, 2, 5, 8, 11, 14])
    iota(T.io5[:], [[1, 4], [0, 32]], 0, 0, ["io5"])
    between = [lambda: ms(T.ones[:], 1.0, ["ones"]),
               lambda: ts(T.pc[:, 1:2], T.pc[:, 0:1], 15, None, OP.bitwise_and, None, ["pc0"], ["pc1"]),
               lambda: ts(T.pc[:, 2:3], T.pc[:, 0:1], 4, None, OP.arith_shift_right, None, ["pc0"], ["pc1"]),
               lambda: ts(T.pc[:, 3:4], T.pc[:, 0:1], 31, None, OP.bitwise_and, None, ["pc0"], ["pc1"]),
               lambda: ts(T.pc[:, 4:5], T.pc[:, 0:1], 5, None, OP.arith_shift_right, None, ["pc0"], ["pc1"])]
    for s in range(5):
        ts(T.br[:, :, 2 ** s:2 ** (s + 1)], T.br[:, :, 0:2 ** s], float(4 * 2 ** (4 - s)), None, OP.add, None, ["br"], ["br"])
        between[s]()
    ms(T.TP[:], 0.0, ["TP"])
    cp(T.pf[:, 1:5], T.pc[:, 1:5], ["pc1"], ["pf"])
    P_, G_, K_, Q_ = T.pf[:, 1:2], T.pf[:, 2:3], T.pf[:, 3:4], T.pf[:, 4:5]
    act(T.IDN[:], ident("1"), AF.Identity, ["ID.1"], ["IDN"], scale=DOWN)
    act(T.IU[:], ident("1"), AF.Identity, ["ID.1"], ["IU"], scale=UP)
    act(T.topl[0:1, :], T.br[0:1, :, :], AF.Identity, ["br"], ["topl"], scale=2.0 ** -7)
    act(ident("-1024"), ident("1"), AF.Identity, ["ID.1"], ["ID.-1024"], scale=-1024.0)
    tops([1, 0])
    ms(T.urow[0:1, :], 192.0 * 1024, ["urow"])
    ms(T.kc[:, 0:1], 4096.0 * 33 - 2.0 ** 23, ["kc"])
    cp(T.amf[:], T.ami[:], ["ami"], ["amf"])
    cp(T.wf[:, 0:1], T.wi[:, 0:1], ["wi"], ["wf"])
    ms(T.TP[32:33, 1:4:2, :], -64.0 * 8192, ["TP.c"], ["TP"])
    ts(T.BW[:], T.io3[:], G_, T.wf[:, 0:1], OP.is_equal, OP.mult, ["io3", "pf", "wf"], ["BW"])
    ms(T.TP[64:65, 0:2, :], -4096.0, ["TP.c"])
    mm(T.TG[:, 0:8, :], T.ones[0:1, :], T.topl[0:1, :], True, False, ["ones", "topl"], ["TG"])
    for b in range(2):
        mm(T.TG[:, 0:8, 16 * b:16 * b + 16], T.amf[:, 128 * b:128 * b + 128], T.IDN[:], False, b == 1, ["amf", "IDN"], ["TG"])
    ms(T.TP[64:65, 2:4, :], 32.0, ["TP.c"])
    ms(T.TP[32:33, 5, :], -4.0 * 8192, ["TP.c"])
    ms(T.CT[:], 0.0, ["CT"])
    ms(T.WZ[:], 0.0, ["WZ"])
    for e in (1, 0):
        cp(T.VA[:, e, :], T.TG[:, 0:8, e::2], ["TG"], ["VA.%d" % e])
    ts(T.WZ[:, 16::16], T.io1[:], G_, T.wf[:, 0:1], OP.is_equal, OP.mult, ["io1", "pf", "wf", "WZ"], ["WZ"])
    for e in (1, 0):
        send_names(0, e)
    WK = ["W.%d" % l for l in range(6)]

    def make_u(step):
        raw, big, small = part("X0", 0, 128), part("X0", 256, 128), T.Y0[:, 4, 0:8]
        if step == 0:
            mm(raw, T.BW[:], T.Z[:], True, True, ["BW", "Z"], ["X0"])
            act(T.gu[:], raw, AF.Identity, ["X0"], ["gu"], bias=192.0 - 0.5 + 2.0 ** -11, scale=2.0 ** -10)
        if step == 1:
            mm(big, T.urow[0:1, :], T.ones[0:1, :], True, False, ["urow", "ones"], ["X0"])
            mm(big, T.BW[:], T.Z[:], False, False, ["BW", "Z"], ["X0"])
            mm(big, ident("-1024"), T.gu[:], False, True, ["ID.-1024", "gu"], ["X0"])
            act(T.cm[:], big, AF.Identity, ["X0"], ["cm"], bias=33.0, scale=2.0)
            act(T.Dm[:], big, AF.Identity, ["X0", "kc"], ["Dm"], bias=T.kc[:, 0:1], scale=8192.0)
            act(T.u32[:], big, AF.Identity, ["X0"], ["u32"], scale=1.0 / 32)
            act(T.ZC[:], T.Z[:], AF.Identity, ["Z"], ["ZC"], bias=255.0, scale=-1.0)
        if step == 2:
            for r in range(16):
                mm(small, T.WZ[:, 16 - r:144 - r], T.Z[:, r::16], r == 0, r == 15, ["WZ", "Z"], ["Y0"])

    def columns(k):
        if k == 0:
            cp(T.si[:], T.Y0[:, 4, 0:8], ["Y0"], ["si"])
        if k == 1:
            ts(T.sj[:], T.si[:], 63, None, OP.bitwise_and, None, ["si"], ["sj"])
        if k == 2:
            tt(T.sk[:], T.sj[:], T.cx[:], OP.add, ["sj", "cx"], ["sk"])
        if k == 3:
            cp(T.offX[:], T.sk[:], ["sk"], ["offX"])
        if k == 4:
            tt(T.sl[:], T.sj[:], T.cs[:], OP.add, ["sj", "cs"], ["sl"])
        if k == 5:
            cp(T.offS[:], T.sl[:], ["sl"], ["offS"])

    OWN, GOT, FIL = [("X2", 0), ("X1", 0)], [("OB", 256), ("TG", 0)], [("Y2", 0), ("Y2", 128)]

    def turn_init(where, top, es=(1, 0)):
        for e in es:
            bk, c0 = where[e]
            mm(part(bk, c0, 128), T.TP[:, top + e, :], T.ones[:], True, False, ["TP", "TP.c", "TP.%d" % (top + e), "ones"], [bk])

    def turn(where, src, es=(1, 0)):
        for e in es:
            bk, c0 = where[e]
            mm(part(bk, c0, 128), T[src][:, e, :], T.IU[:], False, True, ["%s.%d" % (src, e), "IU"], [bk])

    def hash_step(where, off, step, e, q):
        bk, c0 = where[e]
        c, ln, key = slice(128 * e + 64 * q, 128 * e + 64 * q + 64), slice(64 * q, 64 * q + 64), "%d%d" % (e, q)
        if step == 0:
            tt(part(bk, c0 + 64 * q, 64), part(bk, c0 + 64 * q, 64), T.cm[:, ln], OP.mult, [bk, "cm"], [bk + ".p" + key])
        if step == 1:
            tt(T.h1[:, c], part(bk, c0 + 64 * q, 64), T.Dm[:, ln], OP.add, [bk + ".p" + key, "Dm"], ["h1." + key])
        if step == 2:
            ts(T.h2[:, c], T.h1[:, c], 5, 8191, OP.arith_shift_right, OP.bitwise_and, ["h1." + key], ["h2." + key])
        if step == 3:
            cp(T[off][:, c], T.h2[:, c], ["h2." + key], ["%s.%s" % (off, key)])

    def fill_product(e):
        tt(T.ft[:, 128 * e:128 * e + 128], part("Y2", 128 * e, 128), T.u32[:], OP.mult, ["Y2", "u32"], ["ft"])

    def turn_own():
        turn(OWN, "VA")
        for e in range(2):
            turn_init(FIL, 2, (e,))
            turn(FIL, "VA", (e,))
        make_u(2)
        for step in range(4):
            for e in (1, 0):
                for q in (1, 0):
                    hash_step(OWN, "offA", step, e, q)

    def gather(eng, dst, off, e, i0, i1):
        c0, c1 = 128 * e + i0, 128 * e + i1
        o, x = T[dst][:, 16 * c0:16 * c1], T.X[:, 0:8192].indirect(T[off][:, c0:c1])
        key, R = "%s.%d%s" % (dst, e, eng), XK + ["%s.%d%d" % (off, e, q) for q in range(i0 // 64, (i1 - 1) // 64 + 1)]
        if eng == "V":
            ts(o, x, -1.0, 255.0, OP.mult, OP.add, R, [key])
        else:
            act(o, x, AF.Identity, R, [key], bias=255.0, scale=-1.0)

    def allkeys(dst):
        return ["%s.%d%s" % (dst, e, q) for e in range(2) for q in "VA"]

    def keys(dst, name, e, j, stop=False):
        for r in range(16):
            k = 2 * r + e
            mm(YB[j][:, :, k] if name == "Y" else XB[j][:, k::32], T[dst][:, 2048 * e + r:2048 * e + 2048:16], T.W[:, 16 * j:16 * j + 16],
               e == 1 and r == 0, stop and r == 15, ["%s.%dV" % (dst, e), "%s.%dA" % (dst, e)] + WK, ["%s%d" % (name, j)])

    def blocks(bk, c0, terms, stop, start=False):
        for n_, (src, buf, names, name) in enumerate(terms):
            for h in range(2):
                mm(part(bk, c0 + 128 * h, 128), half(src, h), pick(buf, names, name), start and h == 0 and n_ == 0,
                   stop and h == 1 and n_ == len(terms) - 1, [src, "%s.%d" % (src, h), "%s.%s" % (buf, name)], [bk])

    def sign_marks(bk, c0, marks):
        for h in range(2):
            mm(part(bk, c0 + 128 * h, 128), half(marks, h), ident("big"), False, False, [marks, "ID.big"], [bk])

    def sign_whole(bk, c0, flag):
        for h in range(2):
            mm(part(bk, c0 + 128 * h, 128), T.BD[:, 1, 4 * h:4 * h + 4, :], T[flag][:], h == 0, False, ["BD.big", flag], [bk])

    def sign_levels(bk, c0, src, which, stop, start=False):
        for c in which:
            for h in range(2):
                mm(part(bk, c0 + 128 * h, 128), T[src][:, 256 * c + 128 * h:256 * c + 128 * h + 128], ident("1"), start and c == which[0] and h == 0,
                   stop and c == which[-1] and h == 1, ["%s.%d" % (src, c), "ID.1"], [bk])

    make_u(0)
    turn_init(OWN, 0)
    make_u(1)

    def widen(s):
        act(T.WR[:, :, 2 ** s:2 ** (s + 1)], T.WR[:, :, 0:2 ** s], AF.Copy, ["WR"], ["WR"])
    act(T.WR[:, :, 0:1], T.W[:], AF.Identity, WK, ["WR"], scale=-1.0)
    tops([2, 3])
    widen(0)
    act(T.CT[0:1, :], T.zero[0:1, :], AF.Identity, ["zero", "CT"], ["CT.c"], bias=280.0)
    widen(1)
    act(T.CT[32:33, :], T.br[32:33, :, :], AF.Identity, ["br", "CT"], ["CT.c"], bias=0.5, scale=-1.0 / 128)
    widen(2)
    ms(T.r0[:], 0.0, ["r0"])
    ms(T.w[:, 63::64], HUGE, four("w."))
    ms(T.OB[:, 63:256:64], HUGE, four("OB.w"))
    ms(T.r0[:, 31::32], HUGE, ["r0"], ["r0"])
    fill0 = -131072.0 - 31.0 / 64
    ts(T.pf[:, 8:9], P_, 74.0, fill0, OP.mult, OP.add, ["pf"], ["pf8"])
    ts(T.pf[:, 9:10], P_, 74.0, fill0 + 37, OP.mult, OP.add, ["pf"], ["pf8"])
    ts(T.pf[:, 11:12], P_, 16.0 * DOWN, None, OP.mult, None, ["pf"], ["pf10"])
    ts(T.pf[:, 12:13], P_, 64.0, None, OP.mult, None, ["pf"], ["pf12"])
    ts(T.dp[:], T.io1[:], G_, None, OP.is_equal, None, ["io1", "pf"], ["dp"])
    ts(T.jb[:], T.io1[:], 256.0 * DOWN, T.pf[:, 11:12], OP.mult, OP.add, ["io1", "pf10"], ["jb"])
    ts(T.cx[:], T.io1[:], 1024.0, T.pf[:, 12:13], OP.mult, OP.add, ["io1", "pf12"], ["cx"])
    ts(T.B16[:], T.io3[:], G_, None, OP.is_equal, None, ["io3", "pf"], ["B16"])
    turn_own()
    ts(T.dia[:], ident("1"), K_, 0.5, OP.mult, OP.mult, ["ID.1", "pf"], ["dia"])
    for n_, c in OS.items():
        ts(pick("OM", OS, n_), T.io5[:], Q_, c, OP.is_equal, OP.mult, ["io5", "pf"], ["OM." + n_])
    diagonals(["1/2", "-64"])
    select(T.tri[:], pick("OM", OS, "1/2"), [[1, 128]], OP.is_ge, 0.0, 0, -1, ["OM.1/2"], ["tri"])
    diagonals(["big"])
    iota(T.io2[:], [[0, 8], [1, 16]], 0, 0, ["io2"])
    iota(T.io6[:], [[0, 4], [1024, 2]], 0, 0, ["io6"])
    iota(T.inc[:, :, 16:48], [[0, 128], [-4095, 2]], 2048, 0, ["inc"])
    iota(T.inc[:, :, 0:16], [[0, 128]], 0, 0, ["inc"])
    iota(T.LX[:, :, 0:16], [[0, 128]], 1, 0, ["LX"])
    select(T.OT[:], T.zero[:], [[-128, 2], [32, 8], [0, 16]], OP.is_ge, 1.0, -1, -1, ["zero"], ["OT"])
    select(T.OT[:], T.OT[:], [[-128, 2], [32, 8], [0, 16]], OP.is_ge, 0.0, 31, -1, ["OT"], ["OT"])
    diagonals(["g1", "g2", "g3", "g4", "g5", "-1/128"])
    for n_, (sign, c) in enumerate(ROWS.values()):
        iota(T.rows[:, n_, :], [[0, 8], [sign, 32]], c, 0, ["rows"])
    iota(T.onesf[:], [[0, 128]], -32, 0, ["onesf"])
    first_spare = [
        lambda: ts(pick("LM", LS, "own"), part("Y1", 0, 128), 2.0, None, OP.mult, None, ["Y1"], ["LM.own"]),
        lambda: ts(pick("LM", LS, "got"), part("Y1", 128, 128), -1.0, None, OP.mult, None, ["Y1"], ["LM.got"]),
        lambda: ts(T.mine[:], T.io2[:], P_, None, OP.is_equal, None, ["io2", "pf"], ["mine"]),
        lambda: ts(T.cs[:], T.io6[:], T.pf[:, 12:13], None, OP.add, None, ["io6", "pf12"], ["cs"])]

    def late_constants(k):
        if k == 0:
            for n_ in range(2):
                o = part("Y1", 128 * n_, 128)
                mm(o, ident("1"), T.tri[:], n_ == 0, False, ["ID.1", "tri"], ["Y1"])
                mm(o, ident("1"), T.dia[:], False, False, ["ID.1", "dia"], ["Y1"])
            mm(part("Y1", 128, 128), ident("-64"), ident("1/2"), False, True, ["ID.-64", "ID.1/2"], ["Y1"])
        if k == 1:
            for n_, (name, c) in enumerate(BDS.items()):
                for b in range(2):
                    act(T.BD[:, n_, :, 16 * b:16 * b + 16], T.B16[:], AF.Identity, ["B16"], ["BD." + name], scale=c)

    def sums(j, bk):
        for q in range(4):
            mm(T[bk][:], ident("1"), T.X[:, 2048 * q + 512 * j:2048 * q + 512 * j + 512], q == 0, q == 3, ["ID.1"] + XK, [bk])

    def keep_sums(j, bk):
        act(T.S[:, 512 * j:512 * j + 512], T[bk][:], AF.Copy, [bk], ["S"])

    def patch(k):
        q = k // 2
        win, c = T.S[:, 0:2048].indirect(T.offS[:, 2 * q:2 * q + 2]), slice(32 * q, 32 * q + 32)
        if k % 2 == 0:
            tt(T.xp[:, c], win, T.xd[:, c], OP.subtract, ["S", "offS", "xd"], ["xp"])
        else:
            cp(win, T.xp[:, c], ["xp", "offS"], ["S"])

    def span(h):
        return (0, 256, (0, 1)) if h is None else (128 * h, 128, (h,))

    def quot(eng, s, lst, h=None):
        c0, n, hs = span(h)
        o, x, off = T["G" + lst][:, s - 1, c0:c0 + n], T["D" + lst][:, c0:c0 + n], 192.0 - 0.5 + 2.0 ** -(s + 1)
        R, W = ["D%s.%d" % (lst, k) for k in hs], ["G%s%d.%d" % (lst, s, k) for k in hs]
        if eng == "V":
            ts(o, x, 2.0 ** -s, off, OP.mult, OP.add, R, W)
        else:
            act(o, x, AF.Identity, R, W, bias=off, scale=2.0 ** -s)

    def quot_add(bk, lst, h, which, stop=False):
        c0, n, hs = span(h)
        for s in which:
            name = "g%d" % s if s else "1/2"
            x = T["G" + lst][:, s - 1, c0:c0 + n] if s else T["D" + lst][:, c0:c0 + n]
            mm(part(bk, c0, n), ident(name), x, False, stop and s == which[-1],
               ["ID." + name] + [("G%s%d.%d" % (lst, s, k) if s else "D%s.%d" % (lst, k)) for k in hs], [bk])

    def stage(s, h):
        ei, eo = ("E0", "E1") if s % 2 == 0 else ("E1", "E0")
        ki, ko = ("Y1", "TG") if s % 2 == 0 else ("TG", "Y1")
        c = slice(8 * h, 8 * h + 8)
        for hi, alu in ((0, OP.min), (1, OP.max)):
            for par in range(2):
                ok = eo if par == 0 else ko
                tt(T[ok][:, c, 8 * hi:8 * hi + 8], T[ei][:, c, par::2], T[ki][:, c, par:16:2], alu,
                   ["%s.%d" % (ei, h), "%s.%d" % (ki, h)], ["%s.%d" % (ok, h)])

    for t in range(RO):
        last = t == RO - 1
        VB, LB, JB = "VB%d" % t, "LB%d" % t, "JB%d" % t

        def new_columns(h):
            c = (slice(0, 6), slice(6, 8))[h]
            if not last:
                cp(T.X[:, 0:8192].indirect(T.offX[:, c]), T.xh[:, 16 * c.start:16 * c.stop], ["xh", "offX"], XK)

        def early(k):
            if last:
                patch(k)
        s1, s0 = SPLIT
        gather("A", "xg", "offA", 1, s1, 128)
        gather("A", "xg", "offA", 0, s0, 128)
        turn_init(GOT, 0)
        if t == 0:
            widen(3)
            act(T.topf[0:1, :], T.br[0:1, :, :], AF.Identity, ["br"], ["topf"], bias=1.5, scale=2.0 ** -7)
        if t == 1:
            tops([4, 5])
        if last:
            sums(2, "Y1")
            keep_sums(2, "Y1")
        turn(GOT, VB, (1,))
        gather("V", "xg", "offA", 1, 0, s1)
        turn(GOT, VB, (0,))
        gather("V", "xg", "offA", 0, 0, s0 // 2)
        for step in range(5):
            for e, k in ((1, step), (0, step - 1)):
                if 0 <= k < 4:
                    for q in range(2):
                        hash_step(GOT, "offB", k, e, q)
            if step == 0:
                gather("V", "xg", "offA", 0, s0 // 2, s0)
            if step == 3:
                columns(0)
                fill_product(0)
        fill_product(1)
        spare = [lambda: columns(1), lambda: gather("V", "yg", "offB", 0, 128 - SHARE, 128), lambda: [f() for f in first_spare[0:3] if t == 0],
                 lambda: gather("V", "yg", "offB", 0, 128 - 2 * SHARE, 128 - SHARE)]
        spare += [lambda k=k: columns(k) for k in range(2, 6 if last else 4)]
        if t == 0:
            spare += first_spare[3:]
        gather("A", "yg", "offB", 1, 0, 128)
        for j in range(3):
            keys("xg", "X", 1, j)
        keys("xg", "X", 0, 0, True)
        keys("xg", "X", 0, 1)
        if t == 0:
            late_constants(0)
        r = "r0"
        for l in range(6):
            src, c0, wb = (XB[l], 0, T.w) if l < 3 else (T.NV, 512 * (l - 3) + 256, T.OB)
            kx = ["X%d" % l] * 4 if l < 3 else ["NV.%d%d" % (l, h) for h in range(4)]
            kw = ["w.%d" % h if l < 3 else "OB.w%d" % h for h in range(4)]
            nv = [src[:, c0 + 64 * h:c0 + 64 * h + 64] for h in range(4)]
            w = [wb[:, 64 * h:64 * h + 64] for h in range(4)]
            for h in range(4):
                back = slice(64 * h + 62, 64 * h - 1 if h else None, -1)
                scan(wb[:, back], src[:, c0 + 64 * h + 63:c0 + 64 * h:-1], T[r][:, back], HUGE, OP.min, OP.max,
                     [kx[h], r if l == 0 else "%s.%d" % (r, h)], [kw[h]])
            if spare:
                spare.pop(0)()
            if l == 2:
                gather("A", "yg", "offB", 0, 0, 128 - 2 * SHARE)
            if l == 3 and t == 0:
                widen(4)
            if l < 5:
                for h in range(4):
                    tt(quarter("lt", h), nv[h], w[h], OP.is_gt, [kx[h], kw[h]], ["lt.%d" % h])
                    if l < 2 and h % 2:
                        mm(XB[l + 1][:, 64 * h - 64:64 * h + 64], ident("big"), half("lt", h // 2), False, h == 3,
                           ["ID.big", "lt.%d" % (h - 1), "lt.%d" % h], ["X%d" % (l + 1)])
                if l == 0:
                    keys("xg", "X", 0, 2)
                if l == 1 and last:
                    sums(3, "TG")
                if l == 2:
                    if last:
                        keep_sums(3, "TG")
                    for j in range(3):
                        keys("yg", "Y", 1, j)
                r = "rA" if l % 2 == 0 else "rB"
                tt(T[r][:], wb[:, 0:256], src[:, c0:c0 + 256], OP.subtract, kx + kw, four(r + "."))
                if l >= 2:
                    for h in range(4):
                        c1 = 256 + 64 * h
                        tt(T.NV[:, 512 * (l - 2) + c1:512 * (l - 2) + c1 + 64], XB[l - 2][:, c1:c1 + 64], quarter("lt", h), OP.add,
                           ["X%d" % (l - 2), "lt.%d" % h], ["NV.%d%d" % (l + 1, h)])
                if l == 2:
                    keys("xg", "X", 1, 0)
                    keys("xg", "X", 0, 0)
                if spare:
                    spare.pop(0)()
                if l == 4:
                    for j in (None, 2, 1) if not last else (2, 1, None):
                        if j is None:
                            mm(T.TG[:, 8, 0:8], T.IU[:], T.jb[:], True, False, ["IU", "jb"], ["TG"])
                        else:
                            keys("yg", "Y", 0, j)
            else:
                for h in range(4):
                    tt(T.LX[:, 2 * h:2 * h + 2, 16:48], nv[h], w[h], OP.is_gt, [kx[h], kw[h]], ["LX.%d" % h])
        for l in (1, 2):
            act(T.NV[:, 512 * l:512 * l + 256], lev(l), AF.Copy, ["X%d" % l], ["NV.%d" % l])
            if l == 1:
                act(T.LT[:], T.LX[:, :, 16:48], AF.Copy, four("LX."), ["LT"])

        def fill_names(k):
            if k == 0:
                for e in range(2):
                    ts(half("f1", e), half("ft", e), T.pf[:, 8 + e:9 + e], MAGIC, OP.add, OP.add, ["ft", "pf8"], ["f1"])
            elif k == 1:
                ts(T.fbf[:], T.f1[:], -MAGIC, None, OP.add, None, ["f1"], ["fbf"])
            else:
                act(T.gf[:], T.fbf[:], AF.Identity, ["fbf"], ["gf"], bias=192.0 - 0.5 + 2.0 ** -14, scale=2.0 ** -13)
        send(2, t, T.LT[:], T[LB][:], ["LT"], [LB])
        for gq in range(8):
            scan(T.KF[:, gq, ::-1], T.inc[:, gq, ::-1], T.LX[:, gq, ::-1], 0.0, OP.add, OP.mult, ["inc", "LX", "LX.%d" % (gq // 2)], ["KF.%d" % (gq // 2)])
        while spare:
            spare.pop(0)()
        for h in range(4):
            c = slice(32 * h, 32 * h + 32)
            tt(T.HS[:, c], T.KF[:, 2 * h:2 * h + 2, 0:16], T.mine[:, c], OP.mult, ["mine", "KF.%d" % h], ["HS.%d" % h])
        mm(T.TG[:, 8, 0:8], T.HS[:], T.dp[:], False, True, four("HS.") + ["dp"], ["TG"])
        for h in range(2):
            mm(part("OB", 256 + 128 * h, 128), half("LT", h), ident("1"), h == 0, h == 1, ["LT", "ID.1"], ["OB"])
        act(T.LTt[:], part("OB", 256, 256), AF.Identity, ["OB"], ["LTt", "rs"], scale=-1.0, acc=T.rs[:, 0:1])
        if t == 0:
            late_constants(1)
        fill_names(0)
        cp(T.J[:], T.TG[:, 8, 0:8], ["TG"], ["J"])
        fill_names(1)
        keys("yg", "Y", 0, 0)
        send(3, t, T.J[:], T[JB][:], ["J"], [JB])
        mm(part("X0", 0, 256), ident("big"), T.LT[:], False, False, ["LT", "ID.big"], ["X0"])
        mm(part("TG", 0, 256), T.ones[:], T.CT[:], True, False, ["ones", "CT.c"], ["TG"])
        cp(T.M[:], T.xg[:, 0:4096].indirect(T.J[:, 0:8]), allkeys("xg") + ["J"], ["M"])
        tt(T.ge[:], T.xg[:, 0:4096].indirect(T.J[:, 0:8]), T.ZC[:], OP.is_ge, allkeys("xg") + ["J", "ZC"], ["ge"])
        tt(T.xs[:], T.X[:, 0:8192].indirect(T.offX[:, 0:8]), T.M[:], OP.subtract, XK + ["offX", "M"], ["xs"])
        for j in (2, 1, 0):
            mm(YB[j][:], T.M[:], T.WR[:, 16 * j:16 * j + 16, :], False, True, ["M", "WR"], ["Y%d" % j])
            if j == 2:
                mm(part("X2", 0, 128), T.B16[:], T.ge[:], True, True, ["ge", "B16"], ["X2"])
        ts(T.xh[:], T.xs[:], 0.5, 127.25, OP.mult, OP.add, ["xs"], ["xh"])
        cp(T.cY[:, 1024:1536], T.Y2[:], ["Y2"], ["cY.4", "cY.5"])
        if last:
            tt(T.xd[:], T.X[:, 0:8192].indirect(T.offX[:, 0:8]), T.xh[:], OP.subtract, XK + ["offX", "xh"], ["xd"])
        early(0)
        act(T.fr[:], part("X2", 0, 128), AF.Relu, ["X2"], ["fr"], bias=-6.0)
        act(T.nf[:], part("X2", 0, 128), AF.Relu, ["X2"], ["nf"], bias=7.0 * 256, scale=-256.0)
        act(T.cY[:, 512:1024], T.Y1[:], AF.Copy, ["Y1"], ["cY.2", "cY.3"])
        sign_whole("OB", 256, "fr")
        mm(part("X2", 0, 128), ident("-64"), T.fr[:], True, False, ["ID.-64", "fr"], ["X2"])
        for h in range(2):
            mm(part("X2", 0, 128), T.OT[:, h, :], half("LTt", h), False, h == 1, ["OT", "LTt"], ["X2"])
        act(T.mm[:], part("X2", 0, 128), AF.Relu, ["X2"], ["mm"], bias=32.0)
        act(T.cY[:, 0:512], T.Y0[:], AF.Copy, ["Y0"], ["cY.0", "cY.1"])
        sign_levels("OB", 256, "cY", (4, 5), False)
        mm(part("Y2", 0, 256), T.ones[:], T.CT[:], True, False, ["ones", "CT.c"], ["Y2"])
        tt(T.y0[:], T.yg[:, 0:4096].indirect(T[JB][:, 0:8]), T.nf[:], OP.add, allkeys("yg") + [JB, "nf"], ["y0"])
        early(1)
        tt(T.zd[:], T.yg[:, 0:4096].indirect(T[JB][:, 0:8]), T.Z[:], OP.add, allkeys("yg") + [JB, "Z"], ["zd"])
        sign_levels("OB", 256, "cY", (2, 3), False)
        blocks("Y1", 0, [("LTt", "LM", LS, "own")], False, True)
        for j in (1, 0, 2):
            mm(XB[j][:], T.y0[:], T.WR[:, 16 * j:16 * j + 16, :], j > 0, True, ["y0", "WR"], ["X%d" % j])
        sign_marks("OB", 256, LB)
        sign_levels("OB", 256, "cY", (0, 1), True)
        for c in range(2):
            act(T.cA[:, 256 * c:256 * c + 256], part("X0", 256 * c, 256), AF.Copy, ["X0"], ["cA.%d" % c])
        act(T.KB[:], part("OB", 256, 256), AF.Sign, ["OB"], ["KB"], bias=-2.0 ** -70)
        act(T.s2[:], part("OB", 256, 256), AF.Sign, ["OB"], ["s2"], bias=BIG1 / 2)
        act(T.zd[:] if last else T.Z[:], T.zd[:], AF.Abs, ["zd"], ["zd" if last else "Z"], bias=-255.0)
        if last:
            dma("S", T.yz[:], T.zd[:], ["zd"], [])
        early(2)
        for c in range(2, 6):
            j = c // 2
            tt(T.cA[:, 256 * c:256 * c + 256], part("X%d" % j, 256 * (c % 2), 256), T.NV[:, 256 * c:256 * c + 256], OP.add,
               ["X%d" % j, "NV.%d" % j] + four("NV.%d" % (j + 3)), ["cA.%d" % c])
            early(c + 1)
        early(7)
        if last:
            dma("S", T.yx[:], T.S[:], ["S"], [])
        sign_levels("Y0", 0, "cA", (2, 0, 3, 4, 1, 5), True, True)
        blocks("X1", 0, [("KB", "LM", LS, "got")], False, True)
        mm(part("X1", 0, 256), T.mm[:], T.BD[:, 0, :, :], False, False, ["mm", "BD.-1/16"], ["X1"])
        blocks("Y1", 0, [("KB", "OM", OS, "-1/2"), ("s2", "OM", OS, "1/2")], True)
        new_columns(0)
        for h in range(2):
            ts(half("KA", h), part("Y0", 128 * h, 128), 0.0, -2.0, OP.is_gt, OP.mult, ["Y0"], ["KA.%d" % h])
        blocks("X1", 0, [("KA", "OM", OS, "1/2")], True)
        tt(T.DA[:], part("Y1", 0, 256), T.rows[:, 0, :], OP.add, ["Y1", "rows"], ["DA.0", "DA.1"])
        for h in range(2):
            ts(half("DB", h), part("X1", 128 * h, 128), 63.5, None, OP.add, None, ["X1"], ["DB.%d" % h])
        blocks("Y2", 0, [("KA", "ID", IDS, "-1/128")], False)
        if not last:
            make_u(0)
        for lst, s in (("B", 5), ("A", 5), ("A", 4)):
            quot("A", s, lst)
        for h in range(2):
            for s in range(1, 5):
                quot("V", s, "B", h)
        for s in (1, 2, 3):
            quot("V", s, "A")
        for h in range(2):
            quot_add("TG", "B", h, (0, 1, 2, 3, 4))
        quot_add("TG", "B", None, (5,), True)
        quot_add("Y2", "A", None, (0, 1, 5, 2, 3, 4), True)
        mm(part("X2", 0, 256), T.ones[0:1, :], T.rows[0:1, 1, :], True, False, ["ones", "rows"], ["X2"])
        blocks("X2", 0, [("KB", "OM", OS, "-1/2"), ("KA", "OM", OS, "1/2")], True)
        act(T.nr[:], part("X2", 0, 256), AF.Relu, ["X2"], ["nr"])
        fill_names(2)
        if not last:
            mm(T.OB[:, 256:257], T.onesf[:], T.rs[:, 0:1], True, True, ["onesf", "rs"], ["OB"])
            act(T.kc[:, 0:1], T.OB[:, 256:257], AF.Identity, ["OB"], ["kc"], bias=4096.0 * 33 - 2.0 ** 23)
            make_u(1)

        def step(h, s):
            if s < 0:
                src, bk = (("VA", "Y2"), (VB, "TG"))[h]
                tt(T.E0[:, 8 * h:8 * h + 8, :], T[bk][:, 0:8, 0::2], T[src][:, 0], OP.add, [bk, src + ".0"], ["E0.%d" % h])
                tt(T.Y1[:, 8 * h:8 * h + 8, 0:16], T[bk][:, 0:8, 1::2], T[src][:, 1], OP.add, [bk, src + ".1"], ["Y1.%d" % h])
            elif s < 4:
                stage(s, h)
            else:
                o, key = ((T.TG, "TG"), (T.BP, "BP"))[h]
                for hi, alu in ((0, OP.min), (1, OP.max)):
                    tt(o[:, 0:8, 16 * hi:16 * hi + 16], T.E0[:, 8 * h:8 * h + 8, :], T.Y1[:, 8 * h:8 * h + 8, 0:16], alu,
                       ["E0.%d" % h, "Y1.%d" % h], ["%s.s%d" % (key, hi)])
        step(1, -1)
        new_columns(1)
        fill = T.Y0[:, 8:16, :]
        mm(fill, T.ones[0:1, :], T.topf[0:1, :], True, False, ["ones", "topf"], ["Y0"])
        for e in range(2):
            mm(T.Y0[:, 8:16, e::2], T.fbf[:, 128 * e:128 * e + 128], T.IDN[:], False, False, ["fbf", "IDN"], ["Y0"])
        for e in range(2):
            mm(T.Y0[:, 8:16, e::2], T.gf[:, 128 * e:128 * e + 128], ident("-1/128"), False, False, ["gf", "ID.-1/128"], ["Y0"])
        mm(fill, ident("1"), T.nr[:], False, True, ["ID.1", "nr"], ["Y0"])
        for s in range(5):
            step(1, s)
            step(0, s - 1)
            if s == 0 and not last:
                turn_init(OWN, 0)
            if s == 0 and t == RO - 2:
                for j, bk in enumerate(("Y2", "X0")):
                    sums(j, bk)
                    keep_sums(j, bk)
        for hi in range(2):
            c = slice(16 * hi, 16 * hi + 16)
            tt(T.v1[:, :, c], T.BP[:, :, c], T.Y0[:, 8:16, c], OP.min, ["BP.s%d" % hi, "Y0"], ["v1.%d" % hi])
        step(0, 4)
        if not last:
            for e, hi in ((1, 0), (1, 1), (0, 0), (0, 1)):
                c = slice(16 * hi + e, 16 * hi + 16, 2)
                tt(T.VA[:, e, :, 8 * hi:8 * hi + 8], T.v1[:, :, c], T.TG[:, 0:8, c], OP.min, ["v1.%d" % hi, "TG.s%d" % hi], ["VA.%d" % e])
            for e in (1, 0):
                send_names(t + 1, e)
            turn_own()
        else:
            turn_init(OWN, 4, (0, 1))
            for b in range(2):
                c = slice(16 * b, 16 * b + 16)
                tt(T.VL[:, 128 * b:128 * b + 128], T.v1[:, :, c], T.TG[:, 0:8, c], OP.min, ["v1.%d" % b, "TG.s%d" % b], ["VL.%d" % b])
                mm(part(OWN[b][0], 0, 128), T.VL[:, 128 * b:128 * b + 128], T.IU[:], False, True, ["VL.%d" % b, "IU"], [OWN[b][0]])
            act(half("amf", 0), part(OWN[0][0], 0, 128), AF.Copy, [OWN[0][0]], ["amf.0"])
            cp(half("amf", 1), part(OWN[1][0], 0, 128), [OWN[1][0]], ["amf.1"])
            dma("A", T.ya[:, 0:128], half("amf", 0), ["amf.0"], [])
            dma("S", T.ya[:, 128:256], half("amf", 1), ["amf.1"], [])
    plan["emit"](g, T)
